import numpy as np, ml_dtypes
CORES = [66,74,82,90,194,202,210,218]
N = 8
BF = ml_dtypes.bfloat16
V, A, M, RO, BN = 2048, 1024, 192, 4, 3
HOPS = [1, 2, 4, 7]
def parts(rng):
    x = rng.integers(0, 256, (N, 8, 16, V)); sb = rng.integers(0, V, (N, 8, 16, A)); la = rng.integers(0, A, (N, 8, 16, M)); lw = rng.integers(0, A, (N, 8, 16, M))
    z = rng.integers(0, 256, (N, 8, 16, M)); b = rng.integers(0, 16, (N, 8, M)); th = rng.integers(1420, 1680, (N, 8, 1)) - 60 * (BN - 3)
    return x, sb, la, lw, z, b, th
def pack(x, sb, la, lw, z, b, th):
    return {"xs": x.reshape(N, 128, V).astype(np.float32).astype(BF), "sb": np.ascontiguousarray(sb.reshape(N, 128, A)).astype(np.int32),
            "la": np.ascontiguousarray(la.reshape(N, 128, M)).astype(np.int32), "lw": np.ascontiguousarray(lw.reshape(N, 128, M)).astype(np.int32),
            "z0": z.reshape(N, 128, M).astype(np.float32).astype(BF), "b0": b.astype(np.int32), "th": th.astype(np.int32)}
def setup_inputs(rng):
    return pack(*parts(rng))
def setup_inputs_spread(rng):
    x, sb, la, lw, z, b, th = parts(rng)
    x = (np.exp2(8 * rng.random((N, 8, 1, V))) * rng.random((N, 8, 16, V))).astype(np.int64)
    z = (np.exp2(8 * rng.random((N, 8, 1, M))) * rng.random((N, 8, 16, M))).astype(np.int64)
    th = np.minimum(np.exp2(4 + 8 * rng.random((N, 8, 1))).astype(np.int64), 4080)
    sb = (V * rng.random((N, 8, 16, A)) ** 2).astype(np.int64); la = (A * rng.random((N, 8, 16, M)) ** 2).astype(np.int64)
    lw = A - 1 - (A * rng.random((N, 8, 16, M)) ** 3).astype(np.int64)
    return pack(np.minimum(x, 255), np.minimum(sb, V - 1), np.minimum(la, A - 1), np.maximum(lw, 0), np.minimum(z, 255), b, th)
def edge(rng, hi, shape):
    return np.where(rng.random(shape) < 0.7, hi * rng.integers(0, 2, shape), rng.integers(0, hi + 1, shape))
def setup_inputs_ends(rng):
    kind = rng.integers(0, 4, (N, 8, 1, V)); x = 255 * np.where(kind == 0, 0, np.where(kind < 3, 1, rng.integers(0, 2, (N, 8, 16, V))))
    kind = rng.integers(0, 4, (N, 8, 1, M)); z = 255 * np.where(kind == 0, 0, np.where(kind == 1, 1, rng.integers(0, 2, (N, 8, 16, M))))
    sb = edge(rng, V - 1, (N, 8, 16, A)); la = edge(rng, A - 1, (N, 8, 16, M)); lw = edge(rng, A - 1, (N, 8, 16, M)); b = 15 * rng.integers(0, 2, (N, 8, M))
    m = rng.random((N, 8, 1, M)); la = np.where(m < 0.1, 0, np.where(m < 0.2, A - 1, la)); m = rng.random((N, 8, 1, M)); lw = np.where(m < 0.1, 0, np.where(m < 0.2, A - 1, lw))
    th = np.zeros((N, 8, 1), np.int64); th[:, :6, 0] = np.where(np.argsort(rng.random((N, 6)), axis=1) < 3, 1, 4080); th[:, 6] = 1; th[:, 7] = 4080
    x[:, 6:, :, 0] = 0; x[:, 6:, :, V - 1] = 255; x[:, 6:, :, A - 1] = 255; sb[:, 6:, :, A - 1] = V - 1
    for c in (0, 1, M - 2, M - 1):
        la[:, 6:, :, c] = A - 1; lw[:, 6:, :, c] = (A - 1) * (c % 2); z[:, 6, :, c] = 255; z[:, 7, :, c] = 0
    return pack(x, sb, la, lw, z, b, th)
def setup_inputs_corners(rng):
    x, sb, la, lw, z, b, th = parts(rng); odd = np.arange(V) & 1
    th[:, 0] = 1; b[:, 0] = 0
    th[:, 1] = 4080; b[:, 1] = 15
    x[:, 2] = 85 * rng.integers(0, 4, (N, 1, V)); z[:, 2] = 85 * rng.integers(0, 4, (N, 1, M)); th[:, 2] = rng.choice(np.array([1360, 1361, 2720]), (N, 1)); th[0, 2] = 1360; th[N - 1, 2] = 2720
    sb[:, 3] = sb[:, 3, :1]
    la[:, 4] = la[:, 4, :1]; lw[:, 4] = la[:, 4]; z[:, 4] = 255 * rng.integers(0, 2, (N, 1, M))
    x[:, 5] = np.where(odd == 0, 255, 0); th[:, 5, 0] = 3072 + (np.arange(N) & 1)
    n = rng.choice(np.array([0, BN - 1, BN, BN + 1, 16]), (N, 1, A))
    sb[:, 5] = 2 * rng.integers(0, V // 2, (N, 16, A)) + (np.argsort(rng.random((N, 16, A)), axis=1) >= n)
    la[:, 5] = 2 * rng.integers(0, A // 2, (N, 16, M)) + (rng.random((N, 16, M)) < 0.125)
    x[:, 6] = np.where(odd == 0, rng.integers(0, 8, (N, 16, V)), rng.integers(248, 256, (N, 16, V))); th[:, 6] = 40
    sb[:, 6] = 2 * rng.integers(0, V // 2, (N, 16, A)); la[:, 6] = 2 * rng.integers(0, A // 2, (N, 16, M)) + 1
    la[:, 7] = rng.choice(np.array([0, A - 1, A // 2]), (N, 16, M)); lw[:, 7] = rng.choice(np.array([0, A - 1, A // 2 + 1, 1]), (N, 16, M))
    sb[:, 7] = rng.choice(np.array([0, V - 1, 1, V // 2]), (N, 16, A)); sb[:, 7, :8] = np.arange(A)
    return pack(x, sb, la, lw, z, b, th)
def setup_inputs_crowd(rng):
    x, sb, la, lw, z, b, th = parts(rng); q = np.arange(V - 20, V - 4)
    o = np.arange(V) & 3; turn = ((np.arange(16)[None, :] + np.arange(N)[:, None]) & 15) < BN
    x[:, 3] = np.where(o == 0, x[:, 3], np.where(o == 1, rng.integers(110, 128, (N, 16, V)), np.where(o == 2, rng.integers(0, 41, (N, 16, V)), rng.integers(250, 256, (N, 16, V)))))
    sb[:, 3] = np.where(turn[:, :, None] & (o[:A] == 1), 4 * rng.integers(0, A // 4 - 5, (N, 16, A)) + 3, 4 * rng.integers(0, V // 4 - 5, (N, 16, A)) + 2)
    x[..., 0] = 0; x[..., A - 1] = 255; x[..., q] = 255; sb[..., A - 1] = q
    hot = np.zeros((8, M), bool); hot[1, M - 1] = True; hot[2] = True; hot[3] = True; hot[5] = rng.random(M) < 0.5; hot[6, M - 1] = True; hot[7, :M - 1] = True
    for e in (2, 4, 6):
        la[:, e] = la[:, e, :, :1]; lw[:, e] = lw[:, e, :, :1]; z[:, e] = z[:, e, :, :1]; b[:, e] = b[:, e, :1]
    la[:, 5] = rng.choice(np.array([1, 3, A // 2, A - 2]), (N, 16, M)); lw[:, 5] = rng.choice(np.array([0, 2, A // 2 + 1, A - 3]), (N, 16, M))
    la = np.where(np.arange(16)[None, None, :, None] == b[:, :, None, :], np.where(hot[None, :, None, :], A - 1, 0), la)
    kinds = rng.permutation(N) & 3
    for r in range(N):
        n, k = ((1, 2), (3, 1), (0, 3), (2, 2))[int(kinds[r])]; p = rng.permutation(M)
        for c, i in ((p[:n], 0), (p[n:n + k], 1)):
            la[r, 3][:, c] = 4 * rng.integers(0, A // 4 - 5, (16, c.size)) + i; lw[r, 3][:, c] = 4 * rng.integers(0, A // 4 - 5, (16, c.size)) + i
    return pack(x, sb, la, lw, z, b, th)
def setup_inputs_full(rng):
    x, sb, la, lw, z, b, th = parts(rng); n = np.arange(V) & 3; c = np.arange(M); v = np.arange(2, V, 4)
    for r in range(N):
        for e in (0, 7):
            x[r, e] = np.where(n == 3, rng.integers(250, 256, (16, V)), np.where(n == 1, rng.integers(228, 250, (16, V)), rng.integers(208, 256, (16, V))))
            x[r, e, (v >> 2) & 15, v] = rng.integers(208, 228, v.size)
            p = 4 * rng.permutation(A // 4)[:M] + 1
            sb[r, e] = 4 * rng.integers(0, V // 4, (16, A)) + 2
            sb[r, e, rng.integers(0, 16, M), p] = 4 * rng.permutation(V // 4)[:M] + 3
            la[r, e, b[r, e], c] = p; th[r, e, 0] = rng.integers(3300, 3329)
        for e in (1, 4):
            x[r, e] = np.where(n == 0, rng.integers(0, 64, (16, V)), np.where(n == 3, rng.integers(240, 256, (16, V)), rng.integers(128, 240, (16, V))))
            u = 4 * rng.permutation(A // 4)[:M] + 1; k = rng.integers(0, 16, M)
            sb[r, e] = 4 * rng.integers(0, V // 4, (16, A)) + np.where(n[:A] == 0, 0, 2)
            sb[r, e, k, u] = 4 * rng.permutation(V // 4)[:M] + 3
            la[r, e] = 4 * rng.integers(0, A // 4, (16, M)) + 2; lw[r, e] = 4 * rng.integers(0, A // 4, (16, M)) + 2
            la[r, e, b[r, e], c] = 4 * rng.integers(0, A // 4, M); la[r, e, (b[r, e] + rng.integers(1, 16, M)) & 15, c] = u
            lw[r, e, k, c] = 4 * rng.integers(0, A // 4, M)
            z[r, e] = x[r, e][:, u]; th[r, e, 0] = rng.integers(1800, 2049)
    for e in (2, 5):
        x[:, e] = rng.integers(208, 256, (N, 16, V)); z[:, e] = rng.integers(208, 256, (N, 16, M)); th[:, e] = rng.integers(3560, 3640, (N, 1))
    side = rng.integers(0, 2, (N, 1, M)); side[:, 0, 0] = 0; side[:, 0, M - 1] = 1
    x[:, 6] = 255 * (np.arange(V) & 1); z[:, 6] = 255 * side; b[:, 6] = 0
    la[:, 6] = 2 * rng.integers(0, A // 2, (N, 16, M)) + np.where(np.arange(16)[None, :, None] == 0, side, 1 - side)
    return pack(x, sb, la, lw, z, b, th)
def check_inputs(d):
    bad = []
    for k, lo, hi in (("xs", 0, 255), ("sb", 0, V - 1), ("la", 0, A - 1), ("lw", 0, A - 1), ("z0", 0, 255), ("b0", 0, 15), ("th", 1, 4080)):
        a = np.asarray(d[k]).astype(np.float64)
        if not np.all((a >= lo) & (a <= hi)): bad.append("range of " + k)
        elif not np.all(a == np.floor(a)): bad.append("whole numbers of " + k)
    return bad
def pick(x, ix):
    return np.stack([np.stack([np.take(x[r, e], ix[r, e].reshape(-1), axis=1).reshape(16, 16, M) for e in range(8)]) for r in range(N)])
def slot_of(a, k):
    return np.take_along_axis(a, k[:, :, None, :], 2)[:, :, 0]
def first(p, m):
    c = np.flatnonzero(m)
    return c[np.unique(p[c], return_index=True)[1]]
def reference(xs, sb, la, lw, z0, b0, th):
    x = xs.astype(np.float32).astype(np.int32).reshape(N, 8, 16, V); t = sb.astype(np.int64).reshape(N, 8, 16, A)
    l = la.astype(np.int64).reshape(N, 8, 16, M); w = lw.astype(np.int64).reshape(N, 8, 16, M)
    z = z0.astype(np.float32).astype(np.int32).reshape(N, 8, 16, M); b = b0.astype(np.int64).reshape(N, 8, M); h = th.astype(np.int64).reshape(N, 8, 1, 1)
    al = np.zeros((N, 8), np.int64); slot = np.arange(16)[None, None, :, None]
    for rnd in range(RO):
        hop = HOPS[rnd]
        y = pick(x, l); d = np.add.reduce(np.abs(y - z[:, :, :, None, :]), axis=2)
        j = np.argmin(np.where(slot == b[:, :, None], 9999, d), axis=2)
        yj = np.take_along_axis(y, j[:, :, None, None, :], 3)[:, :, :, 0]
        yb = np.take_along_axis(y, b[:, :, None, None, :], 3)[:, :, :, 0]
        lb = slot_of(l, b); lj = slot_of(l, j)
        s = np.take_along_axis(t, lb[:, :, None, :], 3)
        xc = np.roll(x, -hop, axis=0); hc = np.roll(h, -hop, axis=0); need = (BN + (al & 1))[:, :, None]
        g = np.add.reduce(np.minimum(pick(xc, s), yb[:, :, :, None, :]), axis=2)
        occ = np.add.reduce((g >= hc).astype(np.int64), axis=2) >= need
        place = slot_of(s, np.argmax(g, axis=2))
        new = np.maximum(np.take_along_axis(xc, place[:, :, None, :], 3) - (yb >> 2), 0)
        for r in range(N):
            for e in range(8):
                c = first(place[r, e], occ[r, e]); xc[r, e][:, place[r, e, c]] = new[r, e][:, c]
        q = pick(xc, s); g = np.add.reduce(np.minimum(q, yb[:, :, :, None, :]), axis=2)
        keep = occ & (np.add.reduce((g >= hc).astype(np.int64), axis=2) >= need); out = ~keep
        f = np.maximum.reduce(q, axis=3); xk = np.take_along_axis(xc, place[:, :, None, :], 3)
        x = np.roll(xc, hop, axis=0)
        u = np.argmin(np.add.reduce(np.abs(pick(x, w) - f[:, :, :, None, :]), axis=2), axis=2)
        wu = slot_of(w, u); su = slot_of(s, u)
        l = np.where((slot == b[:, :, None]) & out[:, :, None], wu[:, :, None], l)
        w = np.where((slot == u[:, :, None]) & out[:, :, None], lb[:, :, None], w)
        if rnd < RO - 1:
            for r in range(N):
                for e in range(8):
                    c = first(lj[r, e], out[r, e]); t[r, e][u[r, e, c], lj[r, e, c]] = su[r, e, c]
        z = np.where(keep[:, :, None], (z + xk) >> 1, (z + yj) >> 1)
        b = np.where(out, j, b); al = np.add.reduce(out.astype(np.int64), axis=2)
    return {"yx": x.reshape(N, 128, V).astype(np.float32).astype(BF), "yl": l.reshape(N, 128, M).astype(np.float32), "yw": w.reshape(N, 128, M).astype(np.float32),
            "yz": z.reshape(N, 128, M).astype(np.float32).astype(BF), "yb": b.astype(np.float32)}

@@ -1,0 +1,743 @@
+import numpy as np
+from concourse.bass import DstId, RemoteDMATransfer
+from concourse.mybir import AluOpType as OP, AxisListType, ActivationFunctionType as AF
+
+V_, A_, M_, RO = 2048, 1024, 192, 4
+HOPS = [1, 2, 4, 7]
+S = np.s_
+F, B, I, U = "float32", "bfloat16", "int32", "uint16"
+SEG = [8 * q * (q + 1) for q in range(13)]
+NP = SEG[12]
+MAGIC, HALF = 12582912.0, 0.5 - 2.0 ** -11
+
+P = {"S2": [4, 4, 4, 4],
+     "G4V": [2, 2, 2, 2],
+     "G5V": [0, 0, 0, 2],
+     "ZS": 1, "AS": 1,
+     "PS1": 6,
+     "KCH": [(0, 10), (10, 16)], "KC4": [(0, 10), (10, 16)],
+     "CY": 1.04, "PE": 0.55, "GA": 1.56, "SC": 3.8, "TT": 2.0, "FIX": 20.0, "SAME": 60.0, "OTHER": 120.0, "SLACK": 150.0, "NET": 1.0,
+     "SEED": 0, "ROUNDS": 5000, "HEAT": 800.0}
+XH = 2
+SAMEQ_WAR = True
+
+SCRATCH = {}
+
+
+def _sb(names, shape, dt):
+    for n in names.split():
+        SCRATCH[n] = ("sbuf", list(shape), dt)
+
+
+_sb("X R0 R1 R2 R3", [128, 2240], B)
+_sb("TT", [128, 1216], F)
+_sb("SBI", [128, 1024], I)
+_sb("LAI LWI KI Q4 B0I", [128, 192], I)
+_sb("S208 LQ WQ", [128, 208], F)
+_sb("TR TR2", [128, 384], F)
+_sb("EX", [128, 192], "float16")
+_sb("BLKH", [128, 128], "float16")
+_sb("SQK KS ST PS TOLD MD OHW AW SW CW LJ ZT OL OW RIM", [128, 192], F)
+_sb("Z Y RI RV MR MRV RBIG BI CN OH OHJ EXW XS MW NV0 NV1 NV2 NV3 OV0 OV1 OV2 OV3 NOH", [128, 192], B)
+_sb("SKQ SSL LK WK", [128, 192], U)
+_sb("M1 M2 M5", [128, 192, 16], B)
+_sb("KMN KMX", [128, 12, 16], B)
+_sb("RAW4 FS RAW5", [128, 3072], B)
+_sb("YW", [128, 3264], B)
+_sb("NE FL MM", [128, NP], B)
+_sb("R01", [128, 768], B)
+_sb("SEL NSEL", [128, 144], B)
+_sb("T143", [128, 144], F)
+_sb("BLKF IDF NIDF", [128, 128], F)
+_sb("BLKB ID NID IBG E8", [128, 128], B)
+_sb("WF", [128, 512], F)
+_sb("WN", [128, 128], I)
+_sb("WU", [128, 448], U)
+_sb("TH", [128, 16], F)
+_sb("THI THB", [128, 8], I)
+for _n in "KA KB".split():
+    SCRATCH[_n] = ("psum", [128, 32, 16], F)
+for _n in "D0 D1 YP B0 B1 KC".split():
+    SCRATCH[_n] = ("psum", [128, 512], F)
+
+WFN = "PV A PV2 A2 WO O4 LB BB SL DL DB JA NOC LT J Q E1 E2 E3 DU1 DU2 CC C T1 T2 T3 DS DS2 DS3 THM LT4".split()
+WNN = "P JI WI N1 N2 KK".split()
+WUN = "IQ IE IR IEND IQK IKQ PKQ IE16 IR3 LBU BBU SELU PLU LJU O2 NO0 NO1 NO2 NO3 OO0 OO1 OO2 OO3".split()
+
+SEMAPHORES = (["cV", "cS", "cP", "cG", "loc", "th"] + ["d%d" % i for i in range(16)] + ["r%d" % i for i in range(3 + XH)]
+              + ["l%d" % i for i in range(3 + XH)] + ["eo%d" % i for i in range(4)])
+IOS = "xs sb la lw z0 b0 th yx yl yw yz yb".split()
+
+
+def ap(name, idx=S[:]):
+    return ("ap", name, idx)
+
+
+def c2(name, a, b, s=1):
+    return ap(name, S[:, a:b:s])
+
+
+def wf(n, a=0, b=12):
+    return c2("WF", 16 * WFN.index(n) + a, 16 * WFN.index(n) + b)
+
+
+def wn(n, a=0, b=12):
+    return c2("WN", 16 * WNN.index(n) + a, 16 * WNN.index(n) + b)
+
+
+def wu(n, a=0, b=12):
+    return c2("WU", 16 * WUN.index(n) + a, 16 * WUN.index(n) + b)
+
+
+def ind(win, off):
+    return ("ind", win, off)
+
+
+def cols(a):
+    shape = SCRATCH[a[1]][1]
+    idx = a[2] if isinstance(a[2], tuple) else (a[2],)
+    return np.arange(int(np.prod(shape[1:]))).reshape(shape[1:])[idx[1:]].reshape(-1)
+
+
+def build():
+    ops = []
+    acc = {}
+    sec = ["i"]
+    CY = P["CY"]
+
+    def touch(me, a, write):
+        if a[1] in IOS:
+            return
+        psum = SCRATCH[a[1]][0] == "psum"
+        m = 0
+        for x in cols(a):
+            m |= 1 << int(x)
+        for (o, om, ow) in acc.setdefault(a[1], []):
+            if o == me["id"]:
+                continue
+            other = ops[o]["eng"] != me["eng"] or bool(ops[o]["dma"]) or bool(me["dma"])
+            hit = (m & om) != 0
+            if hit and ow and not write:
+                me["deps"][o] = True
+            elif (hit and (write or ow)) or (psum and ops[o]["eng"] != me["eng"]):
+                me["deps"][o] = me["deps"].get(o, False) or other or SAMEQ_WAR
+        acc[a[1]].append((me["id"], m, write))
+
+    def add(eng, calls, cost, dma=None, after=(), ext=(), busy=None):
+        me = {"id": len(ops), "eng": eng, "calls": calls, "cost": cost, "dma": dma, "deps": {}, "ext": list(ext),
+              "busy": cost if busy is None else busy, "after": list(after)}
+        ops.append(me)
+        a = calls[0][1][0]
+        if a is None or a[0] == "ind":
+            name = "send" if a is None else a[1][1][0] + "s"
+        elif a[1] in ("WF", "WN", "WU"):
+            name = {"WF": WFN, "WN": WNN, "WU": WUN}[a[1]][a[2][1].start // 16]
+        else:
+            name = a[1]
+        me["tag"] = sec[0] + eng + name
+        for (_, args, kw) in calls:
+            for n, a in enumerate(list(args) + list(kw.values())):
+                if isinstance(a, tuple) and a[0] == "ap":
+                    touch(me, a, n == 0 or a is kw.get("accum_out"))
+                elif isinstance(a, tuple) and a[0] == "ind":
+                    touch(me, a[1], n == 0)
+                    touch(me, a[2], False)
+                elif isinstance(a, tuple) and a[0] == "rd":
+                    touch(me, a[1], False)
+        return me["id"]
+
+    def vcost(eng, out, in0, rate):
+        if in0[0] == "ind":
+            return (50 if eng == "V" else 65) + 16 * len(cols(in0[2])) * P["GA"] * CY
+        if out[0] == "ind":
+            return 50 + 16 * len(cols(out[2])) * P["SC"] * CY
+        return P["FIX"] + max(64, len(cols(in0)) * rate) * CY
+
+    def half(*aps):
+        return 0.5 if all(a[0] == "ap" and SCRATCH[a[1]][2] in (B, U) for a in aps) else 1.0
+
+    def cp(out, in_, **k):
+        return add("V", [("tensor_copy", [out, in_], {})], vcost("V", out, in_, half(out, in_)), **k)
+
+    def tt(out, a, b, op):
+        ps = any(x[0] == "ap" and SCRATCH[x[1]][0] == "psum" for x in (a, b))
+        return add("V", [("tensor_tensor", [out, a, b, op], {})], vcost("V", out, a, 1.0 if ps else P["TT"]))
+
+    def ts(out, a, s1, o0, s2=None, o1=None):
+        args = [out, a, s1, s2, o0] + ([o1] if o1 is not None else [])
+        return add("V", [("tensor_scalar", args, {})], vcost("V", out, a, half(out, a)))
+
+    def scan(out, d0, d1, init, o0, o1):
+        return add("V", [("tensor_tensor_scan", [out, d0, d1, init, o0, o1], {})], vcost("V", out, d1, half(out, d0, d1)))
+
+    def red(out, a, op):
+        return add("V", [("tensor_reduce", [out, a, AxisListType.X, op], {})], vcost("V", out, a, 1.0))
+
+    def tr(out, a):
+        return add("V", [("transpose", [out, a], {})], vcost("V", out, a, 1.0))
+
+    def ms(out, v):
+        return add("V", [("memset", [out, v], {})], vcost("V", out, out, half(out)))
+
+    def act(out, a, f=AF.Identity, **kw):
+        return add("S", [("activation", [out, a, f], kw)], vcost("S", out, a, 1.0))
+
+    def gat(eng, out, win, off):
+        return cp(out, ind(win, off)) if eng == "V" else act(out, ind(win, off), AF.Copy)
+
+    def mm(out, pairs):
+        calls, cost = [], 60
+        for n, (l, r) in enumerate(pairs):
+            calls.append(("matmul", [out, l, r, n == 0, n == len(pairs) - 1], {}))
+            cost += max(64, len(cols(r))) * P["PE"] * (4 if SCRATCH[l[1]][2] == F else 1)
+        return add("P", calls, cost)
+
+    def iota(out, pat, base, cm):
+        kw = {} if SCRATCH[out[1]][2] == I else {"allow_small_or_imprecise_dtypes": True}
+        return add("G", [("iota", [out, pat, base, cm], kw)], 130 + 2 * len(cols(out)) * CY)
+
+    nd = [0]
+
+    def dma(eng, out, in_, cost):
+        nd[0] += 1
+        return add(eng, [("dma_start", [out, in_], {})], cost, dma=("d%d" % (nd[0] - 1), 16), busy=60)
+
+    def send(parts, loc, cost, busy=1000):
+        return add("G", [("send", [None, parts] + [("rd", p[0]) for p in parts], {})], cost * P["NET"], dma=(loc, None), busy=busy)
+
+    def sel(r):
+        return c2("SEL", 15 - r, 143 - r)
+
+    def sums(bank, m, extra, ranges=None):
+        for (a, b) in ranges or P["KCH"]:
+            out = ap(bank, S[:, 0:12, a:b])
+            mm(out, [(l, ap(t, S[:, 0:12, a:b])) for (l, t) in extra] + [(sel(r), ap(m, S[:, r::16, a:b])) for r in range(16)])
+
+    def ends(name):
+        return c2(name, 15, 192, 16)
+
+    PM, WC, NEED = wf("C", 0, 1), wf("C", 1, 2), wf("C", 2, 3)
+    r01 = c2("R01", 0, 192)
+    xw = c2("X", 0, V_)
+
+    w = V_ // XH
+    for h in range(XH):
+        dma("Y", c2("X", h * w, (h + 1) * w), ap("xs", S[:, h * w:(h + 1) * w]), 2600 + 900 * h)
+    dma("S", ap("B0I", S[0:8, :]), ap("b0"), 2200)
+    dma("S", ap("LAI"), ap("la"), 2500)
+    dma("S", ap("THI", S[0:1, :]), ap("th"), 2200)
+    dma("Y", ap("SBI"), ap("sb"), 5000)
+    dma("S", ap("LWI"), ap("lw"), 3000)
+    dma("S", ap("Z"), ap("z0"), 3000)
+    arrive = {}
+    for h in range(XH):
+        arrive[h] = send([(c2("X", h * w, (h + 1) * w), c2("R0", h * w, (h + 1) * w), -HOPS[0], "r%d" % h)], "l%d" % h,
+                         6000 if h == 0 else 6500, busy=2500 if h == 0 else 1000)
+    iota(wn("P", 0, 1), [[0, 1]], 0, 1)
+    iota(ap("RI"), [[0, 12], [1, 16]], 0, 0)
+    iota(wf("Q", 0, 16), [[1, 16]], 0, 0)
+    iota(ap("BLKF"), [[-16, 8], [0, 16]], 0, 1)
+    iota(ap("E8", S[0:8, :]), [[-1, 8], [0, 16]], 0, 1)
+    iota(ap("T143"), [[-1, 144]], 15, 1)
+    ts(wn("P", 1, 2), wn("P", 0, 1), 15, OP.bitwise_and)
+    ts(wn("P", 2, 3), wn("P", 0, 1), 4, OP.arith_shift_right, 1, OP.bitwise_and)
+    cp(wf("C", 0, 2), wn("P", 1, 3))
+    ms(NEED, 3.0)
+    ts(wf("C", 3, 4), WC, 192.0, OP.mult)
+    ts(ap("E8", S[0:8, :]), ap("E8", S[0:8, :]), 0.0, OP.is_equal)
+    ts(ap("MR"), ap("RI"), PM, OP.is_equal)
+    act(ap("RV"), ap("RI"), AF.Identity, scale=-1.0, bias=15.0)
+    ts(ap("MRV"), ap("RV"), PM, OP.is_equal)
+    ts(ap("RBIG"), ap("RI"), 0.0, OP.is_equal, 1048576.0, OP.mult)
+    ts(ap("BLKB"), ap("BLKF"), PM, OP.is_equal)
+    act(ap("BLKF"), ap("BLKB"), AF.Copy)
+    cp(ap("BLKH"), ap("BLKB"))
+    ts(ap("SEL"), ap("T143"), PM, OP.is_equal, 16.0, OP.mult)
+    act(ap("NSEL"), ap("SEL"), AF.Identity, scale=-1.0)
+    ts(ap("ID"), c2("T143", 15, 143), 0.0, OP.is_equal)
+    act(ap("NID"), ap("ID"), AF.Identity, scale=-1.0)
+    act(ap("IBG"), ap("ID"), AF.Identity, scale=65536.0)
+    act(ap("IDF"), ap("ID"), AF.Copy)
+    act(ap("NIDF"), ap("ID"), AF.Identity, scale=-1.0)
+    ms(ap("R01"), 1.0)
+    ms(c2("R01", 0, 768, 16), 0.0)
+    ts(wf("J", 0, 16), wf("Q", 0, 16), 16.0, OP.mult, PM, OP.add)
+    cp(wu("IQ"), wf("Q"))
+    ts(wu("IE"), wf("Q"), 16.0, OP.mult, 15.0, OP.add)
+    ts(wu("IR"), wf("Q"), -1.0, OP.mult, 11.0, OP.add)
+    act(wf("DU1"), wf("J"), AF.Identity, bias=float(V_))
+    act(wf("DU2"), wf("J"), AF.Identity, bias=float(A_))
+    act(wf("CC", 0, 16), wf("J", 0, 16), AF.Identity, bias=3072.0)
+    ms(wf("PV", 0, 16 * 14), 0.0)
+    ms(wn("JI", 0, 32), 0)
+    ts(wf("T1", 0, 1), PM, 11.0, OP.min, 1.0, OP.add)
+    ts(wf("T1", 1, 2), wf("T1", 0, 1), 1.0, OP.add, wf("T1", 0, 1), OP.mult)
+    ts(wu("IEND", 0, 1), wf("T1", 1, 2), 8.0, OP.mult, -1.0, OP.add)
+    ts(wf("T1", 2, 3), PM, 12.0, OP.is_lt, PM, OP.mult)
+    ts(wu("IE16", 0, 1), wf("T1", 2, 3), 16.0, OP.mult, 15.0, OP.add)
+    ts(wu("IR3", 0, 3), wf("Q", 0, 3), 0.0, OP.mult, wf("T1", 2, 3), OP.add)
+
+    def turned(dst, qq, base):
+        ts(wn("N1"), qq, WC, OP.add)
+        ts(wn("N2"), wn("N1"), 1, OP.bitwise_and)
+        ts(wf("T2"), wn("N2"), 176.0, OP.mult)
+        tt(wf("T2"), wf("T2"), base, OP.add)
+        ts(wf("T3"), qq, 0.0, OP.is_equal, wf("C", 3, 4), OP.mult)
+        tt(wf("T2"), wf("T2"), wf("T3"), OP.add)
+        cp(dst, wf("T2"))
+
+    turned(wu("IQK"), wf("Q"), wf("J"))
+    ts(wn("KK"), wf("J"), 1.0 / 12, OP.mult, -5.5 / 12, OP.add)
+    ts(wf("E1"), wn("KK"), -12.0, OP.mult)
+    tt(wf("E1"), wf("E1"), wf("J"), OP.add)
+    ts(wf("E2"), wf("E1"), 16.0, OP.mult)
+    tt(wf("E2"), wf("E2"), wn("KK"), OP.add)
+    cp(wu("PKQ"), wf("E2"))
+    turned(wu("IKQ"), wf("E1"), wf("E2"))
+    ms(ap("MM"), 0.0)
+    ts(c2("MM", 0, 16), c2("RV", 0, 16), PM, OP.is_ge)
+    for q in range(1, 12):
+        act(c2("MM", SEG[q], SEG[q] + 16), c2("MM", 0, 16), AF.Copy)
+    act(ap("KMN"), ap("RI"), AF.Copy)
+    act(ap("KMX"), ap("RV"), AF.Copy)
+    act(ap("RIM"), ap("RI"), AF.Identity, bias=-4096.0)
+    add("G", [("partition_broadcast", [ap("THB"), ap("THI", S[0:1, :]), 128], {})], 180)
+    tt(wf("THM", 0, 8), ap("THB"), c2("SEL", 15, 143, 16), OP.mult)
+    red(wf("THM", 8, 9), wf("THM", 0, 8), OP.add)
+    tho = send([(wf("THM", 8, 9), c2("TH", 4 * n, 4 * n + 1), -HOPS[n], "th") for n in range(RO)], "loc", 3000)
+
+    def turn(src, dst):
+        tr(c2(dst, 0, 192), c2(src, 0, 192))
+        tr(c2(dst, 192, 384), c2(src, 16, 208))
+
+    for (src, dst, t, u) in (("LAI", "LQ", "TR", "LK"), ("LWI", "WQ", "TR2", "WK")):
+        cp(c2("S208", 0, 192), ap(src))
+        cp(c2("S208", 192, 208), c2(src, 0, 16))
+        turn("S208", t)
+        gat("V", ap(u), ap(t), wu("IKQ"))
+        gat("S", c2(dst, 0, 192), ap(t), wu("IQK"))
+    cp(ap("BI", S[0:8, :]), ap("B0I", S[0:8, :]))
+    mm(c2("B0", 0, 192), [(ap("E8", S[0:8, :]), ap("BI", S[0:8, :]))])
+    tt(ap("ST"), c2("B0", 0, 192), ap("MR"), OP.mult)
+    scan(ap("PS"), r01, ap("ST"), 0.0, OP.mult, OP.add)
+    cp(wf("BB"), ends("PS"))
+    tt(ap("OH"), ind(wf("BB", 0, 16), wu("IQ")), ap("RI"), OP.is_equal)
+    tt(ap("ST"), ap("OH"), c2("LQ", 0, 192), OP.mult)
+    scan(ap("PS"), r01, ap("ST"), 0.0, OP.mult, OP.add)
+    gat("V", wf("LB", 0, 16), ap("PS"), wu("IE16", 0, 1))
+    cp(wu("LBU", 0, 16), wf("LB", 0, 16))
+    cp(c2("TT", 0, A_), ap("SBI"))
+
+    def bound():
+        gat("S", ap("Y"), xw, wu("LBU"))
+        mm(c2("YP", 0, 192), [(ap("ID"), ap("Y"))])
+        ts(ap("Q4"), ap("Y"), 0.25, OP.mult, -0.375, OP.add)
+
+    def dist(raw, m, sub, pairs=8):
+        for j in range(pairs):
+            d = "D%d" % (j % 2)
+            for h in range(2):
+                k = 2 * j + h
+                mm(c2(d, h, 384, 2), [(ap("ID"), c2(raw, 192 * k, 192 * k + 192)), (ap("NID"), sub)])
+            act(ap(m, S[:, :, 2 * j:2 * j + 2]), c2(d, 0, 384), AF.Abs)
+
+    def steps(bank, src):
+        mm(c2(bank, 256, 447), [(ap("IDF"), c2(src, 0, 191)), (ap("NIDF"), c2(src, 1, 192))])
+        mm(c2(bank, 271, 448, 16), [(ap("IDF"), ends(src))])
+
+    def lowest(pv, a, du, off):
+        tt(ap("EX"), ind(wf(pv, 0, 16), wu("IR")), ap("MRV"), OP.mult)
+        tt(wf(a), wf(du), wf(pv), OP.subtract)
+        act(wf(a), wf(a), AF.Relu)
+        mm(c2("B0", 0, 192), [(ap("BLKH"), ap("EX"))])
+        if P["PS1"]:
+            mm(c2("B1", 0, 192), [(ap("BLKH"), ap("EX"))])
+        for q in range(11, -1, -1):
+            n = 16 * (q + 1)
+            o = c2("NE", SEG[q], SEG[q + 1])
+            if q >= 12 - P["PS1"]:
+                act(o, c2("B1", 192 - n, 192), AF.Abs, bias=wf(pv, q, q + 1), scale=-1.0)
+            else:
+                ts(o, c2("B0", 192 - n, 192), wf(pv, q, q + 1), OP.not_equal)
+        scan(ap("FL"), ap("NE"), ap("MM"), 1.0, OP.min, OP.max)
+        tt(wf("E1", 0, 16), ind(ap("FL"), wu("IEND", 0, 1)), wf(a, 0, 16), OP.mult)
+        tt(wf("E2"), wf(du), wf("E1"), OP.subtract)
+        cp(off, wf("E2"))
+
+    bound()
+    ka, kb, kc = ap("KA", S[:, 0:12, :]), ap("KB", S[:, 0:12, :]), c2("KC", 0, 192)
+    side = c2("YP", 256, 448)
+    for n in range(RO):
+        sec[0] = "a"
+        R = "R%d" % n
+        rw = c2(R, 0, V_)
+        last = n == RO - 1
+        thc = c2("TH", 4 * n, 4 * n + 1)
+        gat("V", ap("S208"), c2("TT", 0, A_), wu("LBU", 0, 13))
+        turn("S208", "TR")
+        gat("V", ap("SKQ"), ap("TR"), wu("IKQ"))
+        gat("S", ap("SQK"), ap("TR"), wu("IQK"))
+        steps("YP", "SQK")
+        first = []
+        S2 = P["S2"][n]
+        for k in range(S2):
+            first.append(gat("S", ap("M5", S[:, :, k]), rw, c2("SKQ", 12 * k, 12 * k + 12)))
+            mm(c2("D%d" % (k // 2 % 2), k % 2, 384, 2), [(ap("ID"), ap("M5", S[:, :, k])), (ap("NID"), ap("Y"))])
+            if k % 2:
+                act(ap("M2", S[:, :, k - 1:k + 1]), c2("D%d" % (k // 2 % 2), 0, 384), AF.Relu)
+        for k in range(S2, 16):
+            first.append(tt(ap("M2", S[:, :, k]), ind(rw, c2("SKQ", 12 * k, 12 * k + 12)), ap("Y"), OP.min))
+        for o in first:
+            for h in (range(XH) if n == 0 else [XH + n - 1]):
+                ops[o]["ext"].append("r%d" % h)
+                ops[o]["after"].append(arrive[h])
+        if S2:
+            mm(ap("KA", S[:, 0:12, 0:S2]), [(ap("ID"), ap("KMX", S[:, :, 0:S2]))] + [(sel(r), ap("M5", S[:, r::16, 0:S2])) for r in range(16)]
+               + [(c2("NSEL", 15 - r, 143 - r), ap("M2", S[:, r::16, 0:S2])) for r in range(16)])
+        sums("KA", "M2", [(ap("ID"), "KMX")], [(S2, 12), (12, 16)])
+        cp(ap("SSL"), c2("S208", 0, 192))
+        sec[0] = "b"
+        for j in range(8):
+            gat("V" if (n == 0 and j % 2) else "S", c2("YW", 384 * j, 384 * j + 384), xw, c2("LK", 24 * j, 24 * j + 24))
+        dist("YW", "M1", ap("Z"))
+        if not last:
+            steps("KC", "LQ")
+        mm(kc, [(ap("ID"), ap("RI")), (ap("IBG"), ap("OH"))] + [(sel(r), ap("M1", S[:, r::16, :])) for r in range(16)])
+        scan(ap("KI"), ap("RBIG"), kc, 0.0, OP.add, OP.min)
+        ts(wn("JI"), ends("KI"), 15, OP.bitwise_and)
+        tt(wf("DB", 0, 16), wn("JI", 0, 16), wf("BB", 0, 16), OP.subtract)
+        ts(wf("JA", 0, 16), wn("JI", 0, 16), 192.0, OP.mult, -3072.0, OP.add)
+        if not last:
+            tt(ap("OHJ"), ap("KI"), kc, OP.not_equal)
+            scan(ap("LJ"), ap("OHJ"), c2("KC", 256, 448), 0.0, OP.mult, OP.add)
+            gat("S", wf("LT", 0, 16), ap("LJ"), wu("IE16", 0, 1))
+            cp(wu("LJU"), ends("LJ"))
+            tt(wf("DL", 0, 16), wf("LT", 0, 16), wf("LB", 0, 16), OP.subtract)
+            act(wf("LT4"), wf("LT"), AF.Identity, bias=4096.0)
+            gat("S", ap("TOLD"), c2("TT", 0, A_), wu("LJU"))
+            mm(c2("KC", 256, 448), [(ap("IDF"), c2("S208", 0, 192)), (ap("NIDF"), ap("TOLD"))])
+        act(wf("DS", 0, 48), wf("DL", 0, 48), AF.Identity, scale=1.0 / 4096)
+        act(wf("SL", 0, 16), wf("CC", 0, 16), AF.Copy)
+        if P["AS"]:
+            gat("S", ap("AW"), wf("LB", 0, 16), wu("IQ"))
+        else:
+            tt(ap("AW"), ind(wf("LB", 0, 16), wu("IQ")), c2("WQ", 0, 192), OP.subtract)
+        sec[0] = "c"
+        cp(ap("ST"), ka)
+        scan(ap("KS"), r01, ap("ST"), 0.0, OP.mult, OP.max)
+        tt(ap("NOH"), ap("KS"), ka, OP.not_equal)
+        o = ts(ap("BI"), ka, thc, OP.is_ge)
+        if n == 0:
+            ops[o]["ext"].append("th")
+            ops[o]["after"].append(tho)
+        scan(ap("PS"), ap("NOH"), side, 0.0, OP.mult, OP.add)
+        scan(ap("CN"), r01, ap("BI"), 0.0, OP.mult, OP.add)
+        ts(wf("NOC"), ends("CN"), NEED, OP.is_lt, 4096.0, OP.mult)
+        tt(wf("PV"), ends("PS"), wf("NOC"), OP.add)
+        cp(wu("PLU"), ends("PS"))
+        nv, no = ap("NV%d" % n), wu("NO%d" % n)
+        tt(ap("XS"), ind(rw, wu("PLU")), ap("Q4"), OP.subtract)
+        act(nv, ap("XS"), AF.Relu)
+        s1 = send([(nv, ap("OV%d" % n), HOPS[n], "eo%d" % n)], "loc", 2500)
+        lowest("PV", "A", "DU1", no)
+        cp(ind(ap(R), no), nv)
+        s2 = send([(no, wu("OO%d" % n), HOPS[n], "eo%d" % n)], "loc", 2500)
+        sec[0] = "d"
+        for j in range(4):
+            gat("V" if j < P["G4V"][n] else "S", c2("RAW4", 768 * j, 768 * j + 768), rw, c2("SSL", 48 * j, 48 * j + 48))
+        for j in range(4):
+            scan(c2("FS", 768 * j, 768 * j + 768), ap("R01"), c2("RAW4", 768 * j, 768 * j + 768), 0.0, OP.mult, OP.max)
+        cp(ind(ap("X"), wu("OO%d" % n)), ap("OV%d" % n), ext=["eo%d" % n], after=[s1, s2])
+        if last:
+            dma("Y", ap("yx"), xw, 4000)
+        else:
+            arrive[XH + n] = send([(xw, c2("R%d" % (n + 1), 0, V_), -HOPS[n + 1], "r%d" % (XH + n))], "l%d" % (XH + n), 8000)
+        for k in range(16):
+            tt(ap("M2", S[:, :, k]), c2("RAW4", k, 3072, 16), c2("YP", 0, 192), OP.min)
+        sums("KA", "M2", [], P["KC4"])
+        gat("S", c2("YW", 3072, 3264), rw, wu("PLU"))
+        ts(ap("BI"), ka, thc, OP.is_ge)
+        scan(ap("CN"), r01, ap("BI"), 0.0, OP.mult, OP.add)
+        ts(wf("O4"), ends("CN"), NEED, OP.is_lt, 4096.0, OP.mult)
+        tt(wf("O4"), wf("O4"), wf("NOC"), OP.max)
+        sec[0] = "e"
+        f, ns = c2("FS", 15, 3072, 16), 8 - P["G5V"][n]
+        for j in range(ns):
+            gat("S", c2("RAW5", 384 * j, 384 * j + 384), xw, c2("WK", 24 * j, 24 * j + 24))
+        dist("RAW5", "M5", f, ns)
+        for j in range(ns, 8):
+            for h in range(2):
+                tt(c2("RAW5", 384 * j + h, 384 * j + 384, 2), ind(xw, c2("WK", 24 * j + 12 * h, 24 * j + 12 * h + 12)), f, OP.subtract)
+            act(ap("M5", S[:, :, 2 * j:2 * j + 2]), c2("RAW5", 384 * j, 384 * j + 384), AF.Abs)
+        if not last:
+            tt(wf("PV2"), wf("LT4"), wf("O4"), OP.subtract)
+            lowest("PV2", "A2", "DU2", wu("O2"))
+        tt(wf("T1", 0, 48), ind(wf("O4", 0, 16), wu("IR3", 0, 3)), wf("DS", 0, 48), OP.mult)
+        tt(wf("LB", 0, 48), wf("LB", 0, 48), wf("T1", 0, 48), OP.add)
+        cp(wu("LBU", 0, 48), wf("LB", 0, 48))
+        if not last:
+            bound()
+            act(wf("E3"), wf("O4"), AF.Identity, scale=1.0 / 4096, accum_out=wf("C", 4, 5))
+            mm(c2("B1", 448, 449), [(ap("BLKF"), wf("C", 4, 5))])
+            act(wf("C", 5, 6), c2("B1", 448, 449), AF.Identity, bias=3.0)
+            act(wf("C", 6, 7), c2("B1", 448, 449), AF.Identity, bias=MAGIC, scale=HALF)
+            act(wf("C", 7, 8), wf("C", 6, 7), AF.Identity, bias=-MAGIC)
+            act(NEED, wf("C", 7, 8), AF.Identity, bias=wf("C", 5, 6), scale=-2.0)
+        if P["ZS"]:
+            gat("S", ap("XS"), ap("YW"), wu("SELU"))
+            mm(c2("B0", 256, 448), [(ap("ID"), ap("XS")), (ap("ID"), ap("Z"))])
+            act(ap("ZT"), c2("B0", 256, 448), AF.Identity, bias=MAGIC, scale=HALF)
+        else:
+            tt(ap("ZT"), ind(ap("YW"), wu("SELU")), ap("Z"), OP.add)
+            act(ap("ZT"), ap("ZT"), AF.Identity, bias=MAGIC, scale=HALF)
+        act(ap("Z"), ap("ZT"), AF.Identity, bias=-MAGIC)
+        sums("KB", "M5", [(ap("ID"), "KMN")])
+        if P["AS"]:
+            mm(c2("B1", 256, 448), [(ap("IDF"), ap("AW")), (ap("NIDF"), c2("WQ", 0, 192))])
+        sec[0] = "g" if last else "f"
+        act(ap("ST"), kb, AF.Copy)
+        scan(ap("KI"), ap("RBIG"), ap("ST"), 0.0, OP.add, OP.min)
+        ts(wn("WI"), ends("KI"), 15, OP.bitwise_and)
+        if not last:
+            tt(ap("EXW"), ind(wn("WI", 0, 16), wu("IQ")), ap("MR"), OP.mult)
+            mm(c2("B0", 0, 192), [(ap("BLKB"), ap("EXW"))])
+            ts(ap("MW"), c2("B0", 0, 192), PM, OP.is_equal)
+            tt(ap("MD"), ap("MW"), c2("KC", 256, 448), OP.mult)
+            tt(ind(ap("TT"), wu("O2")), ap("MD"), ap("TOLD"), OP.add)
+        tt(wf("WO"), wn("WI"), wf("O4"), OP.subtract)
+        tt(ap("OHW"), ind(wf("WO", 0, 16), wu("IQ")), ap("RIM"), OP.is_equal)
+        bw = c2("B1", 256, 448)
+        tt(bw, ap("OHW"), bw if P["AS"] else ap("AW"), OP.mult)
+        scan(ap("SW"), r01, bw, 0.0, OP.mult, OP.add)
+        tt(c2("WQ", 0, 192), c2("WQ", 0, 192), bw, OP.add)
+        tt(ap("CW"), ind(ap("SW"), wu("IE")), ap("OH"), OP.mult)
+        tt(c2("LQ", 0, 192), c2("LQ", 0, 192), ap("CW"), OP.subtract)
+        if not last:
+            gat("V", ap("LK"), c2("LQ", 0, 192), wu("PKQ"))
+            gat("V", ap("WK"), c2("WQ", 0, 192), wu("PKQ"))
+            tt(ap("OH"), ind(wf("BB", 0, 16), wu("IQ")), ap("RI"), OP.is_equal)
+    dma("Y", ap("yz"), ap("Z"), 2200)
+    tt(ap("EXW"), ind(wf("BB", 0, 16), wu("IQ")), ap("MR"), OP.mult)
+    mm(ap("B0", S[0:8, 0:192]), [(c2("BLKB", 0, 128, 16), ap("EXW"))])
+    act(ap("ZT", S[0:8, :]), ap("B0", S[0:8, 0:192]), AF.Copy)
+    dma("Y", ap("yb"), ap("ZT", S[0:8, :]), 2200)
+    for (src, t, o, y) in (("WQ", "TR2", "OW", "yw"), ("LQ", "TR", "OL", "yl")):
+        act(c2(src, 192, 208), c2(src, 0, 16), AF.Copy)
+        turn(src, t)
+        gat("S", ap(o), ap(t), wu("IQK"))
+        dma("Y", ap(y), ap(o), 2200)
+    return ops
+
+
+def links(ops):
+    pred = []
+    for o in ops:
+        p = {}
+        for d, wait in o["deps"].items():
+            p[d] = (P["OTHER"] if ops[d]["eng"] != o["eng"] else P["SAME"]) if wait else None
+        for d in o["after"]:
+            p[d] = P["OTHER"]
+        pred.append(p)
+    return pred
+
+
+def schedule(ops, bias=None):
+    n = len(ops)
+    pred = links(ops)
+    succ = [[] for _ in ops]
+    for i in range(n):
+        for d in pred[i]:
+            succ[d].append(i)
+    prio = [0.0] * n
+    for i in range(n - 1, -1, -1):
+        prio[i] = ops[i]["cost"] + max([prio[s] + (pred[s][i] or 0.0) for s in succ[i]] + [0.0])
+    if bias is not None:
+        prio = [p + float(b) for p, b in zip(prio, bias)]
+    left = [len(p) for p in pred]
+    start, fin = [0.0] * n, [0.0] * n
+    free = {e: 0.0 for e in "VSPGY"}
+    order = {e: [] for e in "VSPGY"}
+    ready = {i: 0.0 for i in range(n) if left[i] == 0}
+    while ready:
+        est = {i: max(t, free[ops[i]["eng"]]) for i, t in ready.items()}
+        i0 = min(est, key=lambda i: (est[i], -prio[i]))
+        e = ops[i0]["eng"]
+        i = max([j for j in est if ops[j]["eng"] == e and est[j] <= est[i0] + min(P["SLACK"], ops[i0]["busy"])], key=lambda j: prio[j])
+        start[i] = est[i]
+        fin[i] = est[i] + ops[i]["cost"]
+        free[e] = est[i] + ops[i]["busy"]
+        order[e].append(i)
+        del ready[i]
+        for s in succ[i]:
+            left[s] -= 1
+            if left[s] == 0:
+                ready[s] = max((fin[d] + l) if l is not None else start[d] for d, l in pred[s].items())
+    return order, start, fin
+
+
+def place_all(ops, seq, lag, first):
+    st = [0.0] * len(ops)
+    used = {e: ([], []) for e in "VSPGY"}
+    for i in seq:
+        t = first[i]
+        for d, l in lag[i]:
+            if st[d] + l > t:
+                t = st[d] + l
+        a, b = used[ops[i]["eng"]]
+        busy = ops[i]["busy"]
+        lo, hi = 0, len(b)
+        while lo < hi:
+            mid = (lo + hi) // 2
+            if b[mid] <= t:
+                lo = mid + 1
+            else:
+                hi = mid
+        while lo < len(a) and a[lo] < t + busy:
+            t = b[lo]
+            lo += 1
+        a.insert(lo, t)
+        b.insert(lo, t + busy)
+        st[i] = t
+    return st
+
+
+def refine(ops, start, rounds, judge=None):
+    n = len(ops)
+    pred = links(ops)
+    above, fwd = [], []
+    for i in range(n):
+        far = 0
+        for d in pred[i]:
+            far |= above[d]
+        fwd.append([(d, 1.0 if l is None else ops[d]["cost"] + l) for d, l in pred[i].items() if not far >> d & 1 or ops[d]["dma"]])
+        for d in pred[i]:
+            far |= 1 << d
+        above.append(far)
+    bwd = [[] for _ in ops]
+    for i in range(n):
+        for d, l in fwd[i]:
+            bwd[d].append((i, l + ops[i]["busy"] - ops[d]["busy"] if l > 1.0 else 1.0))
+    tail = [o["cost"] - o["busy"] for o in ops]
+    zero = [0.0] * n
+    rng = np.random.default_rng(P["SEED"])
+
+    def topo(key, lag, rev):
+        k = list(key)
+        for i in (range(n - 1, -1, -1) if rev else range(n)):
+            for d, _ in lag[i]:
+                if k[d] >= k[i]:
+                    k[i] = k[d] + 1e-3
+        return sorted(range(n), key=lambda i: k[i])
+
+    def worth(st):
+        return judge(st) if judge else max(st[i] + ops[i]["cost"] for i in range(n))
+
+    best, bst = worth(start), list(start)
+    tags = sorted(set(o["tag"] for o in ops if o["tag"][0] != "i"))
+    now, cst = best, bst
+    for it in range(rounds):
+        kind = rng.random()
+        if kind < 0.6:
+            shift = {tags[int(rng.integers(len(tags)))]: float(rng.normal() * rng.choice([300.0, 1500.0, 5000.0])) for _ in range(int(rng.integers(1, 4)))}
+            cur = [s + shift.get(o["tag"], 0.0) for s, o in zip(cst, ops)]
+        else:
+            lo = float(rng.random()) * best
+            noise = rng.normal(size=n) * float(rng.choice([100.0, 400.0, 1500.0]))
+            cur = [s + float(x) if lo <= s < lo + 8000.0 else s for s, x in zip(cst, noise)]
+        if rng.random() < 0.5:
+            r = place_all(ops, topo([-(cur[i] + ops[i]["busy"]) for i in range(n)], bwd, True), bwd, tail)
+            cur = [-(r[i] + ops[i]["busy"]) for i in range(n)]
+        st = place_all(ops, topo(cur, fwd, False), fwd, zero)
+        v = worth(st)
+        if v <= now + P["HEAT"] * (1.0 - it / rounds) * rng.random():
+            now, cst = v, st
+        if v < best:
+            best, bst = v, st
+    order = {e: sorted([i for i in range(n) if ops[i]["eng"] == e], key=lambda i: bst[i]) for e in "VSPGY"}
+    return order, bst
+
+
+PLAN = {}
+
+
+def rank_program(g, core, T, topo):
+    rank = T.rank_of(core)
+    if rank is None:
+        return
+    if not PLAN:
+        PLAN["ops"] = build()
+        PLAN["order"] = refine(PLAN["ops"], schedule(PLAN["ops"])[1], P["ROUNDS"])[0]
+    ops, order = PLAN["ops"], PLAN["order"]
+    N = len(T.cores)
+    q = {"V": g.vector, "S": g.scalar, "P": g.tensor, "G": g, "Y": g.sync}
+    place = {i: n for e in order for n, i in enumerate(order[e])}
+    waits = []
+    for o in ops:
+        far = {}
+        for d, wait in o["deps"].items():
+            key = d if ops[d]["dma"] else ops[d]["eng"]
+            if wait and (key not in far or place[d] > place[far[key]]):
+                far[key] = d
+        waits.append(list(far.values()))
+    needed = set(d for w in waits for d in w)
+    mark, total = {}, {}
+    for e in "VSPGY":
+        for i in order[e]:
+            o = ops[i]
+            if o["dma"]:
+                sem, inc = o["dma"]
+                if inc is None:
+                    parts = o["calls"][0][1][1]
+                    per = min(len(topo.engines(core, T.cores[(rank + p[2]) % N])) for p in parts) // len(parts)
+                    inc = per * len(parts)
+                    for p in parts:
+                        total[p[3]] = total.get(p[3], 0) + per
+            elif i in needed:
+                sem, inc = "c" + e, 1
+            else:
+                continue
+            total[sem] = total.get(sem, 0) + inc
+            mark[i] = (sem, total[sem])
+
+    def real(a):
+        if isinstance(a, tuple) and a[0] == "ap":
+            return T[a[1]][a[2]]
+        if isinstance(a, tuple) and a[0] == "ind":
+            return real(a[1]).indirect(real(a[2]))
+        return a
+
+    meth = {"tensor_copy": lambda e: e.tensor_copy, "tensor_tensor": lambda e: e.tensor_tensor, "tensor_scalar": lambda e: e.tensor_scalar,
+            "tensor_tensor_scan": lambda e: e.tensor_tensor_scan, "tensor_reduce": lambda e: e.tensor_reduce, "transpose": lambda e: e.transpose,
+            "memset": lambda e: e.memset, "activation": lambda e: e.activation, "matmul": lambda e: e.matmul, "iota": lambda e: e.iota,
+            "dma_start": lambda e: e.dma_start, "partition_broadcast": lambda e: e.partition_broadcast}
+    for e in "VSPYG":
+        seen = {}
+        for i in order[e]:
+            o = ops[i]
+            want = {}
+            for (sem, val) in [mark[d] for d in waits[i]] + [(s, total[s]) for s in o["ext"]]:
+                want[sem] = max(want.get(sem, 0), val)
+            for sem, val in want.items():
+                if seen.get(sem, 0) < val:
+                    q[e].wait_ge(T.sem[sem], val)
+                    seen[sem] = val
+            for (name, args, kw) in o["calls"]:
+                if name == "send":
+                    parts = args[1]
+                    trs = []
+                    for n, (src, dst, off, sem) in enumerate(parts):
+                        peer = T.cores[(rank + off) % N]
+                        eng = topo.engines(core, peer)
+                        per = len(eng) // len(parts)
+                        rid, pid = topo.addr(peer, core)
+                        trs.append(RemoteDMATransfer(dst_ids=[DstId(rid=rid, pnc=pid)], dma_engine_mask=sum(1 << x for x in eng[n * per:(n + 1) * per]),
+                                                     remote_sem=T.sem[sem], src=real(src), dst=real(dst)))
+                    g.remote_dma_fused(trs, local_sem=T.sem[o["dma"][0]])
+                else:
+                    ins = meth[name](q[e])(*[real(a) for a in args], **{k: real(v) for k, v in kw.items()})
+            if i in mark and o["calls"][0][0] != "send":
+                ins.then_inc(T.sem[mark[i][0]], o["dma"][1] if o["dma"] else 1)
+        if e == "G":
+            for sem, val in total.items():
+                if seen.get(sem, 0) < val:
+                    g.wait_ge(T.sem[sem], val)

@@ -5,21 +5,21 @@ from concourse.mybir import AluOpType as OP, AxisListType, ActivationFunctionTyp
 V_, A_, M_, RO = 2048, 1024, 192, 4
 HOPS = [1, 2, 4, 7]
 S = np.s_
-F, B, I, U = "float32", "bfloat16", "int32", "uint16"
-SEG = [8 * q * (q + 1) for q in range(13)]
+F, B, I, U, H = "float32", "bfloat16", "int32", "uint16", "float16"
+X0, R0 = 16, 16 + A_
+FA, OWN = V_ + M_, V_ + M_ + 16
+MB_ = 6
+SEG = [(q // MB_) * 8 * MB_ * (MB_ + 1) + 8 * (q % MB_) * (q % MB_ + 1) for q in range(13)]
 NP = SEG[12]
-MAGIC, HALF = 12582912.0, 0.5 - 2.0 ** -11
 
 P = {"S2": [4, 4, 4, 4],
-     "G4V": [2, 2, 2, 2],
-     "G5V": [0, 0, 0, 2],
-     "ZS": 1, "AS": 1,
-     "PS1": 6,
-     "KCH": [(0, 10), (10, 16)], "KC4": [(0, 10), (10, 16)],
-     "CY": 1.04, "PE": 0.55, "GA": 1.56, "SC": 3.8, "TT": 2.0, "FIX": 20.0, "SAME": 60.0, "OTHER": 120.0, "SLACK": 150.0, "NET": 1.0,
-     "SEED": 0, "ROUNDS": 5000, "HEAT": 800.0}
-XH = 2
-SAMEQ_WAR = True
+     "A4": 8,
+     "G1V": [(0, 2, 4), (), (), ()],
+     "G5V": [(0, 2), (0, 2), (0, 2), (0, 2)],
+     "DB": {"1": "01", "2": "2", "4": "012", "5": "012"},
+     "C2": [(4, 10), (0, 4), (10, 16)], "O4": 0, "ZS": 1, "M0S": 0, "SCAN3": 0, "WAW": 1, "EBV": 8, "NS1": (5, 11, 4, 10), "NS2": (),
+     "CY": 0.87, "PE": 0.46, "GA": 1.56, "SC": 3.8, "TT": 2.0, "FIX": 20.0, "SAME": 150.0, "OTHER": 200.0, "SLACK": 150.0, "NET": 1.1,
+     "SEED": 0, "ROUNDS": 4000, "HEAT": 800.0}
 
 SCRATCH = {}
 
@@ -29,43 +29,46 @@ def _sb(names, shape, dt):
         SCRATCH[n] = ("sbuf", list(shape), dt)
 
 
-_sb("X R0 R1 R2 R3", [128, 2240], B)
-_sb("TT", [128, 1216], F)
-_sb("SBI", [128, 1024], I)
-_sb("LAI LWI KI Q4 B0I", [128, 192], I)
-_sb("S208 LQ WQ", [128, 208], F)
-_sb("TR TR2", [128, 384], F)
-_sb("EX", [128, 192], "float16")
-_sb("BLKH", [128, 128], "float16")
-_sb("SQK KS ST PS TOLD MD OHW AW SW CW LJ ZT OL OW RIM", [128, 192], F)
-_sb("Z Y RI RV MR MRV RBIG BI CN OH OHJ EXW XS MW NV0 NV1 NV2 NV3 OV0 OV1 OV2 OV3 NOH", [128, 192], B)
-_sb("SKQ SSL LK WK", [128, 192], U)
-_sb("M1 M2 M5", [128, 192, 16], B)
-_sb("KMN KMX", [128, 12, 16], B)
-_sb("RAW4 FS RAW5", [128, 3072], B)
-_sb("YW", [128, 3264], B)
+_sb("XR0 XR1 XR2 XR3 XR4", [128, OWN + FA], B)
+_sb("NV0 NV1 NV2 NV3 OV0 OV1 OV2 OV3", [128, 192], B)
+_sb("NO OO", [128, 64], U)
 _sb("NE FL MM", [128, NP], B)
-_sb("R01", [128, 768], B)
-_sb("SEL NSEL", [128, 144], B)
+_sb("TT", [128, R0 + M_], F)
+_sb("SBI", [128, R0], I)
+_sb("LAI LWI KI B0I", [128, 192], I)
+_sb("GG", [128, 224], F)
+_sb("TR", [128, 416], F)
+_sb("KS ST PS TOLD MD THR OL OW OB", [128, 192], F)
+_sb("EXP Z ZT LJM LJX MBR BW SQK L1 W", [128, 192], H)
+_sb("Z0 Y RI RV RBIG R01 MRV BI CN NOH XS Q MW MJ MB ZO VW VA", [128, 192], B)
+_sb("SKQ LK WK", [128, 192], U)
+_sb("M1 M2 M5", [128, 192, 16], B)
+_sb("KMX", [128, 12, 16], B)
+_sb("A4 FS D4 RAW1 RAW5", [128, 3072], B)
+_sb("SEL NSEL SE1 NSE1", [128, 144], B)
 _sb("T143", [128, 144], F)
-_sb("BLKF IDF NIDF", [128, 128], F)
-_sb("BLKB ID NID IBG E8", [128, 128], B)
+_sb("IDF NIDF BLKF", [128, 128], F)
+_sb("BLK NBLK ID NID E8 IOB", [128, 128], B)
+_sb("EB", [128, 2048], B)
 _sb("WF", [128, 512], F)
 _sb("WN", [128, 128], I)
-_sb("WU", [128, 448], U)
+_sb("WU", [128, 256], U)
+_sb("WH", [128, 128], H)
+_sb("WB", [128, 64], B)
 _sb("TH", [128, 16], F)
 _sb("THI THB", [128, 8], I)
-for _n in "KA KB".split():
-    SCRATCH[_n] = ("psum", [128, 32, 16], F)
-for _n in "D0 D1 YP B0 B1 KC".split():
+SCRATCH["KA"] = ("psum", [128, 32, 16], F)
+for _n in "D0 D1 D2 KB PA PB PC".split():
     SCRATCH[_n] = ("psum", [128, 512], F)
 
-WFN = "PV A PV2 A2 WO O4 LB BB SL DL DB JA NOC LT J Q E1 E2 E3 DU1 DU2 CC C T1 T2 T3 DS DS2 DS3 THM LT4".split()
-WNN = "P JI WI N1 N2 KK".split()
-WUN = "IQ IE IR IEND IQK IKQ PKQ IE16 IR3 LBU BBU SELU PLU LJU O2 NO0 NO1 NO2 NO3 OO0 OO1 OO2 OO3".split()
+TABS = {"WF": "LJ LB PL BB DL DP DB T1 T1b T1c OCC C4 E16 E1 E2 SY A A2 AM J Q C DU1 DU2 HE T2 T3 THM".split(),
+        "WN": "P JI WI N1 N2 KK J0".split(),
+        "WU": "LBU SELU PLU LJU IQ IQK IKQ IR WWU O2 IRV IEND".split(),
+        "WH": "XL JB LBH".split(),
+        "WB": "EX WB BH".split()}
 
-SEMAPHORES = (["cV", "cS", "cP", "cG", "loc", "th"] + ["d%d" % i for i in range(16)] + ["r%d" % i for i in range(3 + XH)]
-              + ["l%d" % i for i in range(3 + XH)] + ["eo%d" % i for i in range(4)])
+SEMAPHORES = (["cV", "cS", "cP", "cG", "loc", "th"] + ["d%d" % i for i in range(20)] + ["r%d" % i for i in range(5)]
+              + ["x%d" % i for i in range(4)])
 IOS = "xs sb la lw z0 b0 th yx yl yw yz yb".split()
 
 
@@ -77,16 +80,13 @@ def c2(name, a, b, s=1):
     return ap(name, S[:, a:b:s])
 
 
-def wf(n, a=0, b=12):
-    return c2("WF", 16 * WFN.index(n) + a, 16 * WFN.index(n) + b)
+def tab(t):
+    def f(n, a=0, b=12, s=1):
+        return c2(t, 16 * TABS[t].index(n) + a, 16 * TABS[t].index(n) + b, s)
+    return f
 
 
-def wn(n, a=0, b=12):
-    return c2("WN", 16 * WNN.index(n) + a, 16 * WNN.index(n) + b)
-
-
-def wu(n, a=0, b=12):
-    return c2("WU", 16 * WUN.index(n) + a, 16 * WUN.index(n) + b)
+wf, wn, wu, wh, wb = tab("WF"), tab("WN"), tab("WU"), tab("WH"), tab("WB")
 
 
 def ind(win, off):
@@ -99,9 +99,17 @@ def cols(a):
     return np.arange(int(np.prod(shape[1:]))).reshape(shape[1:])[idx[1:]].reshape(-1)
 
 
+def bits(a):
+    m = 0
+    for x in cols(a):
+        m |= 1 << int(x)
+    return m
+
+
 def build():
     ops = []
     acc = {}
+    lands = {}
     sec = ["i"]
     CY = P["CY"]
 
@@ -109,9 +117,11 @@ def build():
         if a[1] in IOS:
             return
         psum = SCRATCH[a[1]][0] == "psum"
-        m = 0
-        for x in cols(a):
-            m |= 1 << int(x)
+        m = bits(a)
+        for (lm, sem, o) in lands.get(a[1], []):
+            if lm & m and o not in me["after"]:
+                me["ext"].append(sem)
+                me["after"].append(o)
         for (o, om, ow) in acc.setdefault(a[1], []):
             if o == me["id"]:
                 continue
@@ -120,18 +130,20 @@ def build():
             if hit and ow and not write:
                 me["deps"][o] = True
             elif (hit and (write or ow)) or (psum and ops[o]["eng"] != me["eng"]):
-                me["deps"][o] = me["deps"].get(o, False) or other or SAMEQ_WAR
+                me["deps"][o] = me["deps"].get(o, False) or other or not ow or bool(P["WAW"])
+            elif psum and me["eng"] == "P":
+                me["deps"].setdefault(o, False)
         acc[a[1]].append((me["id"], m, write))
 
-    def add(eng, calls, cost, dma=None, after=(), ext=(), busy=None):
-        me = {"id": len(ops), "eng": eng, "calls": calls, "cost": cost, "dma": dma, "deps": {}, "ext": list(ext),
-              "busy": cost if busy is None else busy, "after": list(after)}
+    def add(eng, calls, cost, dma=None, busy=None):
+        me = {"id": len(ops), "eng": eng, "calls": calls, "cost": cost, "dma": dma, "deps": {}, "ext": [],
+              "busy": cost if busy is None else busy, "after": []}
         ops.append(me)
         a = calls[0][1][0]
         if a is None or a[0] == "ind":
             name = "send" if a is None else a[1][1][0] + "s"
-        elif a[1] in ("WF", "WN", "WU"):
-            name = {"WF": WFN, "WN": WNN, "WU": WUN}[a[1]][a[2][1].start // 16]
+        elif a[1] in TABS:
+            name = TABS[a[1]][a[2][1].start // 16]
         else:
             name = a[1]
         me["tag"] = sec[0] + eng + name
@@ -154,10 +166,10 @@ def build():
         return P["FIX"] + max(64, len(cols(in0)) * rate) * CY
 
     def half(*aps):
-        return 0.5 if all(a[0] == "ap" and SCRATCH[a[1]][2] in (B, U) for a in aps) else 1.0
+        return 0.5 if all(a[0] == "ap" and SCRATCH[a[1]][2] in (B, U, H) for a in aps) else 1.0
 
-    def cp(out, in_, **k):
-        return add("V", [("tensor_copy", [out, in_], {})], vcost("V", out, in_, half(out, in_)), **k)
+    def cp(out, in_):
+        return add("V", [("tensor_copy", [out, in_], {})], vcost("V", out, in_, half(out, in_)))
 
     def tt(out, a, b, op):
         ps = any(x[0] == "ap" and SCRATCH[x[1]][0] == "psum" for x in (a, b))
@@ -174,7 +186,7 @@ def build():
         return add("V", [("tensor_reduce", [out, a, AxisListType.X, op], {})], vcost("V", out, a, 1.0))
 
     def tr(out, a):
-        return add("V", [("transpose", [out, a], {})], vcost("V", out, a, 1.0))
+        return add("V", [("transpose", [out, a], {})], vcost("V", out, a, half(out, a)))
 
     def ms(out, v):
         return add("V", [("memset", [out, v], {})], vcost("V", out, out, half(out)))
@@ -185,12 +197,16 @@ def build():
     def gat(eng, out, win, off):
         return cp(out, ind(win, off)) if eng == "V" else act(out, ind(win, off), AF.Copy)
 
-    def mm(out, pairs):
+    def mms(groups):
         calls, cost = [], 60
-        for n, (l, r) in enumerate(pairs):
-            calls.append(("matmul", [out, l, r, n == 0, n == len(pairs) - 1], {}))
-            cost += max(64, len(cols(r))) * P["PE"] * (4 if SCRATCH[l[1]][2] == F else 1)
+        for out, pairs in groups:
+            for n, (l, r) in enumerate(pairs):
+                calls.append(("matmul", [out, l, r, n == 0, n == len(pairs) - 1], {}))
+                cost += max(min(64, len(cols(l))), len(cols(r))) * P["PE"] * (4 if SCRATCH[l[1]][2] == F else 1)
         return add("P", calls, cost)
+
+    def mm(out, pairs):
+        return mms([(out, pairs)])
 
     def iota(out, pat, base, cm):
         kw = {} if SCRATCH[out[1]][2] == I else {"allow_small_or_imprecise_dtypes": True}
@@ -202,88 +218,113 @@ def build():
         nd[0] += 1
         return add(eng, [("dma_start", [out, in_], {})], cost, dma=("d%d" % (nd[0] - 1), 16), busy=60)
 
-    def send(parts, loc, cost, busy=1000):
-        return add("G", [("send", [None, parts] + [("rd", p[0]) for p in parts], {})], cost * P["NET"], dma=(loc, None), busy=busy)
+    def send(parts, cost, busy=1000):
+        o = add("G", [("send", [None, parts] + [("rd", p[0]) for p in parts], {})], cost * P["NET"], dma=("loc", None), busy=busy)
+        for p in parts:
+            lands.setdefault(p[1][1], []).append((bits(p[1]), p[3], o))
+        return o
 
-    def sel(r):
-        return c2("SEL", 15 - r, 143 - r)
+    def sel(r, t="SEL"):
+        return c2(t, 15 - r, 143 - r)
 
-    def sums(bank, m, extra, ranges=None):
-        for (a, b) in ranges or P["KCH"]:
-            out = ap(bank, S[:, 0:12, a:b])
-            mm(out, [(l, ap(t, S[:, 0:12, a:b])) for (l, t) in extra] + [(sel(r), ap(m, S[:, r::16, a:b])) for r in range(16)])
+    def eb(b, t="EB"):
+        return c2(t, 128 * b, 128 * b + 128)
 
     def ends(name):
         return c2(name, 15, 192, 16)
 
-    PM, WC, NEED = wf("C", 0, 1), wf("C", 1, 2), wf("C", 2, 3)
-    r01 = c2("R01", 0, 192)
-    xw = c2("X", 0, V_)
+    def spread(bank, src, stop=True):
+        n = len(cols(src))
+        calls = [("matmul", [ap(bank, S[:, 16:28, b]) if bank == "KA" else c2(bank, b, 16 * n, 16), eb(b), src, b == 0, stop and b == 15], {}) for b in range(16)]
+        return add("P", calls, 60 + 16 * 64 * P["PE"])
 
-    w = V_ // XH
-    for h in range(XH):
-        dma("Y", c2("X", h * w, (h + 1) * w), ap("xs", S[:, h * w:(h + 1) * w]), 2600 + 900 * h)
+    def more(out, l, r):
+        return add("P", [("matmul", [out, l, r, False, True], {"acc": out})], 60 + len(cols(r)) * P["PE"])
+
+    def pick(out, src, t="SE1", plus=None):
+        mm(out, ([(ap("ID"), plus)] if plus else []) + [(sel(r, t), c2(src, r, 192, 16)) for r in range(16)])
+
+    PM, WC, PAR, PM16, DUM = (wf("C", n, n + 1) for n in range(5))
+    r01 = ap("R01")
+
+    dma("Y", c2("XR0", OWN, OWN + A_), ap("xs", S[:, 0:A_]), 2600)
+    dma("Y", c2("XR0", OWN + A_, OWN + V_), ap("xs", S[:, A_:V_]), 3500)
     dma("S", ap("B0I", S[0:8, :]), ap("b0"), 2200)
     dma("S", ap("LAI"), ap("la"), 2500)
     dma("S", ap("THI", S[0:1, :]), ap("th"), 2200)
-    dma("Y", ap("SBI"), ap("sb"), 5000)
+    dma("S", ap("Z0"), ap("z0"), 3000)
+    dma("Y", c2("SBI", X0, R0), ap("sb"), 5000)
     dma("S", ap("LWI"), ap("lw"), 3000)
-    dma("S", ap("Z"), ap("z0"), 3000)
-    arrive = {}
-    for h in range(XH):
-        arrive[h] = send([(c2("X", h * w, (h + 1) * w), c2("R0", h * w, (h + 1) * w), -HOPS[0], "r%d" % h)], "l%d" % h,
-                         6000 if h == 0 else 6500, busy=2500 if h == 0 else 1000)
+    send([(c2("XR0", OWN, OWN + A_), c2("XR0", 0, A_), -HOPS[0], "r0")], 6000, busy=2500)
+    send([(c2("XR0", OWN + A_, OWN + V_), c2("XR0", A_, V_), -HOPS[0], "r1")], 6500)
     iota(wn("P", 0, 1), [[0, 1]], 0, 1)
-    iota(ap("RI"), [[0, 12], [1, 16]], 0, 0)
     iota(wf("Q", 0, 16), [[1, 16]], 0, 0)
-    iota(ap("BLKF"), [[-16, 8], [0, 16]], 0, 1)
-    iota(ap("E8", S[0:8, :]), [[-1, 8], [0, 16]], 0, 1)
     iota(ap("T143"), [[-1, 144]], 15, 1)
+    iota(ap("IOB"), [[-16, 8], [0, 16]], 0, 1)
+    iota(ap("E8", S[0:8, :]), [[-1, 8], [0, 16]], 0, 1)
+    iota(ap("RI"), [[0, 12], [1, 16]], 0, 0)
+    for h in range(4):
+        iota(c2("D4", 768 * h, 768 * h + 768), [[0, 768]], 0, 0)
     ts(wn("P", 1, 2), wn("P", 0, 1), 15, OP.bitwise_and)
     ts(wn("P", 2, 3), wn("P", 0, 1), 4, OP.arith_shift_right, 1, OP.bitwise_and)
     cp(wf("C", 0, 2), wn("P", 1, 3))
-    ms(NEED, 3.0)
-    ts(wf("C", 3, 4), WC, 192.0, OP.mult)
+    ms(PAR, 0.0)
+    ts(PM16, PM, 16.0, OP.add)
+    for n in range(RO + 1):
+        ms(c2("XR%d" % n, V_ if n < RO else FA, OWN), 1024.0)
+    ms(c2("TT", 0, X0), 0.0)
+    ms(c2("SBI", 0, X0), 0)
+    ms(ap("GG"), 0.0)
+    ms(wf("LJ", 0, 16 * 19), 0.0)
+    ms(wb("EX", 0, 16), 0.0)
+    cp(wh("JB", 0, 32), wf("PL", 0, 32))
     ts(ap("E8", S[0:8, :]), ap("E8", S[0:8, :]), 0.0, OP.is_equal)
-    ts(ap("MR"), ap("RI"), PM, OP.is_equal)
-    act(ap("RV"), ap("RI"), AF.Identity, scale=-1.0, bias=15.0)
-    ts(ap("MRV"), ap("RV"), PM, OP.is_equal)
-    ts(ap("RBIG"), ap("RI"), 0.0, OP.is_equal, 1048576.0, OP.mult)
-    ts(ap("BLKB"), ap("BLKF"), PM, OP.is_equal)
-    act(ap("BLKF"), ap("BLKB"), AF.Copy)
-    cp(ap("BLKH"), ap("BLKB"))
-    ts(ap("SEL"), ap("T143"), PM, OP.is_equal, 16.0, OP.mult)
-    act(ap("NSEL"), ap("SEL"), AF.Identity, scale=-1.0)
+    ts(ap("SE1"), ap("T143"), PM, OP.is_equal)
+    act(ap("SEL"), ap("SE1"), AF.Identity, scale=16.0)
+    act(ap("NSEL"), ap("SE1"), AF.Identity, scale=-16.0)
     ts(ap("ID"), c2("T143", 15, 143), 0.0, OP.is_equal)
     act(ap("NID"), ap("ID"), AF.Identity, scale=-1.0)
-    act(ap("IBG"), ap("ID"), AF.Identity, scale=65536.0)
     act(ap("IDF"), ap("ID"), AF.Copy)
     act(ap("NIDF"), ap("ID"), AF.Identity, scale=-1.0)
-    ms(ap("R01"), 1.0)
-    ms(c2("R01", 0, 768, 16), 0.0)
-    ts(wf("J", 0, 16), wf("Q", 0, 16), 16.0, OP.mult, PM, OP.add)
+    ts(ap("BLK"), ap("IOB"), PM, OP.is_equal)
+    act(ap("NBLK"), ap("BLK"), AF.Identity, scale=-1.0)
+    act(ap("BLKF"), ap("BLK"), AF.Identity, scale=1.0 / 16)
+    act(ap("RV"), ap("RI"), AF.Identity, scale=-1.0, bias=15.0)
+    act(ap("KMX"), ap("RV"), AF.Copy)
+    ts(ap("MRV"), ap("RV"), PM, OP.is_equal)
+    ms(ap("MM"), 0.0)
+    ts(c2("MM", 0, 16), c2("RV", 0, 16), PM, OP.is_ge)
+    for q in range(1, 12):
+        act(c2("MM", SEG[q], SEG[q] + 16), c2("MM", 0, 16), AF.Copy)
+    ts(ap("RBIG"), ap("RI"), 0.0, OP.is_equal, 1048576.0, OP.mult)
+    ts(ap("R01"), ap("RI"), 0.0, OP.not_equal)
+    ms(c2("D4", 0, 3072, 16), -1024.0)
+    act(ap("NSE1"), ap("SE1"), AF.Identity, scale=-1.0)
+    ts(wf("HE", 0, 16), wf("Q", 0, 16), PM, OP.is_equal)
+    for b in range(16):
+        if b < P["EBV"]:
+            ts(eb(b), ap("BLK"), wf("HE", b, b + 1), OP.mult)
+        else:
+            act(eb(b), ap("BLK"), AF.Identity, scale=wf("HE", b, b + 1))
     cp(wu("IQ"), wf("Q"))
-    ts(wu("IE"), wf("Q"), 16.0, OP.mult, 15.0, OP.add)
-    ts(wu("IR"), wf("Q"), -1.0, OP.mult, 11.0, OP.add)
+    ts(wu("IR", 0, 3), wf("Q", 0, 3), 0.0, OP.mult, PM, OP.add)
+    ts(wu("IRV"), wf("Q"), -1.0, OP.mult, 11.0, OP.add)
+    ts(wf("J", 0, 16), wf("Q", 0, 16), 16.0, OP.mult, PM, OP.add)
     act(wf("DU1"), wf("J"), AF.Identity, bias=float(V_))
-    act(wf("DU2"), wf("J"), AF.Identity, bias=float(A_))
-    act(wf("CC", 0, 16), wf("J", 0, 16), AF.Identity, bias=3072.0)
-    ms(wf("PV", 0, 16 * 14), 0.0)
-    ms(wn("JI", 0, 32), 0)
-    ts(wf("T1", 0, 1), PM, 11.0, OP.min, 1.0, OP.add)
-    ts(wf("T1", 1, 2), wf("T1", 0, 1), 1.0, OP.add, wf("T1", 0, 1), OP.mult)
-    ts(wu("IEND", 0, 1), wf("T1", 1, 2), 8.0, OP.mult, -1.0, OP.add)
-    ts(wf("T1", 2, 3), PM, 12.0, OP.is_lt, PM, OP.mult)
-    ts(wu("IE16", 0, 1), wf("T1", 2, 3), 16.0, OP.mult, 15.0, OP.add)
-    ts(wu("IR3", 0, 3), wf("Q", 0, 3), 0.0, OP.mult, wf("T1", 2, 3), OP.add)
+    act(wf("DU2"), wf("J"), AF.Identity, bias=float(R0))
+    t3 = [wf("T3", x, x + 1) for x in range(8, 13)]
+    ts(t3[0], PM, 11.0, OP.min, 1.0, OP.add)
+    ts(wn("N1", 12, 13), t3[0], 1.0 / MB_, OP.mult, -0.5 - 0.5 / MB_, OP.add)
+    ts(t3[1], wn("N1", 12, 13), -float(MB_), OP.mult, t3[0], OP.add)
+    ts(t3[2], t3[1], 1.0, OP.add, t3[1], OP.mult)
+    ts(t3[3], wn("N1", 12, 13), float(MB_ * (MB_ + 1)), OP.mult, t3[2], OP.add)
+    ts(wu("IEND", 0, 1), t3[3], 8.0, OP.mult, -1.0, OP.add)
 
     def turned(dst, qq, base):
         ts(wn("N1"), qq, WC, OP.add)
         ts(wn("N2"), wn("N1"), 1, OP.bitwise_and)
-        ts(wf("T2"), wn("N2"), 176.0, OP.mult)
+        ts(wf("T2"), wn("N2"), 208.0, OP.mult)
         tt(wf("T2"), wf("T2"), base, OP.add)
-        ts(wf("T3"), qq, 0.0, OP.is_equal, wf("C", 3, 4), OP.mult)
-        tt(wf("T2"), wf("T2"), wf("T3"), OP.add)
         cp(dst, wf("T2"))
 
     turned(wu("IQK"), wf("Q"), wf("J"))
@@ -292,240 +333,279 @@ def build():
     tt(wf("E1"), wf("E1"), wf("J"), OP.add)
     ts(wf("E2"), wf("E1"), 16.0, OP.mult)
     tt(wf("E2"), wf("E2"), wn("KK"), OP.add)
-    cp(wu("PKQ"), wf("E2"))
     turned(wu("IKQ"), wf("E1"), wf("E2"))
-    ms(ap("MM"), 0.0)
-    ts(c2("MM", 0, 16), c2("RV", 0, 16), PM, OP.is_ge)
-    for q in range(1, 12):
-        act(c2("MM", SEG[q], SEG[q] + 16), c2("MM", 0, 16), AF.Copy)
-    act(ap("KMN"), ap("RI"), AF.Copy)
-    act(ap("KMX"), ap("RV"), AF.Copy)
-    act(ap("RIM"), ap("RI"), AF.Identity, bias=-4096.0)
     add("G", [("partition_broadcast", [ap("THB"), ap("THI", S[0:1, :]), 128], {})], 180)
-    tt(wf("THM", 0, 8), ap("THB"), c2("SEL", 15, 143, 16), OP.mult)
+    ts(wf("T3", 0, 8), c2("BLK", 0, 128, 16), 16.0, OP.mult)
+    tt(wf("THM", 0, 8), ap("THB"), wf("T3", 0, 8), OP.mult)
     red(wf("THM", 8, 9), wf("THM", 0, 8), OP.add)
-    tho = send([(wf("THM", 8, 9), c2("TH", 4 * n, 4 * n + 1), -HOPS[n], "th") for n in range(RO)], "loc", 3000)
+    send([(wf("THM", 8, 9), c2("TH", 4 * n, 4 * n + 1), -HOPS[n], "th") for n in range(RO)], 3000)
 
-    def turn(src, dst):
-        tr(c2(dst, 0, 192), c2(src, 0, 192))
-        tr(c2(dst, 192, 384), c2(src, 16, 208))
-
-    for (src, dst, t, u) in (("LAI", "LQ", "TR", "LK"), ("LWI", "WQ", "TR2", "WK")):
-        cp(c2("S208", 0, 192), ap(src))
-        cp(c2("S208", 192, 208), c2(src, 0, 16))
-        turn("S208", t)
-        gat("V", ap(u), ap(t), wu("IKQ"))
-        gat("S", c2(dst, 0, 192), ap(t), wu("IQK"))
+    lp, wp = c2("PC", 0, 192), c2("PC", 256, 448)
+    small, small2 = c2("PC", 192, 204), c2("PC", 448, 460)
+    ts(ap("L1"), ap("LAI"), float(X0), OP.add)
     cp(ap("BI", S[0:8, :]), ap("B0I", S[0:8, :]))
-    mm(c2("B0", 0, 192), [(ap("E8", S[0:8, :]), ap("BI", S[0:8, :]))])
-    tt(ap("ST"), c2("B0", 0, 192), ap("MR"), OP.mult)
-    scan(ap("PS"), r01, ap("ST"), 0.0, OP.mult, OP.add)
-    cp(wf("BB"), ends("PS"))
-    tt(ap("OH"), ind(wf("BB", 0, 16), wu("IQ")), ap("RI"), OP.is_equal)
-    tt(ap("ST"), ap("OH"), c2("LQ", 0, 192), OP.mult)
-    scan(ap("PS"), r01, ap("ST"), 0.0, OP.mult, OP.add)
-    gat("V", wf("LB", 0, 16), ap("PS"), wu("IE16", 0, 1))
-    cp(wu("LBU", 0, 16), wf("LB", 0, 16))
-    cp(c2("TT", 0, A_), ap("SBI"))
+    mm(c2("PB", 0, 192), [(ap("E8", S[0:8, :]), ap("BI", S[0:8, :]))])
+    ts(ap("MB"), c2("PB", 0, 192), PM, OP.is_equal)
+    tt(ap("LJM"), ap("MB"), ap("L1"), OP.mult)
+    mm(lp, [(ap("ID"), ap("L1")), (ap("NID"), ap("LJM"))])
+    cp(ap("LK"), lp)
+    pick(small, "LJM")
+    cp(wu("LBU"), small)
+    cp(wf("LB"), small)
+    act(ap("L1"), lp, AF.Copy)
+    ts(ap("MJ"), ap("MB"), PM, OP.mult)
+    pick(small2, "MJ")
+    act(wf("BB"), small2, AF.Copy)
+    ts(ap("WK"), ap("LWI"), float(X0), OP.add)
+    ts(ap("W"), ap("LWI"), float(X0), OP.add)
+    ts(c2("TT", X0, R0), c2("SBI", X0, R0), -float(V_), OP.add)
 
-    def bound():
-        gat("S", ap("Y"), xw, wu("LBU"))
-        mm(c2("YP", 0, 192), [(ap("ID"), ap("Y"))])
-        ts(ap("Q4"), ap("Y"), 0.25, OP.mult, -0.375, OP.add)
+    bank = [0]
 
-    def dist(raw, m, sub, pairs=8):
-        for j in range(pairs):
-            d = "D%d" % (j % 2)
-            for h in range(2):
-                k = 2 * j + h
-                mm(c2(d, h, 384, 2), [(ap("ID"), c2(raw, 192 * k, 192 * k + 192)), (ap("NID"), sub)])
-            act(ap(m, S[:, :, 2 * j:2 * j + 2]), c2(d, 0, 384), AF.Abs)
+    def pair(step):
+        bank[0] += 1
+        return "D" + P["DB"][step][bank[0] % len(P["DB"][step])]
 
-    def steps(bank, src):
-        mm(c2(bank, 256, 447), [(ap("IDF"), c2(src, 0, 191)), (ap("NIDF"), c2(src, 1, 192))])
-        mm(c2(bank, 271, 448, 16), [(ap("IDF"), ends(src))])
+    def bound(n):
+        gat("S", ap("Y"), c2("XR%d" % n, FA, FA + R0), wu("LBU"))
+        act(ap("Q"), ap("Y"), AF.Identity, scale=0.25, bias=191.625)
+        if P["A4"] < 16:
+            act(c2("D4", P["A4"], 3072, 16), ap("Y"), AF.Copy)
+        pick(small, "Y", "SEL")
+        act(wf("SY"), small, AF.Copy)
+        act(ap("THR"), ind(wf("SY", 0, 16), wu("IQ")), AF.Identity, scale=-1.0, bias=c2("TH", 4 * n, 4 * n + 1))
+        act(wh("LBH"), wf("LB"), AF.Copy)
 
-    def lowest(pv, a, du, off):
-        tt(ap("EX"), ind(wf(pv, 0, 16), wu("IR")), ap("MRV"), OP.mult)
-        tt(wf(a), wf(du), wf(pv), OP.subtract)
-        act(wf(a), wf(a), AF.Relu)
-        mm(c2("B0", 0, 192), [(ap("BLKH"), ap("EX"))])
-        if P["PS1"]:
-            mm(c2("B1", 0, 192), [(ap("BLKH"), ap("EX"))])
-        for q in range(11, -1, -1):
-            n = 16 * (q + 1)
-            o = c2("NE", SEG[q], SEG[q + 1])
-            if q >= 12 - P["PS1"]:
-                act(o, c2("B1", 192 - n, 192), AF.Abs, bias=wf(pv, q, q + 1), scale=-1.0)
+    def dist(raw, m, sub, off, u):
+        j, h = u // 2, u % 2
+        d = pair(m[1])
+        mms([(c2(d, k, 512, 8), [(ap("ID"), c2(raw, 1024 * j + 8 * h + k, 1024 * j + 1024, 16)), (ap("NID"), sub(64 * j, 64 * j + 64))]) for k in range(8)])
+        act(ap(m, S[:, 64 * j:64 * j + 64, 8 * h:8 * h + 8]), ap(d), AF.Abs, bias=off)
+
+    def keys(at, m, j):
+        mm(c2("KB", at + 64 * j, at + 64 * j + 64), [(ap("ID"), c2("RI", 0, 64))] + [(sel(r), ap(m, S[:, 64 * j + r:64 * j + 64:16, :])) for r in range(16)])
+
+    def lowest(a, base, du, off, onS):
+        tt(ap("EXP"), ind(wf(a, 0, 16), wu("IRV")), ap("MRV"), OP.mult)
+        tt(wf("AM"), wf(a), wf(base), OP.subtract)
+        mm(c2("PA", 256, 448), [(ap("BLK"), ap("EXP"))])
+        if onS:
+            mm(c2("D2", 256, 448), [(ap("BLK"), ap("EXP"))])
+        for q in sorted(range(12), key=lambda q: -(q % MB_)):
+            lo, o = 256 + 16 * (11 - q), c2("NE", SEG[q], SEG[q + 1])
+            if q in onS:
+                act(o, c2("D2", lo, lo + SEG[q + 1] - SEG[q]), AF.Abs, bias=wf(a, q, q + 1), scale=-1.0)
             else:
-                ts(o, c2("B0", 192 - n, 192), wf(pv, q, q + 1), OP.not_equal)
+                ts(o, c2("PA", lo, lo + SEG[q + 1] - SEG[q]), wf(a, q, q + 1), OP.not_equal)
         scan(ap("FL"), ap("NE"), ap("MM"), 1.0, OP.min, OP.max)
-        tt(wf("E1", 0, 16), ind(ap("FL"), wu("IEND", 0, 1)), wf(a, 0, 16), OP.mult)
-        tt(wf("E2"), wf(du), wf("E1"), OP.subtract)
+        tt(wf("E1", 0, 16), ind(ap("FL"), wu("IEND", 0, 1)), wf("AM", 0, 16), OP.mult)
+        tt(wf("E2"), wf("E1"), wf(du), OP.add)
         cp(off, wf("E2"))
 
-    bound()
-    ka, kb, kc = ap("KA", S[:, 0:12, :]), ap("KB", S[:, 0:12, :]), c2("KC", 0, 192)
-    side = c2("YP", 256, 448)
+    def parts():
+        return [(q, q + MB_) for q in range(12 - MB_, -1, -MB_)]
+
+    def step1(n):
+        sec[0] = "b"
+        for u in range(6):
+            if u % 2 == 0:
+                for x in (u, u + 1):
+                    gat("V" if x in P["G1V"][n] else "S", c2("RAW1", 512 * x, 512 * x + 512), c2("XR%d" % n, FA, FA + R0), c2("LK", 32 * x, 32 * x + 32))
+            dist("RAW1", "M1", lambda a, b: c2("Z" if n else "Z0", a, b), 1024.0 if n else 0.0, u)
+            if u % 2:
+                keys(0, "M1", u // 2)
+
+    bound(0)
+    step1(0)
+    ka = ap("KA", S[:, 0:12, :])
     for n in range(RO):
         sec[0] = "a"
-        R = "R%d" % n
-        rw = c2(R, 0, V_)
+        R, XN = "XR%d" % n, "XR%d" % (n + 1)
+        rw, both = c2(R, 0, V_), c2(R, 0, FA + R0)
+        dma("Y", c2(XN, OWN, OWN + V_), c2(R, OWN, OWN + V_), 4000)
         last = n == RO - 1
         thc = c2("TH", 4 * n, 4 * n + 1)
-        gat("V", ap("S208"), c2("TT", 0, A_), wu("LBU", 0, 13))
-        turn("S208", "TR")
-        gat("V", ap("SKQ"), ap("TR"), wu("IKQ"))
+        zs, zoff = ("Z0", 0.0) if n == 0 else ("Z", 1024.0)
+        gg = c2("GG", 16, 208)
+        if n == 0:
+            ts(gg, ind(ap("SBI"), wu("LBU")), -float(V_), OP.add)
+        else:
+            gat("V", gg, c2("TT", 0, R0), wu("LBU"))
+        tr(c2("TR", 0, 192), gg)
+        tr(c2("TR", 192, 416), ap("GG"))
+        ts(ap("SKQ"), ind(ap("TR"), wu("IKQ")), float(V_), OP.add)
         gat("S", ap("SQK"), ap("TR"), wu("IQK"))
-        steps("YP", "SQK")
-        first = []
+        mms([(c2("PA", 0, 191), [(ap("ID"), c2("SQK", 0, 191)), (ap("NID"), c2("SQK", 1, 192))]), (c2("PA", 15, 192, 16), [(ap("ID"), ends("SQK"))])])
         S2 = P["S2"][n]
         for k in range(S2):
-            first.append(gat("S", ap("M5", S[:, :, k]), rw, c2("SKQ", 12 * k, 12 * k + 12)))
-            mm(c2("D%d" % (k // 2 % 2), k % 2, 384, 2), [(ap("ID"), ap("M5", S[:, :, k])), (ap("NID"), ap("Y"))])
+            gat("S", ap("M5", S[:, :, k]), rw, c2("SKQ", 12 * k, 12 * k + 12))
             if k % 2:
-                act(ap("M2", S[:, :, k - 1:k + 1]), c2("D%d" % (k // 2 % 2), 0, 384), AF.Relu)
+                d = pair("2")
+                mms([(c2(d, h, 384, 2), [(ap("ID"), ap("M5", S[:, :, k - 1 + h])), (ap("NID"), ap("Y"))]) for h in range(2)])
+                act(ap("M2", S[:, :, k - 1:k + 1]), c2(d, 0, 384), AF.Relu)
         for k in range(S2, 16):
-            first.append(tt(ap("M2", S[:, :, k]), ind(rw, c2("SKQ", 12 * k, 12 * k + 12)), ap("Y"), OP.min))
-        for o in first:
-            for h in (range(XH) if n == 0 else [XH + n - 1]):
-                ops[o]["ext"].append("r%d" % h)
-                ops[o]["after"].append(arrive[h])
-        if S2:
-            mm(ap("KA", S[:, 0:12, 0:S2]), [(ap("ID"), ap("KMX", S[:, :, 0:S2]))] + [(sel(r), ap("M5", S[:, r::16, 0:S2])) for r in range(16)]
-               + [(c2("NSEL", 15 - r, 143 - r), ap("M2", S[:, r::16, 0:S2])) for r in range(16)])
-        sums("KA", "M2", [(ap("ID"), "KMX")], [(S2, 12), (12, 16)])
-        cp(ap("SSL"), c2("S208", 0, 192))
+            tt(ap("M2", S[:, :, k]), ind(rw, c2("SKQ", 12 * k, 12 * k + 12)), ap("Y"), OP.min)
+        for (a, b) in P["C2"]:
+            if a >= S2 and b > a:
+                mm(ap("KA", S[:, 0:12, a:b]), [(ap("ID"), ap("KMX", S[:, :, a:b]))] + [(sel(r), ap("M2", S[:, r::16, a:b])) for r in range(16)])
+            elif b > a:
+                mm(ap("KA", S[:, 0:12, 0:S2]), [(ap("ID"), ap("KMX", S[:, :, 0:S2]))] + [(sel(r), ap("M5", S[:, r::16, 0:S2])) for r in range(16)]
+                   + [(sel(r, "NSEL"), ap("M2", S[:, r::16, 0:S2])) for r in range(16)])
         sec[0] = "b"
-        for j in range(8):
-            gat("V" if (n == 0 and j % 2) else "S", c2("YW", 384 * j, 384 * j + 384), xw, c2("LK", 24 * j, 24 * j + 24))
-        dist("YW", "M1", ap("Z"))
+        scan(ap("KI"), ap("RBIG"), c2("KB", 0, 192), 0.0, OP.add, OP.min)
+        if n:
+            tt(wn("J0"), ends("KI"), small2, OP.min)
+        ts(wn("JI"), wn("J0") if n else ends("KI"), 15, OP.bitwise_and)
+        cp(wh("JB"), wn("JI"))
+        tt(wf("DB"), wn("JI"), wf("BB"), OP.subtract)
         if not last:
-            steps("KC", "LQ")
-        mm(kc, [(ap("ID"), ap("RI")), (ap("IBG"), ap("OH"))] + [(sel(r), ap("M1", S[:, r::16, :])) for r in range(16)])
-        scan(ap("KI"), ap("RBIG"), kc, 0.0, OP.add, OP.min)
-        ts(wn("JI"), ends("KI"), 15, OP.bitwise_and)
-        tt(wf("DB", 0, 16), wn("JI", 0, 16), wf("BB", 0, 16), OP.subtract)
-        ts(wf("JA", 0, 16), wn("JI", 0, 16), 192.0, OP.mult, -3072.0, OP.add)
+            act(wb("BH"), wf("BB"), AF.Copy)
+        spread("PB", wh("JB", 0, 28), False)
+        more(c2("PB", 256, 448), ap("NID"), ap("W"))
+        ts(ap("MJ"), c2("PB", 0, 192), PM, OP.is_equal)
+        tt(ap("LJM"), ap("MJ"), lp, OP.mult)
+        pick(small, "LJM")
+        act(wf("LJ"), small, AF.Copy)
+        tt(wf("DL"), wf("LJ"), wf("LB"), OP.subtract)
         if not last:
-            tt(ap("OHJ"), ap("KI"), kc, OP.not_equal)
-            scan(ap("LJ"), ap("OHJ"), c2("KC", 256, 448), 0.0, OP.mult, OP.add)
-            gat("S", wf("LT", 0, 16), ap("LJ"), wu("IE16", 0, 1))
-            cp(wu("LJU"), ends("LJ"))
-            tt(wf("DL", 0, 16), wf("LT", 0, 16), wf("LB", 0, 16), OP.subtract)
-            act(wf("LT4"), wf("LT"), AF.Identity, bias=4096.0)
-            gat("S", ap("TOLD"), c2("TT", 0, A_), wu("LJU"))
-            mm(c2("KC", 256, 448), [(ap("IDF"), c2("S208", 0, 192)), (ap("NIDF"), ap("TOLD"))])
-        act(wf("DS", 0, 48), wf("DL", 0, 48), AF.Identity, scale=1.0 / 4096)
-        act(wf("SL", 0, 16), wf("CC", 0, 16), AF.Copy)
-        if P["AS"]:
-            gat("S", ap("AW"), wf("LB", 0, 16), wu("IQ"))
-        else:
-            tt(ap("AW"), ind(wf("LB", 0, 16), wu("IQ")), c2("WQ", 0, 192), OP.subtract)
+            cp(wu("LJU"), wf("LJ"))
+            gat("S", ap("TOLD"), c2("TT", 0, R0), wu("LJU"))
         sec[0] = "c"
-        cp(ap("ST"), ka)
-        scan(ap("KS"), r01, ap("ST"), 0.0, OP.mult, OP.max)
+        if P["SCAN3"]:
+            scan(ap("KS"), r01, ka, 0.0, OP.mult, OP.max)
+        else:
+            cp(ap("ST"), ka)
+            scan(ap("KS"), r01, ap("ST"), 0.0, OP.mult, OP.max)
         tt(ap("NOH"), ap("KS"), ka, OP.not_equal)
-        o = ts(ap("BI"), ka, thc, OP.is_ge)
-        if n == 0:
-            ops[o]["ext"].append("th")
-            ops[o]["after"].append(tho)
-        scan(ap("PS"), ap("NOH"), side, 0.0, OP.mult, OP.add)
-        scan(ap("CN"), r01, ap("BI"), 0.0, OP.mult, OP.add)
-        ts(wf("NOC"), ends("CN"), NEED, OP.is_lt, 4096.0, OP.mult)
-        tt(wf("PV"), ends("PS"), wf("NOC"), OP.add)
-        cp(wu("PLU"), ends("PS"))
-        nv, no = ap("NV%d" % n), wu("NO%d" % n)
-        tt(ap("XS"), ind(rw, wu("PLU")), ap("Q4"), OP.subtract)
-        act(nv, ap("XS"), AF.Relu)
-        s1 = send([(nv, ap("OV%d" % n), HOPS[n], "eo%d" % n)], "loc", 2500)
-        lowest("PV", "A", "DU1", no)
-        cp(ind(ap(R), no), nv)
-        s2 = send([(no, wu("OO%d" % n), HOPS[n], "eo%d" % n)], "loc", 2500)
-        sec[0] = "d"
-        for j in range(4):
-            gat("V" if j < P["G4V"][n] else "S", c2("RAW4", 768 * j, 768 * j + 768), rw, c2("SSL", 48 * j, 48 * j + 48))
-        for j in range(4):
-            scan(c2("FS", 768 * j, 768 * j + 768), ap("R01"), c2("RAW4", 768 * j, 768 * j + 768), 0.0, OP.mult, OP.max)
-        cp(ind(ap("X"), wu("OO%d" % n)), ap("OV%d" % n), ext=["eo%d" % n], after=[s1, s2])
-        if last:
-            dma("Y", ap("yx"), xw, 4000)
-        else:
-            arrive[XH + n] = send([(xw, c2("R%d" % (n + 1), 0, V_), -HOPS[n + 1], "r%d" % (XH + n))], "l%d" % (XH + n), 8000)
-        for k in range(16):
-            tt(ap("M2", S[:, :, k]), c2("RAW4", k, 3072, 16), c2("YP", 0, 192), OP.min)
-        sums("KA", "M2", [], P["KC4"])
-        gat("S", c2("YW", 3072, 3264), rw, wu("PLU"))
         ts(ap("BI"), ka, thc, OP.is_ge)
+        scan(ap("PS"), ap("NOH"), c2("PA", 0, 192), 0.0, OP.mult, OP.add)
         scan(ap("CN"), r01, ap("BI"), 0.0, OP.mult, OP.add)
-        ts(wf("O4"), ends("CN"), NEED, OP.is_lt, 4096.0, OP.mult)
-        tt(wf("O4"), wf("O4"), wf("NOC"), OP.max)
+        ts(wf("OCC"), ends("CN"), PAR, OP.subtract, 3.0, OP.is_ge)
+        tt(wf("A"), ends("PS"), wf("OCC"), OP.mult)
+        ts(wu("PLU"), ends("PS"), float(V_), OP.add)
+        tt(ap("XS"), ind(rw, wu("PLU")), ap("Q"), OP.subtract)
+        nv, ov = "NV%d" % n, "OV%d" % n
+        ts(ap(nv), ap("XS"), 192.0, OP.add, 0.0, OP.max)
+        send([(ap(nv), ap(ov), HOPS[n], "x%d" % n)], 2500)
+        lowest("A", "J", "DU1", c2("NO", 16 * n, 16 * n + 12), P["NS1"])
+        send([(c2("NO", 16 * n, 16 * n + 12), c2("OO", 16 * n, 16 * n + 12), HOPS[n], "x%d" % n)], 2500)
+        for (a, b) in parts():
+            cp(ind(c2(R, 0, FA), c2("NO", 16 * n + a, 16 * n + b)), c2(nv, 16 * a, 16 * b))
+        if not last:
+            send([(rw, c2(XN, 0, V_), HOPS[n] - HOPS[n + 1], "r%d" % (n + 2))], 8000)
+        sec[0] = "d"
+        for (a, b) in parts():
+            cp(ind(c2(XN, OWN, OWN + FA), c2("OO", 16 * n + a, 16 * n + b)), c2(ov, 16 * a, 16 * b))
+        if last:
+            dma("Y", ap("yx"), c2(XN, OWN, OWN + V_), 4000)
+        sec[0] = "c"
+        ts(wf("PL"), ends("PS"), float(V_ - FA), OP.add)
+        tt(wf("DP"), wf("LJ"), wf("PL"), OP.subtract)
+        if not last:
+            mm(c2("PA", 0, 192), [(ap("IDF"), gg), (ap("NIDF"), ap("TOLD"))])
+        sec[0] = "d"
+        a4 = P["A4"]
+        for k in range(a4):
+            tt(c2("A4", k, 3072, 16), ind(rw, c2("SKQ", 12 * k, 12 * k + 12)), ap("Y"), OP.subtract)
+        for k in range(a4, 16):
+            gat("S", c2("A4", k, 3072, 16), rw, c2("SKQ", 12 * k, 12 * k + 12))
+        for j in range(3):
+            scan(c2("FS", 1024 * j, 1024 * j + 1024), c2("D4", 1024 * j, 1024 * j + 1024), c2("A4", 1024 * j, 1024 * j + 1024), 0.0, OP.add, OP.max)
+        for k in range(a4):
+            if k < P["M0S"]:
+                act(ap("M2", S[:, :, k]), c2("A4", k, 3072, 16), AF.Relu, scale=-1.0)
+            else:
+                ts(ap("M2", S[:, :, k]), c2("A4", k, 3072, 16), -1.0, OP.mult, 0.0, OP.max)
+        for k in range(a4, 16, 2):
+            d = pair("4")
+            mms([(c2(d, h, 384, 2), [(ap("ID"), ap("Y")), (ap("NID"), c2("A4", k + h, 3072, 16))]) for h in range(2)])
+            act(ap("M2", S[:, :, k:k + 2]), c2(d, 0, 384), AF.Relu)
+        for (a, b) in (((0, a4), (a4, 16)) if P["O4"] else ((a4, 16), (0, a4))):
+            mm(ap("KA", S[:, 0:12, a:b]), [(sel(r, "NSEL"), ap("M2", S[:, r::16, a:b])) for r in range(16)])
+        tt(ap("BI"), ka, ap("THR"), OP.is_ge)
+        scan(ap("CN"), r01, ap("BI"), 0.0, OP.mult, OP.add)
+        ts(wf("C4"), ends("CN"), PAR, OP.subtract, 3.0, OP.is_lt)
+        tt(wb("EX"), wf("C4"), wf("OCC"), OP.is_ge)
         sec[0] = "e"
-        f, ns = c2("FS", 15, 3072, 16), 8 - P["G5V"][n]
-        for j in range(ns):
-            gat("S", c2("RAW5", 384 * j, 384 * j + 384), xw, c2("WK", 24 * j, 24 * j + 24))
-        dist("RAW5", "M5", f, ns)
-        for j in range(ns, 8):
-            for h in range(2):
-                tt(c2("RAW5", 384 * j + h, 384 * j + 384, 2), ind(xw, c2("WK", 24 * j + 12 * h, 24 * j + 12 * h + 12)), f, OP.subtract)
-            act(ap("M5", S[:, :, 2 * j:2 * j + 2]), c2("RAW5", 384 * j, 384 * j + 384), AF.Abs)
+        for u in range(6):
+            if u % 2 == 0:
+                for x in (u, u + 1):
+                    gat("V" if x in P["G5V"][n] else "S", c2("RAW5", 512 * x, 512 * x + 512), c2(XN, FA, FA + R0), c2("WK", 32 * x, 32 * x + 32))
+            dist("RAW5", "M5", lambda a, b: c2("FS", 16 * a + 15, 16 * b, 16), 0.0, u)
+            if u % 2:
+                keys(256, "M5", u // 2)
+        act(wf("E16"), wb("EX"), AF.Identity, scale=16.0, **({} if last else {"accum_out": wf("C", 8, 9)}))
+        exw = ind(wb("EX", 0, 16), wu("IR", 0, 2))
+        xp = c2("PB", 0, 192)
         if not last:
-            tt(wf("PV2"), wf("LT4"), wf("O4"), OP.subtract)
-            lowest("PV2", "A2", "DU2", wu("O2"))
-        tt(wf("T1", 0, 48), ind(wf("O4", 0, 16), wu("IR3", 0, 3)), wf("DS", 0, 48), OP.mult)
-        tt(wf("LB", 0, 48), wf("LB", 0, 48), wf("T1", 0, 48), OP.add)
-        cp(wu("LBU", 0, 48), wf("LB", 0, 48))
-        if not last:
-            bound()
-            act(wf("E3"), wf("O4"), AF.Identity, scale=1.0 / 4096, accum_out=wf("C", 4, 5))
-            mm(c2("B1", 448, 449), [(ap("BLKF"), wf("C", 4, 5))])
-            act(wf("C", 5, 6), c2("B1", 448, 449), AF.Identity, bias=3.0)
-            act(wf("C", 6, 7), c2("B1", 448, 449), AF.Identity, bias=MAGIC, scale=HALF)
-            act(wf("C", 7, 8), wf("C", 6, 7), AF.Identity, bias=-MAGIC)
-            act(NEED, wf("C", 7, 8), AF.Identity, bias=wf("C", 5, 6), scale=-2.0)
-        if P["ZS"]:
-            gat("S", ap("XS"), ap("YW"), wu("SELU"))
-            mm(c2("B0", 256, 448), [(ap("ID"), ap("XS")), (ap("ID"), ap("Z"))])
-            act(ap("ZT"), c2("B0", 256, 448), AF.Identity, bias=MAGIC, scale=HALF)
+            tt(wf("A2"), wb("EX"), wf("LJ"), OP.mult)
+            tt(wh("XL"), wb("EX"), wf("LB"), OP.mult)
+            spread("KA", wh("XL"), False)
+            lowest("A2", "DU2", "DU2", wu("O2"), P["NS2"])
+            spread("PB", wb("EX"))
+            tt(ap("LJX"), ap("LJM"), xp, OP.mult)
+            mm(xp, [(ap("ID"), ap("L1")), (ap("NID"), ap("LJX"))])
+            cp(ap("LK"), xp)
         else:
-            tt(ap("ZT"), ind(ap("YW"), wu("SELU")), ap("Z"), OP.add)
-            act(ap("ZT"), ap("ZT"), AF.Identity, bias=MAGIC, scale=HALF)
-        act(ap("Z"), ap("ZT"), AF.Identity, bias=-MAGIC)
-        sums("KB", "M5", [(ap("ID"), "KMN")])
-        if P["AS"]:
-            mm(c2("B1", 256, 448), [(ap("IDF"), ap("AW")), (ap("NIDF"), c2("WQ", 0, 192))])
+            spread("KA", wh("LBH"), False)
+        tt(wf("T1", 0, 48), ind(wb("EX", 0, 16), wu("IR", 0, 3)), wf("DL", 0, 48), OP.mult)
+        tt(wf("LB", 0, 48), wf("LB", 0, 48), wf("T1", 0, 48), OP.add)
+        if last:
+            act(wb("BH"), wf("BB"), AF.Copy)
+            mms([(ap("PA", S[0:8, b:192:16]), [(c2("EB", 128 * b, 128 * b + 128, 16), wb("BH"))]) for b in range(16)])
+            act(ap("OB", S[0:8, :]), ap("PA", S[0:8, 0:192]), AF.Copy)
+            dma("Y", ap("yb"), ap("OB", S[0:8, :]), 2200)
+        cp(wu("LBU"), wf("LB"))
+        ts(wu("SELU"), wf("PL"), float(FA), OP.add)
+        if P["ZS"]:
+            gat("S", ap("XS"), both, wu("SELU"))
+            mm(c2("PB", 0, 192), [(ap("ID"), ap("XS")), (ap("ID"), ap(zs))])
+            act(ap("Z"), c2("PB", 0, 192), AF.Identity, scale=0.5, bias=1023.75 - zoff / 2)
+        else:
+            tt(ap("ZT"), ind(both, wu("SELU")), ap(zs), OP.add)
+            ts(ap("Z"), ap("ZT"), 0.5, OP.mult, 1023.75 - zoff / 2, OP.add)
+        if last:
+            act(ap("ZO"), ap("Z"), AF.Identity, bias=-1024.0)
+            dma("Y", ap("yz"), ap("ZO"), 2200)
+        else:
+            cnt = c2("PA", 448, 449)
+            mm(cnt, [(ap("BLKF"), wf("C", 8, 9))])
+            ts(wn("N1", 0, 1), cnt, 0.5, OP.mult, -0.25, OP.add)
+            ts(PAR, wn("N1", 0, 1), -2.0, OP.mult, cnt, OP.add)
         sec[0] = "g" if last else "f"
-        act(ap("ST"), kb, AF.Copy)
-        scan(ap("KI"), ap("RBIG"), ap("ST"), 0.0, OP.add, OP.min)
+        scan(ap("KI"), ap("RBIG"), c2("KB", 256, 448), 0.0, OP.add, OP.min)
         ts(wn("WI"), ends("KI"), 15, OP.bitwise_and)
+        tt(wb("WB"), wn("WI"), wf("E16"), OP.add)
+        spread("KB", wb("WB"))
+        ts(ap("MW"), c2("KB", 0, 192), PM16, OP.is_equal)
         if not last:
-            tt(ap("EXW"), ind(wn("WI", 0, 16), wu("IQ")), ap("MR"), OP.mult)
-            mm(c2("B0", 0, 192), [(ap("BLKB"), ap("EXW"))])
-            ts(ap("MW"), c2("B0", 0, 192), PM, OP.is_equal)
-            tt(ap("MD"), ap("MW"), c2("KC", 256, 448), OP.mult)
-            tt(ind(ap("TT"), wu("O2")), ap("MD"), ap("TOLD"), OP.add)
-        tt(wf("WO"), wn("WI"), wf("O4"), OP.subtract)
-        tt(ap("OHW"), ind(wf("WO", 0, 16), wu("IQ")), ap("RIM"), OP.is_equal)
-        bw = c2("B1", 256, 448)
-        tt(bw, ap("OHW"), bw if P["AS"] else ap("AW"), OP.mult)
-        scan(ap("SW"), r01, bw, 0.0, OP.mult, OP.add)
-        tt(c2("WQ", 0, 192), c2("WQ", 0, 192), bw, OP.add)
-        tt(ap("CW"), ind(ap("SW"), wu("IE")), ap("OH"), OP.mult)
-        tt(c2("LQ", 0, 192), c2("LQ", 0, 192), ap("CW"), OP.subtract)
-        if not last:
-            gat("V", ap("LK"), c2("LQ", 0, 192), wu("PKQ"))
-            gat("V", ap("WK"), c2("WQ", 0, 192), wu("PKQ"))
-            tt(ap("OH"), ind(wf("BB", 0, 16), wu("IQ")), ap("RI"), OP.is_equal)
-    dma("Y", ap("yz"), ap("Z"), 2200)
-    tt(ap("EXW"), ind(wf("BB", 0, 16), wu("IQ")), ap("MR"), OP.mult)
-    mm(ap("B0", S[0:8, 0:192]), [(c2("BLKB", 0, 128, 16), ap("EXW"))])
-    act(ap("ZT", S[0:8, :]), ap("B0", S[0:8, 0:192]), AF.Copy)
-    dma("Y", ap("yb"), ap("ZT", S[0:8, :]), 2200)
-    for (src, t, o, y) in (("WQ", "TR2", "OW", "yw"), ("LQ", "TR", "OL", "yl")):
-        act(c2(src, 192, 208), c2(src, 0, 16), AF.Copy)
-        turn(src, t)
-        gat("S", ap(o), ap(t), wu("IQK"))
-        dma("Y", ap(y), ap(o), 2200)
+            tt(ap("MD"), ap("MW"), c2("PA", 0, 192), OP.mult)
+            for (a, b) in parts():
+                tt(ind(ap("TT"), wu("O2", a, b)), c2("MD", 16 * a, 16 * b), c2("TOLD", 16 * a, 16 * b), OP.add)
+        tt(ap("BW"), ap("MW"), c2("PB", 256, 448), OP.mult)
+        more(ap("KA", S[:, 16:28, :]), ap("NBLK"), ap("BW"))
+        tt(ap("MBR"), ap("MB"), ap("KA", S[:, 16:28, :]), OP.mult)
+        mm(lp, [(ap("ID"), ap("L1")), (ap("ID"), ap("MBR"))] + ([] if last else [(ap("NID"), ap("LJX"))]))
+        mm(wp, [(ap("ID"), ap("W")), (ap("ID"), ap("BW"))])
+        if last:
+            act(ap("OW"), wp, AF.Identity, bias=-float(X0))
+            dma("Y", ap("yw"), ap("OW"), 2200)
+            act(ap("OL"), lp, AF.Identity, bias=-float(X0))
+            dma("S", ap("yl"), ap("OL"), 2200)
+        else:
+            cp(ap("WK"), wp)
+            act(ap("MB"), lp, AF.Relu, scale=-1.0, bias=1.0)
+            act(ap("L1"), lp, AF.Copy)
+            act(ap("W"), wp, AF.Copy)
+            sec[0] = "e"
+            bound(n + 1)
+            step1(n + 1)
+            pick(small2, "BW", "NSE1", wh("XL"))
+            cp(wu("WWU"), small2)
+            gat("S", ap("VW"), c2(XN, FA, FA + R0), wu("WWU"))
+            mm(xp, [(ap("ID"), ap("VW")), (ap("NID"), ap("Z"))])
+            act(ap("VA"), xp, AF.Abs, bias=1024.0)
+            pick(small2, "VA", "SEL", wb("BH"))
     return ops
 
 
@@ -601,7 +681,7 @@ def place_all(ops, seq, lag, first):
     return st
 
 
-def refine(ops, start, rounds, judge=None):
+def refine(ops, start, rounds):
     n = len(ops)
     pred = links(ops)
     above, fwd = [], []
@@ -630,7 +710,7 @@ def refine(ops, start, rounds, judge=None):
         return sorted(range(n), key=lambda i: k[i])
 
     def worth(st):
-        return judge(st) if judge else max(st[i] + ops[i]["cost"] for i in range(n))
+        return max(st[i] + ops[i]["cost"] for i in range(n))
 
     best, bst = worth(start), list(start)
     tags = sorted(set(o["tag"] for o in ops if o["tag"][0] != "i"))
@@ -734,7 +814,7 @@ def rank_program(g, core, T, topo):
                                                      remote_sem=T.sem[sem], src=real(src), dst=real(dst)))
                     g.remote_dma_fused(trs, local_sem=T.sem[o["dma"][0]])
                 else:
-                    ins = meth[name](q[e])(*[real(a) for a in args], **{k: real(v) for k, v in kw.items()})
+                    ins = meth[name](q[e])(*[real(a) for a in args], **{k: real(v) for k, v in kw.items() if k != "acc"})
             if i in mark and o["calls"][0][0] != "send":
                 ins.then_inc(T.sem[mark[i][0]], o["dma"][1] if o["dma"] else 1)
         if e == "G":

@@ -12,14 +12,14 @@ MB_ = 6
 SEG = [(q // MB_) * 8 * MB_ * (MB_ + 1) + 8 * (q % MB_) * (q % MB_ + 1) for q in range(13)]
 NP = SEG[12]
 
-P = {"S2": [4, 4, 4, 4],
+P = {"S2": [6, 4, 4, 4],
      "A4": 8,
-     "G1V": [(0, 2, 4), (), (), ()],
-     "G5V": [(0, 2), (0, 2), (0, 2), (0, 2)],
+     "G1V": [(0, 2, 4), (0,), (0,), (0,)],
+     "G5V": [(0, 2), (0, 2), (0, 2), (0, 2, 4)],
      "DB": {"1": "01", "2": "2", "4": "012", "5": "012"},
-     "C2": [(4, 10), (0, 4), (10, 16)], "O4": 0, "ZS": 1, "M0S": 0, "SCAN3": 0, "WAW": 1, "EBV": 8, "NS1": (5, 11, 4, 10), "NS2": (),
-     "CY": 0.87, "PE": 0.46, "GA": 1.56, "SC": 3.8, "TT": 2.0, "FIX": 20.0, "SAME": 150.0, "OTHER": 200.0, "SLACK": 150.0, "NET": 1.1,
-     "SEED": 0, "ROUNDS": 4000, "HEAT": 800.0}
+     "K2": 1, "O4": 1, "ZS": 1, "M0S": 0, "SCAN3": 0, "WAW": 1, "EBV": 0, "VS": 1, "JT": 16, "BEFORE": [("bVLJM", 0, "dVA4", 3), ("cPPA", 9, "ePKB", 0)], "FIXROW": 0, "ROW": "aaaaaaaaxmmxfrmmfmmmmrfr", "POS": [6, 6, 6, 6], "D2": ["201", "2", "2", "2"], "XSS": 0, "R1": (), "MWH": 1, "STS": 0, "NS1": (6, 7, 8, 9, 10, 11, 5, 4), "NS2": (),
+     "CY": 0.96, "PE": 0.48, "GA": 1.56, "SC": 3.8, "TT": 2.0, "FIX": 20.0, "SAME": 150.0, "OTHER": 200.0, "SLACK": 150.0, "NET": 1.25,
+     "SEED": 4, "ROUNDS": 2500, "HEAT": 800.0, "HOT": 0.4, "AGAIN": {"SEED": 11, "ROUNDS": 4000, "HEAT": 250.0, "HOT": 0.5}, "POLISH": 2000, "COOL": 40.0, "MASS": 2.0, "WIDE": 300.0}
 
 SCRATCH = {}
 
@@ -39,18 +39,19 @@ _sb("LAI LWI KI B0I", [128, 192], I)
 _sb("GG", [128, 224], F)
 _sb("TR", [128, 416], F)
 _sb("KS ST PS TOLD MD THR OL OW OB", [128, 192], F)
-_sb("EXP Z ZT LJM LJX MBR BW SQK L1 W", [128, 192], H)
-_sb("Z0 Y RI RV RBIG R01 MRV BI CN NOH XS Q MW MJ MB ZO VW VA", [128, 192], B)
+_sb("EXP Z ZT LJM LJX MBR BW SQK L1 W GH TH2", [128, 192], H)
+_sb("YV", [128, 384], B)
+_sb("Z0 RI RV RBIG R01 MRV BI CN NOH XS Q MW MJ MB ZO VW CV OHJ RIM", [128, 192], B)
 _sb("SKQ LK WK", [128, 192], U)
 _sb("M1 M2 M5", [128, 192, 16], B)
 _sb("KMX", [128, 12, 16], B)
 _sb("A4 FS D4 RAW1 RAW5", [128, 3072], B)
 _sb("SEL NSEL SE1 NSE1", [128, 144], B)
 _sb("T143", [128, 144], F)
-_sb("IDF NIDF BLKF", [128, 128], F)
-_sb("BLK NBLK ID NID E8 IOB", [128, 128], B)
+_sb("BLKF", [128, 128], F)
+_sb("BLK NBLK ID NID IBG E8 IOB", [128, 128], B)
 _sb("EB", [128, 2048], B)
-_sb("WF", [128, 512], F)
+_sb("WF", [128, 544], F)
 _sb("WN", [128, 128], I)
 _sb("WU", [128, 256], U)
 _sb("WH", [128, 128], H)
@@ -61,13 +62,13 @@ SCRATCH["KA"] = ("psum", [128, 32, 16], F)
 for _n in "D0 D1 D2 KB PA PB PC".split():
     SCRATCH[_n] = ("psum", [128, 512], F)
 
-TABS = {"WF": "LJ LB PL BB DL DP DB T1 T1b T1c OCC C4 E16 E1 E2 SY A A2 AM J Q C DU1 DU2 HE T2 T3 THM".split(),
+TABS = {"WF": "LJ LB PL BB DL DP DB T1 T1b T1c OCC C4 E16 E1 E2 SY A0 A6 A2 AM AM0 AM6 JX E10 E16b J Q C DU1 DU2 T2 T3 THM".split(),
         "WN": "P JI WI N1 N2 KK J0".split(),
-        "WU": "LBU SELU PLU LJU IQ IQK IKQ IR WWU O2 IRV IEND".split(),
+        "WU": "LBU SELU PLU LJU IQ IQK IKQ IR WWU O2 IRV IEND IENH".split(),
         "WH": "XL JB LBH".split(),
         "WB": "EX WB BH".split()}
 
-SEMAPHORES = (["cV", "cS", "cP", "cG", "loc", "th"] + ["d%d" % i for i in range(20)] + ["r%d" % i for i in range(5)]
+SEMAPHORES = (["cV", "cS", "cP", "cG", "loc", "th"] + ["d%d" % i for i in range(24)] + ["r%d" % i for i in range(5)]
               + ["x%d" % i for i in range(4)])
 IOS = "xs sb la lw z0 b0 th yx yl yw yz yb".split()
 
@@ -118,6 +119,8 @@ def build():
             return
         psum = SCRATCH[a[1]][0] == "psum"
         m = bits(a)
+        if psum:
+            me["banks"].add(a[1])
         for (lm, sem, o) in lands.get(a[1], []):
             if lm & m and o not in me["after"]:
                 me["ext"].append(sem)
@@ -125,18 +128,19 @@ def build():
         for (o, om, ow) in acc.setdefault(a[1], []):
             if o == me["id"]:
                 continue
-            other = ops[o]["eng"] != me["eng"] or bool(ops[o]["dma"]) or bool(me["dma"])
             hit = (m & om) != 0
             if hit and ow and not write:
                 me["deps"][o] = True
-            elif (hit and (write or ow)) or (psum and ops[o]["eng"] != me["eng"]):
-                me["deps"][o] = me["deps"].get(o, False) or other or not ow or bool(P["WAW"])
+            elif hit and (write or ow):
+                me["deps"][o] = True
+            elif psum and ops[o]["eng"] != me["eng"]:
+                me["soft"].add(o)
             elif psum and me["eng"] == "P":
                 me["deps"].setdefault(o, False)
         acc[a[1]].append((me["id"], m, write))
 
     def add(eng, calls, cost, dma=None, busy=None):
-        me = {"id": len(ops), "eng": eng, "calls": calls, "cost": cost, "dma": dma, "deps": {}, "ext": [],
+        me = {"id": len(ops), "eng": eng, "calls": calls, "cost": cost, "dma": dma, "deps": {}, "ext": [], "soft": set(), "banks": set(),
               "busy": cost if busy is None else busy, "after": []}
         ops.append(me)
         a = calls[0][1][0]
@@ -212,6 +216,10 @@ def build():
         kw = {} if SCRATCH[out[1]][2] == I else {"allow_small_or_imprecise_dtypes": True}
         return add("G", [("iota", [out, pat, base, cm], kw)], 130 + 2 * len(cols(out)) * CY)
 
+    def gcp(out, a):
+        n = len(cols(out))
+        return add("G", [("affine_select", [out, a, [[0, n]], OP.is_equal, 0.0, 0, 0], {})], 170 + 2 * n * CY)
+
     nd = [0]
 
     def dma(eng, out, in_, cost):
@@ -238,8 +246,8 @@ def build():
         calls = [("matmul", [ap(bank, S[:, 16:28, b]) if bank == "KA" else c2(bank, b, 16 * n, 16), eb(b), src, b == 0, stop and b == 15], {}) for b in range(16)]
         return add("P", calls, 60 + 16 * 64 * P["PE"])
 
-    def more(out, l, r):
-        return add("P", [("matmul", [out, l, r, False, True], {"acc": out})], 60 + len(cols(r)) * P["PE"])
+    def more(out, l, r, stop=True):
+        return add("P", [("matmul", [out, l, r, False, stop], {"acc": out})], 60 + len(cols(r)) * P["PE"])
 
     def pick(out, src, t="SE1", plus=None):
         mm(out, ([(ap("ID"), plus)] if plus else []) + [(sel(r, t), c2(src, r, 192, 16)) for r in range(16)])
@@ -255,16 +263,16 @@ def build():
     dma("S", ap("Z0"), ap("z0"), 3000)
     dma("Y", c2("SBI", X0, R0), ap("sb"), 5000)
     dma("S", ap("LWI"), ap("lw"), 3000)
-    send([(c2("XR0", OWN, OWN + A_), c2("XR0", 0, A_), -HOPS[0], "r0")], 6000, busy=2500)
-    send([(c2("XR0", OWN + A_, OWN + V_), c2("XR0", A_, V_), -HOPS[0], "r1")], 6500)
+    s0 = send([(c2("XR0", OWN, OWN + A_), c2("XR0", 0, A_), -HOPS[0], "r0")], 6000, busy=2500)
+    ops[send([(c2("XR0", OWN + A_, OWN + V_), c2("XR0", A_, V_), -HOPS[0], "r1")], 5000)]["deps"][s0] = False
     iota(wn("P", 0, 1), [[0, 1]], 0, 1)
     iota(wf("Q", 0, 16), [[1, 16]], 0, 0)
     iota(ap("T143"), [[-1, 144]], 15, 1)
     iota(ap("IOB"), [[-16, 8], [0, 16]], 0, 1)
     iota(ap("E8", S[0:8, :]), [[-1, 8], [0, 16]], 0, 1)
     iota(ap("RI"), [[0, 12], [1, 16]], 0, 0)
-    for h in range(4):
-        iota(c2("D4", 768 * h, 768 * h + 768), [[0, 768]], 0, 0)
+    for q in range(12):
+        iota(c2("MM", SEG[q], SEG[q + 1]), [[-1, SEG[q + 1] - SEG[q]]], 15, 0)
     ts(wn("P", 1, 2), wn("P", 0, 1), 15, OP.bitwise_and)
     ts(wn("P", 2, 3), wn("P", 0, 1), 4, OP.arith_shift_right, 1, OP.bitwise_and)
     cp(wf("C", 0, 2), wn("P", 1, 3))
@@ -275,7 +283,7 @@ def build():
     ms(c2("TT", 0, X0), 0.0)
     ms(c2("SBI", 0, X0), 0)
     ms(ap("GG"), 0.0)
-    ms(wf("LJ", 0, 16 * 19), 0.0)
+    ms(wf("LJ", 0, 16 * 23), 0.0)
     ms(wb("EX", 0, 16), 0.0)
     cp(wh("JB", 0, 32), wf("PL", 0, 32))
     ts(ap("E8", S[0:8, :]), ap("E8", S[0:8, :]), 0.0, OP.is_equal)
@@ -284,28 +292,21 @@ def build():
     act(ap("NSEL"), ap("SE1"), AF.Identity, scale=-16.0)
     ts(ap("ID"), c2("T143", 15, 143), 0.0, OP.is_equal)
     act(ap("NID"), ap("ID"), AF.Identity, scale=-1.0)
-    act(ap("IDF"), ap("ID"), AF.Copy)
-    act(ap("NIDF"), ap("ID"), AF.Identity, scale=-1.0)
     ts(ap("BLK"), ap("IOB"), PM, OP.is_equal)
     act(ap("NBLK"), ap("BLK"), AF.Identity, scale=-1.0)
     act(ap("BLKF"), ap("BLK"), AF.Identity, scale=1.0 / 16)
     act(ap("RV"), ap("RI"), AF.Identity, scale=-1.0, bias=15.0)
     act(ap("KMX"), ap("RV"), AF.Copy)
+    act(ap("RIM"), ap("RI"), AF.Identity, bias=-16.0)
+    act(ap("IBG"), ap("ID"), AF.Identity, scale=131072.0)
     ts(ap("MRV"), ap("RV"), PM, OP.is_equal)
-    ms(ap("MM"), 0.0)
-    ts(c2("MM", 0, 16), c2("RV", 0, 16), PM, OP.is_ge)
-    for q in range(1, 12):
-        act(c2("MM", SEG[q], SEG[q] + 16), c2("MM", 0, 16), AF.Copy)
+    ts(ap("MM"), ap("MM"), PM, OP.is_ge)
     ts(ap("RBIG"), ap("RI"), 0.0, OP.is_equal, 1048576.0, OP.mult)
     ts(ap("R01"), ap("RI"), 0.0, OP.not_equal)
-    ms(c2("D4", 0, 3072, 16), -1024.0)
+    ts(c2("D4", 0, 192), ap("RI"), 0.0, OP.is_equal, -1024.0, OP.mult)
     act(ap("NSE1"), ap("SE1"), AF.Identity, scale=-1.0)
-    ts(wf("HE", 0, 16), wf("Q", 0, 16), PM, OP.is_equal)
     for b in range(16):
-        if b < P["EBV"]:
-            ts(eb(b), ap("BLK"), wf("HE", b, b + 1), OP.mult)
-        else:
-            act(eb(b), ap("BLK"), AF.Identity, scale=wf("HE", b, b + 1))
+        add("G", [("affine_select", [eb(b), ap("BLK"), [[-16, 8], [0, 16]], OP.is_equal, 0.0, -b, 1], {})], 170 + 256 * CY)
     cp(wu("IQ"), wf("Q"))
     ts(wu("IR", 0, 3), wf("Q", 0, 3), 0.0, OP.mult, PM, OP.add)
     ts(wu("IRV"), wf("Q"), -1.0, OP.mult, 11.0, OP.add)
@@ -319,6 +320,7 @@ def build():
     ts(t3[2], t3[1], 1.0, OP.add, t3[1], OP.mult)
     ts(t3[3], wn("N1", 12, 13), float(MB_ * (MB_ + 1)), OP.mult, t3[2], OP.add)
     ts(wu("IEND", 0, 1), t3[3], 8.0, OP.mult, -1.0, OP.add)
+    ts(wu("IENH", 0, 1), t3[2], 8.0, OP.mult, -1.0, OP.add)
 
     def turned(dst, qq, base):
         ts(wn("N1"), qq, WC, OP.add)
@@ -358,7 +360,9 @@ def build():
     act(wf("BB"), small2, AF.Copy)
     ts(ap("WK"), ap("LWI"), float(X0), OP.add)
     ts(ap("W"), ap("LWI"), float(X0), OP.add)
-    ts(c2("TT", X0, R0), c2("SBI", X0, R0), -float(V_), OP.add)
+    for a in range(X0, R0, 256):
+        gcp(c2("TT", a, a + 256), c2("SBI", a, a + 256))
+    ms(ap("CV"), float(V_))
 
     bank = [0]
 
@@ -366,15 +370,19 @@ def build():
         bank[0] += 1
         return "D" + P["DB"][step][bank[0] % len(P["DB"][step])]
 
+    yy, va = c2("YV", 0, 192), c2("YV", 192, 384)
+    sy, kw2, ww = c2("PB", 464, 476), c2("PB", 476, 488), c2("PB", 448, 460)
+
+    def limit(n):
+        calls = [("matmul", [c2("PB", 464, 488 if n else 476), sel(r), c2("YV", r, 384 if n else 192, 16), r == 0, r == 15 and not n], {}) for r in range(16)]
+        if n:
+            calls.append(("matmul", [kw2, ap("ID"), wb("BH"), False, True], {}))
+        add("P", calls, 60 + 64 * len(calls) * P["PE"])
+
     def bound(n):
-        gat("S", ap("Y"), c2("XR%d" % n, FA, FA + R0), wu("LBU"))
-        act(ap("Q"), ap("Y"), AF.Identity, scale=0.25, bias=191.625)
-        if P["A4"] < 16:
-            act(c2("D4", P["A4"], 3072, 16), ap("Y"), AF.Copy)
-        pick(small, "Y", "SEL")
-        act(wf("SY"), small, AF.Copy)
-        act(ap("THR"), ind(wf("SY", 0, 16), wu("IQ")), AF.Identity, scale=-1.0, bias=c2("TH", 4 * n, 4 * n + 1))
-        act(wh("LBH"), wf("LB"), AF.Copy)
+        gat("S", yy, c2("XR%d" % n, FA, FA + R0), wu("LBU"))
+        act(ap("Q"), yy, AF.Identity, scale=0.25, bias=191.625)
+        gcp(wh("LBH"), wf("LB"))
 
     def dist(raw, m, sub, off, u):
         j, h = u // 2, u % 2
@@ -382,8 +390,8 @@ def build():
         mms([(c2(d, k, 512, 8), [(ap("ID"), c2(raw, 1024 * j + 8 * h + k, 1024 * j + 1024, 16)), (ap("NID"), sub(64 * j, 64 * j + 64))]) for k in range(8)])
         act(ap(m, S[:, 64 * j:64 * j + 64, 8 * h:8 * h + 8]), ap(d), AF.Abs, bias=off)
 
-    def keys(at, m, j):
-        mm(c2("KB", at + 64 * j, at + 64 * j + 64), [(ap("ID"), c2("RI", 0, 64))] + [(sel(r), ap(m, S[:, 64 * j + r:64 * j + 64:16, :])) for r in range(16)])
+    def keys(at, m, j, shut=False):
+        mm(c2("KB", at + 64 * j, at + 64 * j + 64), [(ap("ID"), c2("RI", 0, 64))] + [(ap("IBG"), c2("OHJ", 64 * j, 64 * j + 64))] * shut + [(sel(r), ap(m, S[:, 64 * j + r:64 * j + 64:16, :])) for r in range(16)])
 
     def lowest(a, base, du, off, onS):
         tt(ap("EXP"), ind(wf(a, 0, 16), wu("IRV")), ap("MRV"), OP.mult)
@@ -402,35 +410,57 @@ def build():
         tt(wf("E2"), wf("E1"), wf(du), OP.add)
         cp(off, wf("E2"))
 
+    def lowest_half(a, b, off, onS):
+        t, x0, sb = "A%d" % a, 16 * (12 - b), "D2" if a else "D1"
+        tt(c2("EXP", x0, x0 + 16 * MB_), ind(wf(t, 0, 16), wu("IRV", 12 - MB_, 12)), c2("MRV", 0, 16 * MB_), OP.mult)
+        tt(wf("AM%d" % a, 0, MB_), wf(t, 0, MB_), wf("J", a, b), OP.subtract)
+        if any(q not in onS for q in range(a, b)):
+            mm(c2("PA", 256 + x0, 256 + x0 + 16 * MB_), [(ap("BLK"), c2("EXP", x0, x0 + 16 * MB_))])
+        if any(q in onS for q in range(a, b)):
+            mm(c2(sb, x0, x0 + 16 * MB_), [(ap("BLK"), c2("EXP", x0, x0 + 16 * MB_))])
+        for q in range(b - 1, a - 1, -1):
+            lo, o = 16 * (11 - q), c2("NE", SEG[q], SEG[q + 1])
+            if q in onS:
+                act(o, c2(sb, lo, lo + SEG[q + 1] - SEG[q]), AF.Abs, bias=wf(t, q - a, q - a + 1), scale=-1.0)
+            else:
+                ts(o, c2("PA", 256 + lo, 256 + lo + SEG[q + 1] - SEG[q]), wf(t, q - a, q - a + 1), OP.not_equal)
+        fl = c2("FL", SEG[a], SEG[b])
+        scan(fl, c2("NE", SEG[a], SEG[b]), c2("MM", SEG[a], SEG[b]), 1.0, OP.min, OP.max)
+        e1 = "E16b" if a else "E10"
+        tt(wf(e1, 0, 16), ind(fl, wu("IENH", 0, 1)), wf("AM%d" % a, 0, 16), OP.mult)
+        tt(wf("E2", a, b), wf(e1, 0, MB_), wf("DU1", a, b), OP.add)
+        cp(off, wf("E2", a, b))
+
     def parts():
         return [(q, q + MB_) for q in range(12 - MB_, -1, -MB_)]
 
-    def step1(n):
+    def step1(n, lo, hi):
         sec[0] = "b"
-        for u in range(6):
-            if u % 2 == 0:
+        for u in range(lo, hi):
+            if u % 2 == 0 and n and u // 2 in P["R1"]:
+                gat("S", c2("RAW1", 512 * u, 512 * u + 1024), c2("XR%d" % n, FA, FA + R0), c2("LK", 32 * u, 32 * u + 64))
+            elif u % 2 == 0:
                 for x in (u, u + 1):
-                    gat("V" if x in P["G1V"][n] else "S", c2("RAW1", 512 * x, 512 * x + 512), c2("XR%d" % n, FA, FA + R0), c2("LK", 32 * x, 32 * x + 32))
+                    w = 32 // P["VS"] if n and x in P["G1V"][n] else 32
+                    for a in range(32 * x, 32 * x + 32, w):
+                        gat("V" if x in P["G1V"][n] else "S", c2("RAW1", 16 * a, 16 * (a + w)), c2("XR%d" % n, FA, FA + R0), c2("LK", a, a + w))
             dist("RAW1", "M1", lambda a, b: c2("Z" if n else "Z0", a, b), 1024.0 if n else 0.0, u)
             if u % 2:
-                keys(0, "M1", u // 2)
+                keys(0, "M1", u // 2, n > 0)
 
     bound(0)
-    step1(0)
+    limit(0)
+    step1(0, 0, P["POS"][0])
     ka = ap("KA", S[:, 0:12, :])
     for n in range(RO):
         sec[0] = "a"
         R, XN = "XR%d" % n, "XR%d" % (n + 1)
         rw, both = c2(R, 0, V_), c2(R, 0, FA + R0)
-        dma("Y", c2(XN, OWN, OWN + V_), c2(R, OWN, OWN + V_), 4000)
         last = n == RO - 1
         thc = c2("TH", 4 * n, 4 * n + 1)
         zs, zoff = ("Z0", 0.0) if n == 0 else ("Z", 1024.0)
         gg = c2("GG", 16, 208)
-        if n == 0:
-            ts(gg, ind(ap("SBI"), wu("LBU")), -float(V_), OP.add)
-        else:
-            gat("V", gg, c2("TT", 0, R0), wu("LBU"))
+        ts(gg, ind(c2("TT", 0, R0) if n else ap("SBI"), wu("LBU")), -float(V_), OP.add)
         tr(c2("TR", 0, 192), gg)
         tr(c2("TR", 192, 416), ap("GG"))
         ts(ap("SKQ"), ind(ap("TR"), wu("IKQ")), float(V_), OP.add)
@@ -440,97 +470,123 @@ def build():
         for k in range(S2):
             gat("S", ap("M5", S[:, :, k]), rw, c2("SKQ", 12 * k, 12 * k + 12))
             if k % 2:
-                d = pair("2")
-                mms([(c2(d, h, 384, 2), [(ap("ID"), ap("M5", S[:, :, k - 1 + h])), (ap("NID"), ap("Y"))]) for h in range(2)])
+                d = "D" + P["D2"][n][k // 2 % len(P["D2"][n])]
+                mms([(c2(d, h, 384, 2), [(ap("ID"), ap("M5", S[:, :, k - 1 + h])), (ap("NID"), yy)]) for h in range(2)])
                 act(ap("M2", S[:, :, k - 1:k + 1]), c2(d, 0, 384), AF.Relu)
-        for k in range(S2, 16):
-            tt(ap("M2", S[:, :, k]), ind(rw, c2("SKQ", 12 * k, 12 * k + 12)), ap("Y"), OP.min)
-        for (a, b) in P["C2"]:
-            if a >= S2 and b > a:
-                mm(ap("KA", S[:, 0:12, a:b]), [(ap("ID"), ap("KMX", S[:, :, a:b]))] + [(sel(r), ap("M2", S[:, r::16, a:b])) for r in range(16)])
-            elif b > a:
-                mm(ap("KA", S[:, 0:12, 0:S2]), [(ap("ID"), ap("KMX", S[:, :, 0:S2]))] + [(sel(r), ap("M5", S[:, r::16, 0:S2])) for r in range(16)]
-                   + [(sel(r, "NSEL"), ap("M2", S[:, r::16, 0:S2])) for r in range(16)])
-        sec[0] = "b"
+        landed = [tt(ap("M2", S[:, :, k]), ind(rw, c2("SKQ", 12 * k, 12 * k + 12)), yy, OP.min) for k in range(S2, 16)][0]
+        ops[dma("Y", c2(XN, OWN, OWN + V_), c2(R, OWN, OWN + V_), 4000)]["deps"][landed] = True
+        if n == 0:
+            for (a, b) in ((192, 384), (384, 768), (768, 1536), (1536, 3072)):
+                ops[dma("Y", c2("D4", a, b), c2("D4", 0, b - a), 2500)]["deps"][landed] = True
+        gcp(c2("D4", P["A4"], 3072, 16), yy)
+        k2 = (S2 + 16) // 2 + P["K2"]
+        add("P", [("matmul", [ka, ap("ID"), ap("KMX"), True, False], {})], 60 + 192 * P["PE"])
+        for (a, b, t, m) in ((0, S2, "SEL", "M5"), (S2, k2, "SEL", "M2"), (0, S2, "NSEL", "M2"), (k2, 16, "SEL", "M2")):
+            add("P", [("matmul", [ap("KA", S[:, 0:12, a:b]), sel(r, t), ap(m, S[:, r::16, a:b]), False, b == 16 and r == 15], {}) for r in range(16)],
+                60 + 16 * max(64, 12 * (b - a)) * P["PE"])
+        step1(n, P["POS"][n], 6)
         scan(ap("KI"), ap("RBIG"), c2("KB", 0, 192), 0.0, OP.add, OP.min)
         if n:
-            tt(wn("J0"), ends("KI"), small2, OP.min)
+            tt(wn("J0"), ends("KI"), kw2, OP.min)
         ts(wn("JI"), wn("J0") if n else ends("KI"), 15, OP.bitwise_and)
         cp(wh("JB"), wn("JI"))
         tt(wf("DB"), wn("JI"), wf("BB"), OP.subtract)
         if not last:
-            act(wb("BH"), wf("BB"), AF.Copy)
+            gcp(wb("BH"), wf("BB"))
         spread("PB", wh("JB", 0, 28), False)
         more(c2("PB", 256, 448), ap("NID"), ap("W"))
         ts(ap("MJ"), c2("PB", 0, 192), PM, OP.is_equal)
-        tt(ap("LJM"), ap("MJ"), lp, OP.mult)
+        early = tt(ap("LJM"), ap("MJ"), lp, OP.mult)
         pick(small, "LJM")
         act(wf("LJ"), small, AF.Copy)
         tt(wf("DL"), wf("LJ"), wf("LB"), OP.subtract)
         if not last:
-            cp(wu("LJU"), wf("LJ"))
+            cp(wu("LJU"), small)
             gat("S", ap("TOLD"), c2("TT", 0, R0), wu("LJU"))
         sec[0] = "c"
-        if P["SCAN3"]:
-            scan(ap("KS"), r01, ka, 0.0, OP.mult, OP.max)
-        else:
-            cp(ap("ST"), ka)
-            scan(ap("KS"), r01, ap("ST"), 0.0, OP.mult, OP.max)
-        tt(ap("NOH"), ap("KS"), ka, OP.not_equal)
         ts(ap("BI"), ka, thc, OP.is_ge)
-        scan(ap("PS"), ap("NOH"), c2("PA", 0, 192), 0.0, OP.mult, OP.add)
         scan(ap("CN"), r01, ap("BI"), 0.0, OP.mult, OP.add)
         ts(wf("OCC"), ends("CN"), PAR, OP.subtract, 3.0, OP.is_ge)
-        tt(wf("A"), ends("PS"), wf("OCC"), OP.mult)
+        for (a, b) in parts():
+            kh = ap("KA", S[:, a:b, :])
+            if P["STS"] > (a > 0):
+                act(c2("ST", 16 * a, 16 * b), kh, AF.Copy)
+            else:
+                cp(c2("ST", 16 * a, 16 * b), kh)
+            scan(c2("KS", 16 * a, 16 * b), c2("R01", 16 * a, 16 * b), c2("ST", 16 * a, 16 * b), 0.0, OP.mult, OP.max)
+            tt(c2("NOH", 16 * a, 16 * b), c2("KS", 16 * a, 16 * b), kh, OP.not_equal)
+            scan(c2("PS", 16 * a, 16 * b), c2("NOH", 16 * a, 16 * b), c2("PA", 16 * a, 16 * b), 0.0, OP.mult, OP.add)
+            tt(wf("A%d" % a, 0, MB_), c2("PS", 16 * a + 15, 16 * b, 16), wf("OCC", a, b), OP.mult)
         ts(wu("PLU"), ends("PS"), float(V_), OP.add)
-        tt(ap("XS"), ind(rw, wu("PLU")), ap("Q"), OP.subtract)
         nv, ov = "NV%d" % n, "OV%d" % n
-        ts(ap(nv), ap("XS"), 192.0, OP.add, 0.0, OP.max)
+        if P["XSS"] == 2:
+            gat("S", ap("XS"), rw, wu("PLU"))
+            mm(c2("D0", 0, 192), [(ap("ID"), ap("XS")), (ap("NID"), ap("Q"))])
+            act(ap(nv), c2("D0", 0, 192), AF.Relu, bias=192.0)
+        else:
+            tt(ap("XS"), ind(rw, wu("PLU")), ap("Q"), OP.subtract)
+            if P["XSS"]:
+                act(ap(nv), ap("XS"), AF.Relu, bias=192.0)
+            else:
+                ts(ap(nv), ap("XS"), 192.0, OP.add, 0.0, OP.max)
         send([(ap(nv), ap(ov), HOPS[n], "x%d" % n)], 2500)
-        lowest("A", "J", "DU1", c2("NO", 16 * n, 16 * n + 12), P["NS1"])
+        for (a, b) in parts():
+            lowest_half(a, b, c2("NO", 16 * n + a, 16 * n + b), P["NS1"])
         send([(c2("NO", 16 * n, 16 * n + 12), c2("OO", 16 * n, 16 * n + 12), HOPS[n], "x%d" % n)], 2500)
         for (a, b) in parts():
             cp(ind(c2(R, 0, FA), c2("NO", 16 * n + a, 16 * n + b)), c2(nv, 16 * a, 16 * b))
         if not last:
             send([(rw, c2(XN, 0, V_), HOPS[n] - HOPS[n + 1], "r%d" % (n + 2))], 8000)
-        sec[0] = "d"
-        for (a, b) in parts():
-            cp(ind(c2(XN, OWN, OWN + FA), c2("OO", 16 * n + a, 16 * n + b)), c2(ov, 16 * a, 16 * b))
-        if last:
-            dma("Y", ap("yx"), c2(XN, OWN, OWN + V_), 4000)
-        sec[0] = "c"
-        ts(wf("PL"), ends("PS"), float(V_ - FA), OP.add)
+        act(wf("C4"), wf("OCC"), AF.Identity, scale=131072.0, bias=-131072.0)
+        tt(wf("SY"), wf("C4"), sy, OP.add)
+        act(ap("THR"), ind(wf("SY", 0, 16), wu("IQ")), AF.Identity, scale=-1.0, bias=thc)
+        act(wf("PL"), ends("PS"), AF.Identity, bias=float(V_ - FA))
         tt(wf("DP"), wf("LJ"), wf("PL"), OP.subtract)
         if not last:
-            mm(c2("PA", 0, 192), [(ap("IDF"), gg), (ap("NIDF"), ap("TOLD"))])
+            gcp(ap("GH"), gg)
+            gcp(ap("TH2"), ap("TOLD"))
+            mm(c2("PA", 0, 192), [(ap("ID"), ap("CV")), (ap("ID"), ap("GH")), (ap("NID"), ap("TH2"))])
         sec[0] = "d"
         a4 = P["A4"]
-        for k in range(a4):
-            tt(c2("A4", k, 3072, 16), ind(rw, c2("SKQ", 12 * k, 12 * k + 12)), ap("Y"), OP.subtract)
         for k in range(a4, 16):
             gat("S", c2("A4", k, 3072, 16), rw, c2("SKQ", 12 * k, 12 * k + 12))
-        for j in range(3):
-            scan(c2("FS", 1024 * j, 1024 * j + 1024), c2("D4", 1024 * j, 1024 * j + 1024), c2("A4", 1024 * j, 1024 * j + 1024), 0.0, OP.add, OP.max)
-        for k in range(a4):
-            if k < P["M0S"]:
-                act(ap("M2", S[:, :, k]), c2("A4", k, 3072, 16), AF.Relu, scale=-1.0)
+        row = []
+        left = {"a": list(range(a4)), "x": parts(), "f": [0, 1, 2], "r": list(P["G5V"][n]), "m": list(range(a4))}
+        for c in P["ROW"]:
+            if not left[c]:
+                continue
+            k = left[c].pop(0)
+            if c == "a":
+                row.append(tt(c2("A4", k, 3072, 16), ind(rw, c2("SKQ", 12 * k, 12 * k + 12)), yy, OP.subtract))
+                if k >= P["JT"]:
+                    ops[row[-1]]["deps"].setdefault(early, False)
+            elif c == "x":
+                row.append(cp(ind(c2(XN, OWN, OWN + FA), c2("OO", 16 * n + k[0], 16 * n + k[1])), c2(ov, 16 * k[0], 16 * k[1])))
+            elif c == "f":
+                row.append(scan(c2("FS", 1024 * k, 1024 * k + 1024), c2("D4", 1024 * k, 1024 * k + 1024), c2("A4", 1024 * k, 1024 * k + 1024), 0.0, OP.add, OP.max))
+            elif c == "r":
+                row.append(gat("V", c2("RAW5", 512 * k, 512 * k + 512), c2(XN, FA, FA + R0), c2("WK", 32 * k, 32 * k + 32)))
             else:
-                ts(ap("M2", S[:, :, k]), c2("A4", k, 3072, 16), -1.0, OP.mult, 0.0, OP.max)
+                row.append(ts(ap("M2", S[:, :, k]), c2("A4", k, 3072, 16), -1.0, OP.mult, 0.0, OP.max))
+        for x in range(6):
+            if x not in P["G5V"][n]:
+                gat("S", c2("RAW5", 512 * x, 512 * x + 512), c2(XN, FA, FA + R0), c2("WK", 32 * x, 32 * x + 32))
+        if P["FIXROW"]:
+            for a, b in zip(row, row[1:]):
+                ops[b]["deps"].setdefault(a, False)
+        if last:
+            dma("Y", ap("yx"), c2(XN, OWN, OWN + V_), 4000)
         for k in range(a4, 16, 2):
             d = pair("4")
-            mms([(c2(d, h, 384, 2), [(ap("ID"), ap("Y")), (ap("NID"), c2("A4", k + h, 3072, 16))]) for h in range(2)])
+            mms([(c2(d, h, 384, 2), [(ap("ID"), yy), (ap("NID"), c2("A4", k + h, 3072, 16))]) for h in range(2)])
             act(ap("M2", S[:, :, k:k + 2]), c2(d, 0, 384), AF.Relu)
         for (a, b) in (((0, a4), (a4, 16)) if P["O4"] else ((a4, 16), (0, a4))):
             mm(ap("KA", S[:, 0:12, a:b]), [(sel(r, "NSEL"), ap("M2", S[:, r::16, a:b])) for r in range(16)])
         tt(ap("BI"), ka, ap("THR"), OP.is_ge)
         scan(ap("CN"), r01, ap("BI"), 0.0, OP.mult, OP.add)
-        ts(wf("C4"), ends("CN"), PAR, OP.subtract, 3.0, OP.is_lt)
-        tt(wb("EX"), wf("C4"), wf("OCC"), OP.is_ge)
+        ts(wb("EX"), ends("CN"), PAR, OP.subtract, 3.0, OP.is_lt)
         sec[0] = "e"
         for u in range(6):
-            if u % 2 == 0:
-                for x in (u, u + 1):
-                    gat("V" if x in P["G5V"][n] else "S", c2("RAW5", 512 * x, 512 * x + 512), c2(XN, FA, FA + R0), c2("WK", 32 * x, 32 * x + 32))
             dist("RAW5", "M5", lambda a, b: c2("FS", 16 * a + 15, 16 * b, 16), 0.0, u)
             if u % 2:
                 keys(256, "M5", u // 2)
@@ -542,12 +598,14 @@ def build():
             tt(wh("XL"), wb("EX"), wf("LB"), OP.mult)
             spread("KA", wh("XL"), False)
             lowest("A2", "DU2", "DU2", wu("O2"), P["NS2"])
-            spread("PB", wb("EX"))
-            tt(ap("LJX"), ap("LJM"), xp, OP.mult)
-            mm(xp, [(ap("ID"), ap("L1")), (ap("NID"), ap("LJX"))])
-            cp(ap("LK"), xp)
+            tt(wf("JX"), wn("JI"), wf("E16"), OP.subtract)
+            tt(ap("OHJ"), ind(wf("JX", 0, 16), wu("IQ")), ap("RIM"), OP.is_equal)
         else:
             spread("KA", wh("LBH"), False)
+            act(ap("MBR"), ap("MB"), AF.Identity, scale=4096.0, bias=-4096.0 - X0)
+            act(ap("LJX"), ap("L1"), AF.Identity, bias=-float(X0))
+            act(ap("ZT"), ap("W"), AF.Identity, bias=-float(X0))
+            more(ap("KA", S[:, 16:28, :]), ap("ID"), ap("MBR"), False)
         tt(wf("T1", 0, 48), ind(wb("EX", 0, 16), wu("IR", 0, 3)), wf("DL", 0, 48), OP.mult)
         tt(wf("LB", 0, 48), wf("LB", 0, 48), wf("T1", 0, 48), OP.add)
         if last:
@@ -577,42 +635,60 @@ def build():
         ts(wn("WI"), ends("KI"), 15, OP.bitwise_and)
         tt(wb("WB"), wn("WI"), wf("E16"), OP.add)
         spread("KB", wb("WB"))
-        ts(ap("MW"), c2("KB", 0, 192), PM16, OP.is_equal)
+        for (a, b) in (parts() if P["MWH"] and not last else [(0, 12)]):
+            ts(c2("MW", 16 * a, 16 * b), c2("KB", 16 * a, 16 * b), PM16, OP.is_equal)
+            if not last:
+                tt(c2("MD", 16 * a, 16 * b), c2("MW", 16 * a, 16 * b), c2("PA", 16 * a, 16 * b), OP.mult)
         if not last:
-            tt(ap("MD"), ap("MW"), c2("PA", 0, 192), OP.mult)
             for (a, b) in parts():
                 tt(ind(ap("TT"), wu("O2", a, b)), c2("MD", 16 * a, 16 * b), c2("TOLD", 16 * a, 16 * b), OP.add)
         tt(ap("BW"), ap("MW"), c2("PB", 256, 448), OP.mult)
         more(ap("KA", S[:, 16:28, :]), ap("NBLK"), ap("BW"))
-        tt(ap("MBR"), ap("MB"), ap("KA", S[:, 16:28, :]), OP.mult)
-        mm(lp, [(ap("ID"), ap("L1")), (ap("ID"), ap("MBR"))] + ([] if last else [(ap("NID"), ap("LJX"))]))
-        mm(wp, [(ap("ID"), ap("W")), (ap("ID"), ap("BW"))])
         if last:
-            act(ap("OW"), wp, AF.Identity, bias=-float(X0))
-            dma("Y", ap("yw"), ap("OW"), 2200)
-            act(ap("OL"), lp, AF.Identity, bias=-float(X0))
-            dma("S", ap("yl"), ap("OL"), 2200)
+            tt(ap("OW"), ap("BW"), ap("ZT"), OP.add)
+            dma("S", ap("yw"), ap("OW"), 2200)
+            tt(ap("OL"), ap("KA", S[:, 16:28, :]), ap("LJX"), OP.max)
+            dma("Y", ap("yl"), ap("OL"), 2200)
         else:
+            mm(c2("KB", 256, 448), [(ap("BLK"), ap("MW"))])
+            tt(ap("LJX"), ap("LJM"), c2("KB", 256, 448), OP.mult)
+            mm(wp, [(ap("ID"), ap("W")), (ap("ID"), ap("BW"))])
+            tt(ap("MBR"), ap("MB"), ap("KA", S[:, 16:28, :]), OP.mult)
+            mm(lp, [(ap("ID"), ap("L1")), (ap("ID"), ap("MBR")), (ap("NID"), ap("LJX"))])
             cp(ap("WK"), wp)
             act(ap("MB"), lp, AF.Relu, scale=-1.0, bias=1.0)
             act(ap("L1"), lp, AF.Copy)
             act(ap("W"), wp, AF.Copy)
             sec[0] = "e"
             bound(n + 1)
-            step1(n + 1)
-            pick(small2, "BW", "NSE1", wh("XL"))
-            cp(wu("WWU"), small2)
+            step1(n + 1, 0, P["POS"][n + 1])
+            pick(ww, "BW", "NSE1", wh("XL"))
+            cp(wu("WWU"), ww)
             gat("S", ap("VW"), c2(XN, FA, FA + R0), wu("WWU"))
             mm(xp, [(ap("ID"), ap("VW")), (ap("NID"), ap("Z"))])
-            act(ap("VA"), xp, AF.Abs, bias=1024.0)
-            pick(small2, "VA", "SEL", wb("BH"))
+            act(va, xp, AF.Abs, bias=1024.0)
+            limit(n + 1)
+            if n + 2 < RO:
+                cp(ap("LK"), lp)
+    for (a, j, b, k) in P["BEFORE"]:
+        for o in ops:
+            if o["tag"] == "aVGG":
+                first, seen, was = None, 0, 0
+            elif o["tag"] == a:
+                was += 1
+                if was <= j + 1:
+                    first = o["id"]
+            elif o["tag"] == b:
+                seen += 1
+                if seen > k and first is not None:
+                    o["deps"].setdefault(first, False)
     return ops
 
 
-def links(ops):
+def links(ops, soft=True):
     pred = []
     for o in ops:
-        p = {}
+        p = {d: P["OTHER"] for d in o["soft"]} if soft else {}
         for d, wait in o["deps"].items():
             p[d] = (P["OTHER"] if ops[d]["eng"] != o["eng"] else P["SAME"]) if wait else None
         for d in o["after"]:
@@ -715,9 +791,34 @@ def refine(ops, start, rounds):
     best, bst = worth(start), list(start)
     tags = sorted(set(o["tag"] for o in ops if o["tag"][0] != "i"))
     now, cst = best, bst
+
+    def held(st):
+        prev, out = {}, []
+        for e in "VSPGY":
+            row = sorted([i for i in range(n) if ops[i]["eng"] == e], key=lambda i: st[i])
+            prev.update(zip(row[1:], row))
+        i = max(range(n), key=lambda i: st[i] + ops[i]["cost"])
+        while i is not None:
+            d = next((d for d, l in fwd[i] if st[d] + l > st[i] - 1.0), None)
+            if d is None and i in prev and st[prev[i]] + ops[prev[i]]["busy"] > st[i] - 1.0:
+                d = prev[i]
+                if ops[d]["tag"] != ops[i]["tag"]:
+                    out.append((ops[d]["tag"], ops[i]["tag"]))
+            i = d
+        return out
+
     for it in range(rounds):
         kind = rng.random()
-        if kind < 0.6:
+        if it % 20 == 0:
+            hot = held(cst)
+        if kind < P["HOT"] and hot:
+            shift = {}
+            for _ in range(int(rng.integers(1, 3))):
+                u, v = hot[int(rng.integers(len(hot)))]
+                x = float(rng.exponential() * rng.choice([300.0, 1000.0, 3000.0]))
+                shift.update({u: x} if rng.random() < 0.5 else {v: -x})
+            cur = [s + shift.get(o["tag"], 0.0) for s, o in zip(cst, ops)]
+        elif kind < 0.7:
             shift = {tags[int(rng.integers(len(tags)))]: float(rng.normal() * rng.choice([300.0, 1500.0, 5000.0])) for _ in range(int(rng.integers(1, 4)))}
             cur = [s + shift.get(o["tag"], 0.0) for s, o in zip(cst, ops)]
         else:
@@ -737,6 +838,96 @@ def refine(ops, start, rounds):
     return order, bst
 
 
+def polish(ops, start, rounds):
+    n = len(ops)
+    pred = links(ops, False)
+    banks = [sorted(o["banks"]) for o in ops]
+    gap = P["OTHER"]
+    above, lag = [], []
+    for i in range(n):
+        far = 0
+        for d in pred[i]:
+            far |= above[d]
+        lag.append([(d, 0.0 if l is None else ops[d]["cost"] + l) for d, l in pred[i].items() if not far >> d & 1 or ops[d]["dma"]])
+        for d in pred[i]:
+            far |= 1 << d
+        above.append(far)
+    eng = ["VSPGY".index(o["eng"]) for o in ops]
+    busy, cost = [o["busy"] for o in ops], [o["cost"] for o in ops]
+    rng = np.random.default_rng(P["SEED"])
+
+    def run(seq):
+        st, by, free, lastop, inb = [0.0] * n, [-1] * n, [0.0] * 5, [-1] * 5, {}
+        for i in seq:
+            e = eng[i]
+            t, b = free[e], lastop[e]
+            for d, l in lag[i]:
+                if st[d] + l > t:
+                    t, b = st[d] + l, -2 - d
+            for k in banks[i]:
+                d = inb.get(k, i)
+                if eng[d] != e and st[d] + cost[d] + gap > t:
+                    t, b = st[d] + cost[d] + gap, d
+                inb[k] = i
+            st[i], by[i] = t, b
+            free[e], lastop[e] = t + busy[i], i
+        rest, nxt, inb = list(cost), [0.0] * 5, {}
+        for i in reversed(seq):
+            e = eng[i]
+            t = max(rest[i], nxt[e] + busy[i])
+            for k in banks[i]:
+                d = inb.get(k, i)
+                if eng[d] != e and rest[d] + cost[i] + gap > t:
+                    t = rest[d] + cost[i] + gap
+                inb[k] = i
+            rest[i] = nxt[e] = t
+            for d, l in lag[i]:
+                if t + l > rest[d]:
+                    rest[d] = t + l
+        way = np.array(st) + np.array(rest)
+        end = float(way.max())
+        near = way - (end - wide)
+        return end, end + P["MASS"] * float(np.maximum(near, 0.0).sum()) / wide, st, [(by[i], i) for i in np.flatnonzero(near > 0).tolist() if by[i] >= 0]
+
+    wide = P["WIDE"]
+    seq = sorted(range(n), key=lambda i: (start[i], i))
+    best, now, bst, held = run(seq)
+    bseq = seq
+    for it in range(rounds):
+        u, v = held[int(rng.integers(len(held)))]
+        a, b = seq.index(u), seq.index(v)
+        more = int(rng.geometric(0.45)) - 1
+        if rng.random() < 0.5:
+            while more and a > 0:
+                a -= 1
+                more -= eng[seq[a]] == eng[v]
+            mid = seq[a:b + 1]
+            go = [i for i in mid if i == v or above[v] >> i & 1]
+            if u in go:
+                continue
+            new = seq[:a] + go + [i for i in mid if not (i == v or above[v] >> i & 1)] + seq[b + 1:]
+        else:
+            while more and b < n - 1:
+                b += 1
+                more -= eng[seq[b]] == eng[u]
+            mid = seq[a:b + 1]
+            go = [i for i in mid if i == u or above[i] >> u & 1]
+            if v in go:
+                continue
+            new = seq[:a] + [i for i in mid if not (i == u or above[i] >> u & 1)] + go + seq[b + 1:]
+        t, w, s2, h2 = run(new)
+        if w <= now + P["COOL"] * (1.0 - it / rounds) * rng.exponential():
+            now, held = w, h2
+            seq = sorted(new, key=lambda i: s2[i])
+            if t < best:
+                best, bst, bseq = t, s2, seq
+    inb = {}
+    for i in bseq:
+        ops[i]["soft"] = set(inb[k] for k in banks[i] if k in inb and eng[inb[k]] != eng[i])
+        inb.update({k: i for k in banks[i]})
+    return {e: [i for i in bseq if ops[i]["eng"] == e] for e in "VSPGY"}, bst
+
+
 PLAN = {}
 
 
@@ -746,7 +937,9 @@ def rank_program(g, core, T, topo):
         return
     if not PLAN:
         PLAN["ops"] = build()
-        PLAN["order"] = refine(PLAN["ops"], schedule(PLAN["ops"])[1], P["ROUNDS"])[0]
+        start = refine(PLAN["ops"], schedule(PLAN["ops"])[1], P["ROUNDS"])[1]
+        P.update(P["AGAIN"])
+        PLAN["order"] = polish(PLAN["ops"], refine(PLAN["ops"], start, P["ROUNDS"])[1], P["POLISH"])[0]
     ops, order = PLAN["ops"], PLAN["order"]
     N = len(T.cores)
     q = {"V": g.vector, "S": g.scalar, "P": g.tensor, "G": g, "Y": g.sync}
@@ -754,7 +947,7 @@ def rank_program(g, core, T, topo):
     waits = []
     for o in ops:
         far = {}
-        for d, wait in o["deps"].items():
+        for d, wait in list(o["deps"].items()) + [(d, True) for d in o["soft"]]:
             key = d if ops[d]["dma"] else ops[d]["eng"]
             if wait and (key not in far or place[d] > place[far[key]]):
                 far[key] = d
@@ -788,7 +981,7 @@ def rank_program(g, core, T, topo):
 
     meth = {"tensor_copy": lambda e: e.tensor_copy, "tensor_tensor": lambda e: e.tensor_tensor, "tensor_scalar": lambda e: e.tensor_scalar,
             "tensor_tensor_scan": lambda e: e.tensor_tensor_scan, "tensor_reduce": lambda e: e.tensor_reduce, "transpose": lambda e: e.transpose,
-            "memset": lambda e: e.memset, "activation": lambda e: e.activation, "matmul": lambda e: e.matmul, "iota": lambda e: e.iota,
+            "memset": lambda e: e.memset, "activation": lambda e: e.activation, "matmul": lambda e: e.matmul, "iota": lambda e: e.iota, "affine_select": lambda e: e.affine_select,
             "dma_start": lambda e: e.dma_start, "partition_broadcast": lambda e: e.partition_broadcast}
     for e in "VSPYG":
         seen = {}

import numpy as np
from concourse.bass import DstId, RemoteDMATransfer
from concourse.mybir import AluOpType as OP, AxisListType, ActivationFunctionType as AF

V_, A_, M_, RO = 2048, 1024, 192, 4
HOPS = [1, 2, 4, 7]
S = np.s_
F, B, I, U, H = "float32", "bfloat16", "int32", "uint16", "float16"
X0, R0 = 16, 16 + A_
FA, OWN = V_ + M_, V_ + M_ + 16
MB_ = 6
SEG = [(q // MB_) * 8 * MB_ * (MB_ + 1) + 8 * (q % MB_) * (q % MB_ + 1) for q in range(13)]
NP = SEG[12]

P = {"S2": [6, 4, 4, 4],
     "A4": 8,
     "G1V": [(0, 2, 4), (0,), (0,), (0,)],
     "G5V": [(0, 2), (0, 2), (0, 2), (0, 2, 4)],
     "DB": {"1": "01", "2": "2", "4": "012", "5": "012"},
     "K2": 1, "O4": 1, "ZS": 1, "M0S": 0, "SCAN3": 0, "WAW": 1, "EBV": 0, "VS": 1, "JT": 16, "BEFORE": [("bVLJM", 0, "dVA4", 3), ("cPPA", 9, "ePKB", 0)], "FIXROW": 0, "ROW": "aaaaaaaaxmmxfrmmfmmmmrfr", "POS": [6, 6, 6, 6], "D2": ["201", "2", "2", "2"], "XSS": 0, "R1": (), "MWH": 1, "STS": 0, "NS1": (6, 7, 8, 9, 10, 11, 5, 4), "NS2": (),
     "CY": 0.96, "PE": 0.48, "GA": 1.56, "SC": 3.8, "TT": 2.0, "FIX": 20.0, "SAME": 150.0, "OTHER": 200.0, "SLACK": 150.0, "NET": 1.25,
     "SEED": 4, "ROUNDS": 2500, "HEAT": 800.0, "HOT": 0.4, "AGAIN": {"SEED": 11, "ROUNDS": 4000, "HEAT": 250.0, "HOT": 0.5}, "POLISH": 2000, "COOL": 40.0, "MASS": 2.0, "WIDE": 300.0}

SCRATCH = {}


def _sb(names, shape, dt):
    for n in names.split():
        SCRATCH[n] = ("sbuf", list(shape), dt)


_sb("XR0 XR1 XR2 XR3 XR4", [128, OWN + FA], B)
_sb("NV0 NV1 NV2 NV3 OV0 OV1 OV2 OV3", [128, 192], B)
_sb("NO OO", [128, 64], U)
_sb("NE FL MM", [128, NP], B)
_sb("TT", [128, R0 + M_], F)
_sb("SBI", [128, R0], I)
_sb("LAI LWI KI B0I", [128, 192], I)
_sb("GG", [128, 224], F)
_sb("TR", [128, 416], F)
_sb("KS ST PS TOLD MD THR OL OW OB", [128, 192], F)
_sb("EXP Z ZT LJM LJX MBR BW SQK L1 W GH TH2", [128, 192], H)
_sb("YV", [128, 384], B)
_sb("Z0 RI RV RBIG R01 MRV BI CN NOH XS Q MW MJ MB ZO VW CV OHJ RIM", [128, 192], B)
_sb("SKQ LK WK", [128, 192], U)
_sb("M1 M2 M5", [128, 192, 16], B)
_sb("KMX", [128, 12, 16], B)
_sb("A4 FS D4 RAW1 RAW5", [128, 3072], B)
_sb("SEL NSEL SE1 NSE1", [128, 144], B)
_sb("T143", [128, 144], F)
_sb("BLKF", [128, 128], F)
_sb("BLK NBLK ID NID IBG E8 IOB", [128, 128], B)
_sb("EB", [128, 2048], B)
_sb("WF", [128, 544], F)
_sb("WN", [128, 128], I)
_sb("WU", [128, 256], U)
_sb("WH", [128, 128], H)
_sb("WB", [128, 64], B)
_sb("TH", [128, 16], F)
_sb("THI THB", [128, 8], I)
SCRATCH["KA"] = ("psum", [128, 32, 16], F)
for _n in "D0 D1 D2 KB PA PB PC".split():
    SCRATCH[_n] = ("psum", [128, 512], F)

TABS = {"WF": "LJ LB PL BB DL DP DB T1 T1b T1c OCC C4 E16 E1 E2 SY A0 A6 A2 AM AM0 AM6 JX E10 E16b J Q C DU1 DU2 T2 T3 THM".split(),
        "WN": "P JI WI N1 N2 KK J0".split(),
        "WU": "LBU SELU PLU LJU IQ IQK IKQ IR WWU O2 IRV IEND IENH".split(),
        "WH": "XL JB LBH".split(),
        "WB": "EX WB BH".split()}

SEMAPHORES = (["cV", "cS", "cP", "cG", "loc", "th"] + ["d%d" % i for i in range(24)] + ["r%d" % i for i in range(5)]
              + ["x%d" % i for i in range(4)])
IOS = "xs sb la lw z0 b0 th yx yl yw yz yb".split()


def ap(name, idx=S[:]):
    return ("ap", name, idx)


def c2(name, a, b, s=1):
    return ap(name, S[:, a:b:s])


def tab(t):
    def f(n, a=0, b=12, s=1):
        return c2(t, 16 * TABS[t].index(n) + a, 16 * TABS[t].index(n) + b, s)
    return f


wf, wn, wu, wh, wb = tab("WF"), tab("WN"), tab("WU"), tab("WH"), tab("WB")


def ind(win, off):
    return ("ind", win, off)


def cols(a):
    shape = SCRATCH[a[1]][1]
    idx = a[2] if isinstance(a[2], tuple) else (a[2],)
    return np.arange(int(np.prod(shape[1:]))).reshape(shape[1:])[idx[1:]].reshape(-1)


def bits(a):
    m = 0
    for x in cols(a):
        m |= 1 << int(x)
    return m


def build():
    ops = []
    acc = {}
    lands = {}
    sec = ["i"]
    CY = P["CY"]

    def touch(me, a, write):
        if a[1] in IOS:
            return
        psum = SCRATCH[a[1]][0] == "psum"
        m = bits(a)
        if psum:
            me["banks"].add(a[1])
        for (lm, sem, o) in lands.get(a[1], []):
            if lm & m and o not in me["after"]:
                me["ext"].append(sem)
                me["after"].append(o)
        for (o, om, ow) in acc.setdefault(a[1], []):
            if o == me["id"]:
                continue
            hit = (m & om) != 0
            if hit and ow and not write:
                me["deps"][o] = True
            elif hit and (write or ow):
                me["deps"][o] = True
            elif psum and ops[o]["eng"] != me["eng"]:
                me["soft"].add(o)
            elif psum and me["eng"] == "P":
                me["deps"].setdefault(o, False)
        acc[a[1]].append((me["id"], m, write))

    def add(eng, calls, cost, dma=None, busy=None):
        me = {"id": len(ops), "eng": eng, "calls": calls, "cost": cost, "dma": dma, "deps": {}, "ext": [], "soft": set(), "banks": set(),
              "busy": cost if busy is None else busy, "after": []}
        ops.append(me)
        a = calls[0][1][0]
        if a is None or a[0] == "ind":
            name = "send" if a is None else a[1][1][0] + "s"
        elif a[1] in TABS:
            name = TABS[a[1]][a[2][1].start // 16]
        else:
            name = a[1]
        me["tag"] = sec[0] + eng + name
        for (_, args, kw) in calls:
            for n, a in enumerate(list(args) + list(kw.values())):
                if isinstance(a, tuple) and a[0] == "ap":
                    touch(me, a, n == 0 or a is kw.get("accum_out"))
                elif isinstance(a, tuple) and a[0] == "ind":
                    touch(me, a[1], n == 0)
                    touch(me, a[2], False)
                elif isinstance(a, tuple) and a[0] == "rd":
                    touch(me, a[1], False)
        return me["id"]

    def vcost(eng, out, in0, rate):
        if in0[0] == "ind":
            return (50 if eng == "V" else 65) + 16 * len(cols(in0[2])) * P["GA"] * CY
        if out[0] == "ind":
            return 50 + 16 * len(cols(out[2])) * P["SC"] * CY
        return P["FIX"] + max(64, len(cols(in0)) * rate) * CY

    def half(*aps):
        return 0.5 if all(a[0] == "ap" and SCRATCH[a[1]][2] in (B, U, H) for a in aps) else 1.0

    def cp(out, in_):
        return add("V", [("tensor_copy", [out, in_], {})], vcost("V", out, in_, half(out, in_)))

    def tt(out, a, b, op):
        ps = any(x[0] == "ap" and SCRATCH[x[1]][0] == "psum" for x in (a, b))
        return add("V", [("tensor_tensor", [out, a, b, op], {})], vcost("V", out, a, 1.0 if ps else P["TT"]))

    def ts(out, a, s1, o0, s2=None, o1=None):
        args = [out, a, s1, s2, o0] + ([o1] if o1 is not None else [])
        return add("V", [("tensor_scalar", args, {})], vcost("V", out, a, half(out, a)))

    def scan(out, d0, d1, init, o0, o1):
        return add("V", [("tensor_tensor_scan", [out, d0, d1, init, o0, o1], {})], vcost("V", out, d1, half(out, d0, d1)))

    def red(out, a, op):
        return add("V", [("tensor_reduce", [out, a, AxisListType.X, op], {})], vcost("V", out, a, 1.0))

    def tr(out, a):
        return add("V", [("transpose", [out, a], {})], vcost("V", out, a, half(out, a)))

    def ms(out, v):
        return add("V", [("memset", [out, v], {})], vcost("V", out, out, half(out)))

    def act(out, a, f=AF.Identity, **kw):
        return add("S", [("activation", [out, a, f], kw)], vcost("S", out, a, 1.0))

    def gat(eng, out, win, off):
        return cp(out, ind(win, off)) if eng == "V" else act(out, ind(win, off), AF.Copy)

    def mms(groups):
        calls, cost = [], 60
        for out, pairs in groups:
            for n, (l, r) in enumerate(pairs):
                calls.append(("matmul", [out, l, r, n == 0, n == len(pairs) - 1], {}))
                cost += max(min(64, len(cols(l))), len(cols(r))) * P["PE"] * (4 if SCRATCH[l[1]][2] == F else 1)
        return add("P", calls, cost)

    def mm(out, pairs):
        return mms([(out, pairs)])

    def iota(out, pat, base, cm):
        kw = {} if SCRATCH[out[1]][2] == I else {"allow_small_or_imprecise_dtypes": True}
        return add("G", [("iota", [out, pat, base, cm], kw)], 130 + 2 * len(cols(out)) * CY)

    def gcp(out, a):
        n = len(cols(out))
        return add("G", [("affine_select", [out, a, [[0, n]], OP.is_equal, 0.0, 0, 0], {})], 170 + 2 * n * CY)

    nd = [0]

    def dma(eng, out, in_, cost):
        nd[0] += 1
        return add(eng, [("dma_start", [out, in_], {})], cost, dma=("d%d" % (nd[0] - 1), 16), busy=60)

    def send(parts, cost, busy=1000):
        o = add("G", [("send", [None, parts] + [("rd", p[0]) for p in parts], {})], cost * P["NET"], dma=("loc", None), busy=busy)
        for p in parts:
            lands.setdefault(p[1][1], []).append((bits(p[1]), p[3], o))
        return o

    def sel(r, t="SEL"):
        return c2(t, 15 - r, 143 - r)

    def eb(b, t="EB"):
        return c2(t, 128 * b, 128 * b + 128)

    def ends(name):
        return c2(name, 15, 192, 16)

    def spread(bank, src, stop=True):
        n = len(cols(src))
        calls = [("matmul", [ap(bank, S[:, 16:28, b]) if bank == "KA" else c2(bank, b, 16 * n, 16), eb(b), src, b == 0, stop and b == 15], {}) for b in range(16)]
        return add("P", calls, 60 + 16 * 64 * P["PE"])

    def more(out, l, r, stop=True):
        return add("P", [("matmul", [out, l, r, False, stop], {"acc": out})], 60 + len(cols(r)) * P["PE"])

    def pick(out, src, t="SE1", plus=None):
        mm(out, ([(ap("ID"), plus)] if plus else []) + [(sel(r, t), c2(src, r, 192, 16)) for r in range(16)])

    PM, WC, PAR, PM16, DUM = (wf("C", n, n + 1) for n in range(5))
    r01 = ap("R01")

    dma("Y", c2("XR0", OWN, OWN + A_), ap("xs", S[:, 0:A_]), 2600)
    dma("Y", c2("XR0", OWN + A_, OWN + V_), ap("xs", S[:, A_:V_]), 3500)
    dma("S", ap("B0I", S[0:8, :]), ap("b0"), 2200)
    dma("S", ap("LAI"), ap("la"), 2500)
    dma("S", ap("THI", S[0:1, :]), ap("th"), 2200)
    dma("S", ap("Z0"), ap("z0"), 3000)
    dma("Y", c2("SBI", X0, R0), ap("sb"), 5000)
    dma("S", ap("LWI"), ap("lw"), 3000)
    s0 = send([(c2("XR0", OWN, OWN + A_), c2("XR0", 0, A_), -HOPS[0], "r0")], 6000, busy=2500)
    ops[send([(c2("XR0", OWN + A_, OWN + V_), c2("XR0", A_, V_), -HOPS[0], "r1")], 5000)]["deps"][s0] = False
    iota(wn("P", 0, 1), [[0, 1]], 0, 1)
    iota(wf("Q", 0, 16), [[1, 16]], 0, 0)
    iota(ap("T143"), [[-1, 144]], 15, 1)
    iota(ap("IOB"), [[-16, 8], [0, 16]], 0, 1)
    iota(ap("E8", S[0:8, :]), [[-1, 8], [0, 16]], 0, 1)
    iota(ap("RI"), [[0, 12], [1, 16]], 0, 0)
    for q in range(12):
        iota(c2("MM", SEG[q], SEG[q + 1]), [[-1, SEG[q + 1] - SEG[q]]], 15, 0)
    ts(wn("P", 1, 2), wn("P", 0, 1), 15, OP.bitwise_and)
    ts(wn("P", 2, 3), wn("P", 0, 1), 4, OP.arith_shift_right, 1, OP.bitwise_and)
    cp(wf("C", 0, 2), wn("P", 1, 3))
    ms(PAR, 0.0)
    ts(PM16, PM, 16.0, OP.add)
    for n in range(RO + 1):
        ms(c2("XR%d" % n, V_ if n < RO else FA, OWN), 1024.0)
    ms(c2("TT", 0, X0), 0.0)
    ms(c2("SBI", 0, X0), 0)
    ms(ap("GG"), 0.0)
    ms(wf("LJ", 0, 16 * 23), 0.0)
    ms(wb("EX", 0, 16), 0.0)
    cp(wh("JB", 0, 32), wf("PL", 0, 32))
    ts(ap("E8", S[0:8, :]), ap("E8", S[0:8, :]), 0.0, OP.is_equal)
    ts(ap("SE1"), ap("T143"), PM, OP.is_equal)
    act(ap("SEL"), ap("SE1"), AF.Identity, scale=16.0)
    act(ap("NSEL"), ap("SE1"), AF.Identity, scale=-16.0)
    ts(ap("ID"), c2("T143", 15, 143), 0.0, OP.is_equal)
    act(ap("NID"), ap("ID"), AF.Identity, scale=-1.0)
    ts(ap("BLK"), ap("IOB"), PM, OP.is_equal)
    act(ap("NBLK"), ap("BLK"), AF.Identity, scale=-1.0)
    act(ap("BLKF"), ap("BLK"), AF.Identity, scale=1.0 / 16)
    act(ap("RV"), ap("RI"), AF.Identity, scale=-1.0, bias=15.0)
    act(ap("KMX"), ap("RV"), AF.Copy)
    act(ap("RIM"), ap("RI"), AF.Identity, bias=-16.0)
    act(ap("IBG"), ap("ID"), AF.Identity, scale=131072.0)
    ts(ap("MRV"), ap("RV"), PM, OP.is_equal)
    ts(ap("MM"), ap("MM"), PM, OP.is_ge)
    ts(ap("RBIG"), ap("RI"), 0.0, OP.is_equal, 1048576.0, OP.mult)
    ts(ap("R01"), ap("RI"), 0.0, OP.not_equal)
    ts(c2("D4", 0, 192), ap("RI"), 0.0, OP.is_equal, -1024.0, OP.mult)
    act(ap("NSE1"), ap("SE1"), AF.Identity, scale=-1.0)
    for b in range(16):
        add("G", [("affine_select", [eb(b), ap("BLK"), [[-16, 8], [0, 16]], OP.is_equal, 0.0, -b, 1], {})], 170 + 256 * CY)
    cp(wu("IQ"), wf("Q"))
    ts(wu("IR", 0, 3), wf("Q", 0, 3), 0.0, OP.mult, PM, OP.add)
    ts(wu("IRV"), wf("Q"), -1.0, OP.mult, 11.0, OP.add)
    ts(wf("J", 0, 16), wf("Q", 0, 16), 16.0, OP.mult, PM, OP.add)
    act(wf("DU1"), wf("J"), AF.Identity, bias=float(V_))
    act(wf("DU2"), wf("J"), AF.Identity, bias=float(R0))
    t3 = [wf("T3", x, x + 1) for x in range(8, 13)]
    ts(t3[0], PM, 11.0, OP.min, 1.0, OP.add)
    ts(wn("N1", 12, 13), t3[0], 1.0 / MB_, OP.mult, -0.5 - 0.5 / MB_, OP.add)
    ts(t3[1], wn("N1", 12, 13), -float(MB_), OP.mult, t3[0], OP.add)
    ts(t3[2], t3[1], 1.0, OP.add, t3[1], OP.mult)
    ts(t3[3], wn("N1", 12, 13), float(MB_ * (MB_ + 1)), OP.mult, t3[2], OP.add)
    ts(wu("IEND", 0, 1), t3[3], 8.0, OP.mult, -1.0, OP.add)
    ts(wu("IENH", 0, 1), t3[2], 8.0, OP.mult, -1.0, OP.add)

    def turned(dst, qq, base):
        ts(wn("N1"), qq, WC, OP.add)
        ts(wn("N2"), wn("N1"), 1, OP.bitwise_and)
        ts(wf("T2"), wn("N2"), 208.0, OP.mult)
        tt(wf("T2"), wf("T2"), base, OP.add)
        cp(dst, wf("T2"))

    turned(wu("IQK"), wf("Q"), wf("J"))
    ts(wn("KK"), wf("J"), 1.0 / 12, OP.mult, -5.5 / 12, OP.add)
    ts(wf("E1"), wn("KK"), -12.0, OP.mult)
    tt(wf("E1"), wf("E1"), wf("J"), OP.add)
    ts(wf("E2"), wf("E1"), 16.0, OP.mult)
    tt(wf("E2"), wf("E2"), wn("KK"), OP.add)
    turned(wu("IKQ"), wf("E1"), wf("E2"))
    add("G", [("partition_broadcast", [ap("THB"), ap("THI", S[0:1, :]), 128], {})], 180)
    ts(wf("T3", 0, 8), c2("BLK", 0, 128, 16), 16.0, OP.mult)
    tt(wf("THM", 0, 8), ap("THB"), wf("T3", 0, 8), OP.mult)
    red(wf("THM", 8, 9), wf("THM", 0, 8), OP.add)
    send([(wf("THM", 8, 9), c2("TH", 4 * n, 4 * n + 1), -HOPS[n], "th") for n in range(RO)], 3000)

    lp, wp = c2("PC", 0, 192), c2("PC", 256, 448)
    small, small2 = c2("PC", 192, 204), c2("PC", 448, 460)
    ts(ap("L1"), ap("LAI"), float(X0), OP.add)
    cp(ap("BI", S[0:8, :]), ap("B0I", S[0:8, :]))
    mm(c2("PB", 0, 192), [(ap("E8", S[0:8, :]), ap("BI", S[0:8, :]))])
    ts(ap("MB"), c2("PB", 0, 192), PM, OP.is_equal)
    tt(ap("LJM"), ap("MB"), ap("L1"), OP.mult)
    mm(lp, [(ap("ID"), ap("L1")), (ap("NID"), ap("LJM"))])
    cp(ap("LK"), lp)
    pick(small, "LJM")
    cp(wu("LBU"), small)
    cp(wf("LB"), small)
    act(ap("L1"), lp, AF.Copy)
    ts(ap("MJ"), ap("MB"), PM, OP.mult)
    pick(small2, "MJ")
    act(wf("BB"), small2, AF.Copy)
    ts(ap("WK"), ap("LWI"), float(X0), OP.add)
    ts(ap("W"), ap("LWI"), float(X0), OP.add)
    for a in range(X0, R0, 256):
        gcp(c2("TT", a, a + 256), c2("SBI", a, a + 256))
    ms(ap("CV"), float(V_))

    bank = [0]

    def pair(step):
        bank[0] += 1
        return "D" + P["DB"][step][bank[0] % len(P["DB"][step])]

    yy, va = c2("YV", 0, 192), c2("YV", 192, 384)
    sy, kw2, ww = c2("PB", 464, 476), c2("PB", 476, 488), c2("PB", 448, 460)

    def limit(n):
        calls = [("matmul", [c2("PB", 464, 488 if n else 476), sel(r), c2("YV", r, 384 if n else 192, 16), r == 0, r == 15 and not n], {}) for r in range(16)]
        if n:
            calls.append(("matmul", [kw2, ap("ID"), wb("BH"), False, True], {}))
        add("P", calls, 60 + 64 * len(calls) * P["PE"])

    def bound(n):
        gat("S", yy, c2("XR%d" % n, FA, FA + R0), wu("LBU"))
        act(ap("Q"), yy, AF.Identity, scale=0.25, bias=191.625)
        gcp(wh("LBH"), wf("LB"))

    def dist(raw, m, sub, off, u):
        j, h = u // 2, u % 2
        d = pair(m[1])
        mms([(c2(d, k, 512, 8), [(ap("ID"), c2(raw, 1024 * j + 8 * h + k, 1024 * j + 1024, 16)), (ap("NID"), sub(64 * j, 64 * j + 64))]) for k in range(8)])
        act(ap(m, S[:, 64 * j:64 * j + 64, 8 * h:8 * h + 8]), ap(d), AF.Abs, bias=off)

    def keys(at, m, j, shut=False):
        mm(c2("KB", at + 64 * j, at + 64 * j + 64), [(ap("ID"), c2("RI", 0, 64))] + [(ap("IBG"), c2("OHJ", 64 * j, 64 * j + 64))] * shut + [(sel(r), ap(m, S[:, 64 * j + r:64 * j + 64:16, :])) for r in range(16)])

    def lowest(a, base, du, off, onS):
        tt(ap("EXP"), ind(wf(a, 0, 16), wu("IRV")), ap("MRV"), OP.mult)
        tt(wf("AM"), wf(a), wf(base), OP.subtract)
        mm(c2("PA", 256, 448), [(ap("BLK"), ap("EXP"))])
        if onS:
            mm(c2("D2", 256, 448), [(ap("BLK"), ap("EXP"))])
        for q in sorted(range(12), key=lambda q: -(q % MB_)):
            lo, o = 256 + 16 * (11 - q), c2("NE", SEG[q], SEG[q + 1])
            if q in onS:
                act(o, c2("D2", lo, lo + SEG[q + 1] - SEG[q]), AF.Abs, bias=wf(a, q, q + 1), scale=-1.0)
            else:
                ts(o, c2("PA", lo, lo + SEG[q + 1] - SEG[q]), wf(a, q, q + 1), OP.not_equal)
        scan(ap("FL"), ap("NE"), ap("MM"), 1.0, OP.min, OP.max)
        tt(wf("E1", 0, 16), ind(ap("FL"), wu("IEND", 0, 1)), wf("AM", 0, 16), OP.mult)
        tt(wf("E2"), wf("E1"), wf(du), OP.add)
        cp(off, wf("E2"))

    def lowest_half(a, b, off, onS):
        t, x0, sb = "A%d" % a, 16 * (12 - b), "D2" if a else "D1"
        tt(c2("EXP", x0, x0 + 16 * MB_), ind(wf(t, 0, 16), wu("IRV", 12 - MB_, 12)), c2("MRV", 0, 16 * MB_), OP.mult)
        tt(wf("AM%d" % a, 0, MB_), wf(t, 0, MB_), wf("J", a, b), OP.subtract)
        if any(q not in onS for q in range(a, b)):
            mm(c2("PA", 256 + x0, 256 + x0 + 16 * MB_), [(ap("BLK"), c2("EXP", x0, x0 + 16 * MB_))])
        if any(q in onS for q in range(a, b)):
            mm(c2(sb, x0, x0 + 16 * MB_), [(ap("BLK"), c2("EXP", x0, x0 + 16 * MB_))])
        for q in range(b - 1, a - 1, -1):
            lo, o = 16 * (11 - q), c2("NE", SEG[q], SEG[q + 1])
            if q in onS:
                act(o, c2(sb, lo, lo + SEG[q + 1] - SEG[q]), AF.Abs, bias=wf(t, q - a, q - a + 1), scale=-1.0)
            else:
                ts(o, c2("PA", 256 + lo, 256 + lo + SEG[q + 1] - SEG[q]), wf(t, q - a, q - a + 1), OP.not_equal)
        fl = c2("FL", SEG[a], SEG[b])
        scan(fl, c2("NE", SEG[a], SEG[b]), c2("MM", SEG[a], SEG[b]), 1.0, OP.min, OP.max)
        e1 = "E16b" if a else "E10"
        tt(wf(e1, 0, 16), ind(fl, wu("IENH", 0, 1)), wf("AM%d" % a, 0, 16), OP.mult)
        tt(wf("E2", a, b), wf(e1, 0, MB_), wf("DU1", a, b), OP.add)
        cp(off, wf("E2", a, b))

    def parts():
        return [(q, q + MB_) for q in range(12 - MB_, -1, -MB_)]

    def step1(n, lo, hi):
        sec[0] = "b"
        for u in range(lo, hi):
            if u % 2 == 0 and n and u // 2 in P["R1"]:
                gat("S", c2("RAW1", 512 * u, 512 * u + 1024), c2("XR%d" % n, FA, FA + R0), c2("LK", 32 * u, 32 * u + 64))
            elif u % 2 == 0:
                for x in (u, u + 1):
                    w = 32 // P["VS"] if n and x in P["G1V"][n] else 32
                    for a in range(32 * x, 32 * x + 32, w):
                        gat("V" if x in P["G1V"][n] else "S", c2("RAW1", 16 * a, 16 * (a + w)), c2("XR%d" % n, FA, FA + R0), c2("LK", a, a + w))
            dist("RAW1", "M1", lambda a, b: c2("Z" if n else "Z0", a, b), 1024.0 if n else 0.0, u)
            if u % 2:
                keys(0, "M1", u // 2, n > 0)

    bound(0)
    limit(0)
    step1(0, 0, P["POS"][0])
    ka = ap("KA", S[:, 0:12, :])
    for n in range(RO):
        sec[0] = "a"
        R, XN = "XR%d" % n, "XR%d" % (n + 1)
        rw, both = c2(R, 0, V_), c2(R, 0, FA + R0)
        last = n == RO - 1
        thc = c2("TH", 4 * n, 4 * n + 1)
        zs, zoff = ("Z0", 0.0) if n == 0 else ("Z", 1024.0)
        gg = c2("GG", 16, 208)
        ts(gg, ind(c2("TT", 0, R0) if n else ap("SBI"), wu("LBU")), -float(V_), OP.add)
        tr(c2("TR", 0, 192), gg)
        tr(c2("TR", 192, 416), ap("GG"))
        ts(ap("SKQ"), ind(ap("TR"), wu("IKQ")), float(V_), OP.add)
        gat("S", ap("SQK"), ap("TR"), wu("IQK"))
        mms([(c2("PA", 0, 191), [(ap("ID"), c2("SQK", 0, 191)), (ap("NID"), c2("SQK", 1, 192))]), (c2("PA", 15, 192, 16), [(ap("ID"), ends("SQK"))])])
        S2 = P["S2"][n]
        for k in range(S2):
            gat("S", ap("M5", S[:, :, k]), rw, c2("SKQ", 12 * k, 12 * k + 12))
            if k % 2:
                d = "D" + P["D2"][n][k // 2 % len(P["D2"][n])]
                mms([(c2(d, h, 384, 2), [(ap("ID"), ap("M5", S[:, :, k - 1 + h])), (ap("NID"), yy)]) for h in range(2)])
                act(ap("M2", S[:, :, k - 1:k + 1]), c2(d, 0, 384), AF.Relu)
        landed = [tt(ap("M2", S[:, :, k]), ind(rw, c2("SKQ", 12 * k, 12 * k + 12)), yy, OP.min) for k in range(S2, 16)][0]
        ops[dma("Y", c2(XN, OWN, OWN + V_), c2(R, OWN, OWN + V_), 4000)]["deps"][landed] = True
        if n == 0:
            for (a, b) in ((192, 384), (384, 768), (768, 1536), (1536, 3072)):
                ops[dma("Y", c2("D4", a, b), c2("D4", 0, b - a), 2500)]["deps"][landed] = True
        gcp(c2("D4", P["A4"], 3072, 16), yy)
        k2 = (S2 + 16) // 2 + P["K2"]
        add("P", [("matmul", [ka, ap("ID"), ap("KMX"), True, False], {})], 60 + 192 * P["PE"])
        for (a, b, t, m) in ((0, S2, "SEL", "M5"), (S2, k2, "SEL", "M2"), (0, S2, "NSEL", "M2"), (k2, 16, "SEL", "M2")):
            add("P", [("matmul", [ap("KA", S[:, 0:12, a:b]), sel(r, t), ap(m, S[:, r::16, a:b]), False, b == 16 and r == 15], {}) for r in range(16)],
                60 + 16 * max(64, 12 * (b - a)) * P["PE"])
        step1(n, P["POS"][n], 6)
        scan(ap("KI"), ap("RBIG"), c2("KB", 0, 192), 0.0, OP.add, OP.min)
        if n:
            tt(wn("J0"), ends("KI"), kw2, OP.min)
        ts(wn("JI"), wn("J0") if n else ends("KI"), 15, OP.bitwise_and)
        cp(wh("JB"), wn("JI"))
        tt(wf("DB"), wn("JI"), wf("BB"), OP.subtract)
        if not last:
            gcp(wb("BH"), wf("BB"))
        spread("PB", wh("JB", 0, 28), False)
        more(c2("PB", 256, 448), ap("NID"), ap("W"))
        ts(ap("MJ"), c2("PB", 0, 192), PM, OP.is_equal)
        early = tt(ap("LJM"), ap("MJ"), lp, OP.mult)
        pick(small, "LJM")
        act(wf("LJ"), small, AF.Copy)
        tt(wf("DL"), wf("LJ"), wf("LB"), OP.subtract)
        if not last:
            cp(wu("LJU"), small)
            gat("S", ap("TOLD"), c2("TT", 0, R0), wu("LJU"))
        sec[0] = "c"
        ts(ap("BI"), ka, thc, OP.is_ge)
        scan(ap("CN"), r01, ap("BI"), 0.0, OP.mult, OP.add)
        ts(wf("OCC"), ends("CN"), PAR, OP.subtract, 3.0, OP.is_ge)
        for (a, b) in parts():
            kh = ap("KA", S[:, a:b, :])
            if P["STS"] > (a > 0):
                act(c2("ST", 16 * a, 16 * b), kh, AF.Copy)
            else:
                cp(c2("ST", 16 * a, 16 * b), kh)
            scan(c2("KS", 16 * a, 16 * b), c2("R01", 16 * a, 16 * b), c2("ST", 16 * a, 16 * b), 0.0, OP.mult, OP.max)
            tt(c2("NOH", 16 * a, 16 * b), c2("KS", 16 * a, 16 * b), kh, OP.not_equal)
            scan(c2("PS", 16 * a, 16 * b), c2("NOH", 16 * a, 16 * b), c2("PA", 16 * a, 16 * b), 0.0, OP.mult, OP.add)
            tt(wf("A%d" % a, 0, MB_), c2("PS", 16 * a + 15, 16 * b, 16), wf("OCC", a, b), OP.mult)
        ts(wu("PLU"), ends("PS"), float(V_), OP.add)
        nv, ov = "NV%d" % n, "OV%d" % n
        if P["XSS"] == 2:
            gat("S", ap("XS"), rw, wu("PLU"))
            mm(c2("D0", 0, 192), [(ap("ID"), ap("XS")), (ap("NID"), ap("Q"))])
            act(ap(nv), c2("D0", 0, 192), AF.Relu, bias=192.0)
        else:
            tt(ap("XS"), ind(rw, wu("PLU")), ap("Q"), OP.subtract)
            if P["XSS"]:
                act(ap(nv), ap("XS"), AF.Relu, bias=192.0)
            else:
                ts(ap(nv), ap("XS"), 192.0, OP.add, 0.0, OP.max)
        send([(ap(nv), ap(ov), HOPS[n], "x%d" % n)], 2500)
        for (a, b) in parts():
            lowest_half(a, b, c2("NO", 16 * n + a, 16 * n + b), P["NS1"])
        send([(c2("NO", 16 * n, 16 * n + 12), c2("OO", 16 * n, 16 * n + 12), HOPS[n], "x%d" % n)], 2500)
        for (a, b) in parts():
            cp(ind(c2(R, 0, FA), c2("NO", 16 * n + a, 16 * n + b)), c2(nv, 16 * a, 16 * b))
        if not last:
            send([(rw, c2(XN, 0, V_), HOPS[n] - HOPS[n + 1], "r%d" % (n + 2))], 8000)
        act(wf("C4"), wf("OCC"), AF.Identity, scale=131072.0, bias=-131072.0)
        tt(wf("SY"), wf("C4"), sy, OP.add)
        act(ap("THR"), ind(wf("SY", 0, 16), wu("IQ")), AF.Identity, scale=-1.0, bias=thc)
        act(wf("PL"), ends("PS"), AF.Identity, bias=float(V_ - FA))
        tt(wf("DP"), wf("LJ"), wf("PL"), OP.subtract)
        if not last:
            gcp(ap("GH"), gg)
            gcp(ap("TH2"), ap("TOLD"))
            mm(c2("PA", 0, 192), [(ap("ID"), ap("CV")), (ap("ID"), ap("GH")), (ap("NID"), ap("TH2"))])
        sec[0] = "d"
        a4 = P["A4"]
        for k in range(a4, 16):
            gat("S", c2("A4", k, 3072, 16), rw, c2("SKQ", 12 * k, 12 * k + 12))
        row = []
        left = {"a": list(range(a4)), "x": parts(), "f": [0, 1, 2], "r": list(P["G5V"][n]), "m": list(range(a4))}
        for c in P["ROW"]:
            if not left[c]:
                continue
            k = left[c].pop(0)
            if c == "a":
                row.append(tt(c2("A4", k, 3072, 16), ind(rw, c2("SKQ", 12 * k, 12 * k + 12)), yy, OP.subtract))
                if k >= P["JT"]:
                    ops[row[-1]]["deps"].setdefault(early, False)
            elif c == "x":
                row.append(cp(ind(c2(XN, OWN, OWN + FA), c2("OO", 16 * n + k[0], 16 * n + k[1])), c2(ov, 16 * k[0], 16 * k[1])))
            elif c == "f":
                row.append(scan(c2("FS", 1024 * k, 1024 * k + 1024), c2("D4", 1024 * k, 1024 * k + 1024), c2("A4", 1024 * k, 1024 * k + 1024), 0.0, OP.add, OP.max))
            elif c == "r":
                row.append(gat("V", c2("RAW5", 512 * k, 512 * k + 512), c2(XN, FA, FA + R0), c2("WK", 32 * k, 32 * k + 32)))
            else:
                row.append(ts(ap("M2", S[:, :, k]), c2("A4", k, 3072, 16), -1.0, OP.mult, 0.0, OP.max))
        for x in range(6):
            if x not in P["G5V"][n]:
                gat("S", c2("RAW5", 512 * x, 512 * x + 512), c2(XN, FA, FA + R0), c2("WK", 32 * x, 32 * x + 32))
        if P["FIXROW"]:
            for a, b in zip(row, row[1:]):
                ops[b]["deps"].setdefault(a, False)
        if last:
            dma("Y", ap("yx"), c2(XN, OWN, OWN + V_), 4000)
        for k in range(a4, 16, 2):
            d = pair("4")
            mms([(c2(d, h, 384, 2), [(ap("ID"), yy), (ap("NID"), c2("A4", k + h, 3072, 16))]) for h in range(2)])
            act(ap("M2", S[:, :, k:k + 2]), c2(d, 0, 384), AF.Relu)
        for (a, b) in (((0, a4), (a4, 16)) if P["O4"] else ((a4, 16), (0, a4))):
            mm(ap("KA", S[:, 0:12, a:b]), [(sel(r, "NSEL"), ap("M2", S[:, r::16, a:b])) for r in range(16)])
        tt(ap("BI"), ka, ap("THR"), OP.is_ge)
        scan(ap("CN"), r01, ap("BI"), 0.0, OP.mult, OP.add)
        ts(wb("EX"), ends("CN"), PAR, OP.subtract, 3.0, OP.is_lt)
        sec[0] = "e"
        for u in range(6):
            dist("RAW5", "M5", lambda a, b: c2("FS", 16 * a + 15, 16 * b, 16), 0.0, u)
            if u % 2:
                keys(256, "M5", u // 2)
        act(wf("E16"), wb("EX"), AF.Identity, scale=16.0, **({} if last else {"accum_out": wf("C", 8, 9)}))
        exw = ind(wb("EX", 0, 16), wu("IR", 0, 2))
        xp = c2("PB", 0, 192)
        if not last:
            tt(wf("A2"), wb("EX"), wf("LJ"), OP.mult)
            tt(wh("XL"), wb("EX"), wf("LB"), OP.mult)
            spread("KA", wh("XL"), False)
            lowest("A2", "DU2", "DU2", wu("O2"), P["NS2"])
            tt(wf("JX"), wn("JI"), wf("E16"), OP.subtract)
            tt(ap("OHJ"), ind(wf("JX", 0, 16), wu("IQ")), ap("RIM"), OP.is_equal)
        else:
            spread("KA", wh("LBH"), False)
            act(ap("MBR"), ap("MB"), AF.Identity, scale=4096.0, bias=-4096.0 - X0)
            act(ap("LJX"), ap("L1"), AF.Identity, bias=-float(X0))
            act(ap("ZT"), ap("W"), AF.Identity, bias=-float(X0))
            more(ap("KA", S[:, 16:28, :]), ap("ID"), ap("MBR"), False)
        tt(wf("T1", 0, 48), ind(wb("EX", 0, 16), wu("IR", 0, 3)), wf("DL", 0, 48), OP.mult)
        tt(wf("LB", 0, 48), wf("LB", 0, 48), wf("T1", 0, 48), OP.add)
        if last:
            act(wb("BH"), wf("BB"), AF.Copy)
            mms([(ap("PA", S[0:8, b:192:16]), [(c2("EB", 128 * b, 128 * b + 128, 16), wb("BH"))]) for b in range(16)])
            act(ap("OB", S[0:8, :]), ap("PA", S[0:8, 0:192]), AF.Copy)
            dma("Y", ap("yb"), ap("OB", S[0:8, :]), 2200)
        cp(wu("LBU"), wf("LB"))
        ts(wu("SELU"), wf("PL"), float(FA), OP.add)
        if P["ZS"]:
            gat("S", ap("XS"), both, wu("SELU"))
            mm(c2("PB", 0, 192), [(ap("ID"), ap("XS")), (ap("ID"), ap(zs))])
            act(ap("Z"), c2("PB", 0, 192), AF.Identity, scale=0.5, bias=1023.75 - zoff / 2)
        else:
            tt(ap("ZT"), ind(both, wu("SELU")), ap(zs), OP.add)
            ts(ap("Z"), ap("ZT"), 0.5, OP.mult, 1023.75 - zoff / 2, OP.add)
        if last:
            act(ap("ZO"), ap("Z"), AF.Identity, bias=-1024.0)
            dma("Y", ap("yz"), ap("ZO"), 2200)
        else:
            cnt = c2("PA", 448, 449)
            mm(cnt, [(ap("BLKF"), wf("C", 8, 9))])
            ts(wn("N1", 0, 1), cnt, 0.5, OP.mult, -0.25, OP.add)
            ts(PAR, wn("N1", 0, 1), -2.0, OP.mult, cnt, OP.add)
        sec[0] = "g" if last else "f"
        scan(ap("KI"), ap("RBIG"), c2("KB", 256, 448), 0.0, OP.add, OP.min)
        ts(wn("WI"), ends("KI"), 15, OP.bitwise_and)
        tt(wb("WB"), wn("WI"), wf("E16"), OP.add)
        spread("KB", wb("WB"))
        for (a, b) in (parts() if P["MWH"] and not last else [(0, 12)]):
            ts(c2("MW", 16 * a, 16 * b), c2("KB", 16 * a, 16 * b), PM16, OP.is_equal)
            if not last:
                tt(c2("MD", 16 * a, 16 * b), c2("MW", 16 * a, 16 * b), c2("PA", 16 * a, 16 * b), OP.mult)
        if not last:
            for (a, b) in parts():
                tt(ind(ap("TT"), wu("O2", a, b)), c2("MD", 16 * a, 16 * b), c2("TOLD", 16 * a, 16 * b), OP.add)
        tt(ap("BW"), ap("MW"), c2("PB", 256, 448), OP.mult)
        more(ap("KA", S[:, 16:28, :]), ap("NBLK"), ap("BW"))
        if last:
            tt(ap("OW"), ap("BW"), ap("ZT"), OP.add)
            dma("S", ap("yw"), ap("OW"), 2200)
            tt(ap("OL"), ap("KA", S[:, 16:28, :]), ap("LJX"), OP.max)
            dma("Y", ap("yl"), ap("OL"), 2200)
        else:
            mm(c2("KB", 256, 448), [(ap("BLK"), ap("MW"))])
            tt(ap("LJX"), ap("LJM"), c2("KB", 256, 448), OP.mult)
            mm(wp, [(ap("ID"), ap("W")), (ap("ID"), ap("BW"))])
            tt(ap("MBR"), ap("MB"), ap("KA", S[:, 16:28, :]), OP.mult)
            mm(lp, [(ap("ID"), ap("L1")), (ap("ID"), ap("MBR")), (ap("NID"), ap("LJX"))])
            cp(ap("WK"), wp)
            act(ap("MB"), lp, AF.Relu, scale=-1.0, bias=1.0)
            act(ap("L1"), lp, AF.Copy)
            act(ap("W"), wp, AF.Copy)
            sec[0] = "e"
            bound(n + 1)
            step1(n + 1, 0, P["POS"][n + 1])
            pick(ww, "BW", "NSE1", wh("XL"))
            cp(wu("WWU"), ww)
            gat("S", ap("VW"), c2(XN, FA, FA + R0), wu("WWU"))
            mm(xp, [(ap("ID"), ap("VW")), (ap("NID"), ap("Z"))])
            act(va, xp, AF.Abs, bias=1024.0)
            limit(n + 1)
            if n + 2 < RO:
                cp(ap("LK"), lp)
    for (a, j, b, k) in P["BEFORE"]:
        for o in ops:
            if o["tag"] == "aVGG":
                first, seen, was = None, 0, 0
            elif o["tag"] == a:
                was += 1
                if was <= j + 1:
                    first = o["id"]
            elif o["tag"] == b:
                seen += 1
                if seen > k and first is not None:
                    o["deps"].setdefault(first, False)
    return ops


def links(ops, soft=True):
    pred = []
    for o in ops:
        p = {d: P["OTHER"] for d in o["soft"]} if soft else {}
        for d, wait in o["deps"].items():
            p[d] = (P["OTHER"] if ops[d]["eng"] != o["eng"] else P["SAME"]) if wait else None
        for d in o["after"]:
            p[d] = P["OTHER"]
        pred.append(p)
    return pred


def schedule(ops, bias=None):
    n = len(ops)
    pred = links(ops)
    succ = [[] for _ in ops]
    for i in range(n):
        for d in pred[i]:
            succ[d].append(i)
    prio = [0.0] * n
    for i in range(n - 1, -1, -1):
        prio[i] = ops[i]["cost"] + max([prio[s] + (pred[s][i] or 0.0) for s in succ[i]] + [0.0])
    if bias is not None:
        prio = [p + float(b) for p, b in zip(prio, bias)]
    left = [len(p) for p in pred]
    start, fin = [0.0] * n, [0.0] * n
    free = {e: 0.0 for e in "VSPGY"}
    order = {e: [] for e in "VSPGY"}
    ready = {i: 0.0 for i in range(n) if left[i] == 0}
    while ready:
        est = {i: max(t, free[ops[i]["eng"]]) for i, t in ready.items()}
        i0 = min(est, key=lambda i: (est[i], -prio[i]))
        e = ops[i0]["eng"]
        i = max([j for j in est if ops[j]["eng"] == e and est[j] <= est[i0] + min(P["SLACK"], ops[i0]["busy"])], key=lambda j: prio[j])
        start[i] = est[i]
        fin[i] = est[i] + ops[i]["cost"]
        free[e] = est[i] + ops[i]["busy"]
        order[e].append(i)
        del ready[i]
        for s in succ[i]:
            left[s] -= 1
            if left[s] == 0:
                ready[s] = max((fin[d] + l) if l is not None else start[d] for d, l in pred[s].items())
    return order, start, fin


def place_all(ops, seq, lag, first):
    st = [0.0] * len(ops)
    used = {e: ([], []) for e in "VSPGY"}
    for i in seq:
        t = first[i]
        for d, l in lag[i]:
            if st[d] + l > t:
                t = st[d] + l
        a, b = used[ops[i]["eng"]]
        busy = ops[i]["busy"]
        lo, hi = 0, len(b)
        while lo < hi:
            mid = (lo + hi) // 2
            if b[mid] <= t:
                lo = mid + 1
            else:
                hi = mid
        while lo < len(a) and a[lo] < t + busy:
            t = b[lo]
            lo += 1
        a.insert(lo, t)
        b.insert(lo, t + busy)
        st[i] = t
    return st


def refine(ops, start, rounds):
    n = len(ops)
    pred = links(ops)
    above, fwd = [], []
    for i in range(n):
        far = 0
        for d in pred[i]:
            far |= above[d]
        fwd.append([(d, 1.0 if l is None else ops[d]["cost"] + l) for d, l in pred[i].items() if not far >> d & 1 or ops[d]["dma"]])
        for d in pred[i]:
            far |= 1 << d
        above.append(far)
    bwd = [[] for _ in ops]
    for i in range(n):
        for d, l in fwd[i]:
            bwd[d].append((i, l + ops[i]["busy"] - ops[d]["busy"] if l > 1.0 else 1.0))
    tail = [o["cost"] - o["busy"] for o in ops]
    zero = [0.0] * n
    rng = np.random.default_rng(P["SEED"])

    def topo(key, lag, rev):
        k = list(key)
        for i in (range(n - 1, -1, -1) if rev else range(n)):
            for d, _ in lag[i]:
                if k[d] >= k[i]:
                    k[i] = k[d] + 1e-3
        return sorted(range(n), key=lambda i: k[i])

    def worth(st):
        return max(st[i] + ops[i]["cost"] for i in range(n))

    best, bst = worth(start), list(start)
    tags = sorted(set(o["tag"] for o in ops if o["tag"][0] != "i"))
    now, cst = best, bst

    def held(st):
        prev, out = {}, []
        for e in "VSPGY":
            row = sorted([i for i in range(n) if ops[i]["eng"] == e], key=lambda i: st[i])
            prev.update(zip(row[1:], row))
        i = max(range(n), key=lambda i: st[i] + ops[i]["cost"])
        while i is not None:
            d = next((d for d, l in fwd[i] if st[d] + l > st[i] - 1.0), None)
            if d is None and i in prev and st[prev[i]] + ops[prev[i]]["busy"] > st[i] - 1.0:
                d = prev[i]
                if ops[d]["tag"] != ops[i]["tag"]:
                    out.append((ops[d]["tag"], ops[i]["tag"]))
            i = d
        return out

    for it in range(rounds):
        kind = rng.random()
        if it % 20 == 0:
            hot = held(cst)
        if kind < P["HOT"] and hot:
            shift = {}
            for _ in range(int(rng.integers(1, 3))):
                u, v = hot[int(rng.integers(len(hot)))]
                x = float(rng.exponential() * rng.choice([300.0, 1000.0, 3000.0]))
                shift.update({u: x} if rng.random() < 0.5 else {v: -x})
            cur = [s + shift.get(o["tag"], 0.0) for s, o in zip(cst, ops)]
        elif kind < 0.7:
            shift = {tags[int(rng.integers(len(tags)))]: float(rng.normal() * rng.choice([300.0, 1500.0, 5000.0])) for _ in range(int(rng.integers(1, 4)))}
            cur = [s + shift.get(o["tag"], 0.0) for s, o in zip(cst, ops)]
        else:
            lo = float(rng.random()) * best
            noise = rng.normal(size=n) * float(rng.choice([100.0, 400.0, 1500.0]))
            cur = [s + float(x) if lo <= s < lo + 8000.0 else s for s, x in zip(cst, noise)]
        if rng.random() < 0.5:
            r = place_all(ops, topo([-(cur[i] + ops[i]["busy"]) for i in range(n)], bwd, True), bwd, tail)
            cur = [-(r[i] + ops[i]["busy"]) for i in range(n)]
        st = place_all(ops, topo(cur, fwd, False), fwd, zero)
        v = worth(st)
        if v <= now + P["HEAT"] * (1.0 - it / rounds) * rng.random():
            now, cst = v, st
        if v < best:
            best, bst = v, st
    order = {e: sorted([i for i in range(n) if ops[i]["eng"] == e], key=lambda i: bst[i]) for e in "VSPGY"}
    return order, bst


def polish(ops, start, rounds):
    n = len(ops)
    pred = links(ops, False)
    banks = [sorted(o["banks"]) for o in ops]
    gap = P["OTHER"]
    above, lag = [], []
    for i in range(n):
        far = 0
        for d in pred[i]:
            far |= above[d]
        lag.append([(d, 0.0 if l is None else ops[d]["cost"] + l) for d, l in pred[i].items() if not far >> d & 1 or ops[d]["dma"]])
        for d in pred[i]:
            far |= 1 << d
        above.append(far)
    eng = ["VSPGY".index(o["eng"]) for o in ops]
    busy, cost = [o["busy"] for o in ops], [o["cost"] for o in ops]
    rng = np.random.default_rng(P["SEED"])

    def run(seq):
        st, by, free, lastop, inb = [0.0] * n, [-1] * n, [0.0] * 5, [-1] * 5, {}
        for i in seq:
            e = eng[i]
            t, b = free[e], lastop[e]
            for d, l in lag[i]:
                if st[d] + l > t:
                    t, b = st[d] + l, -2 - d
            for k in banks[i]:
                d = inb.get(k, i)
                if eng[d] != e and st[d] + cost[d] + gap > t:
                    t, b = st[d] + cost[d] + gap, d
                inb[k] = i
            st[i], by[i] = t, b
            free[e], lastop[e] = t + busy[i], i
        rest, nxt, inb = list(cost), [0.0] * 5, {}
        for i in reversed(seq):
            e = eng[i]
            t = max(rest[i], nxt[e] + busy[i])
            for k in banks[i]:
                d = inb.get(k, i)
                if eng[d] != e and rest[d] + cost[i] + gap > t:
                    t = rest[d] + cost[i] + gap
                inb[k] = i
            rest[i] = nxt[e] = t
            for d, l in lag[i]:
                if t + l > rest[d]:
                    rest[d] = t + l
        way = np.array(st) + np.array(rest)
        end = float(way.max())
        near = way - (end - wide)
        return end, end + P["MASS"] * float(np.maximum(near, 0.0).sum()) / wide, st, [(by[i], i) for i in np.flatnonzero(near > 0).tolist() if by[i] >= 0]

    wide = P["WIDE"]
    seq = sorted(range(n), key=lambda i: (start[i], i))
    best, now, bst, held = run(seq)
    bseq = seq
    for it in range(rounds):
        u, v = held[int(rng.integers(len(held)))]
        a, b = seq.index(u), seq.index(v)
        more = int(rng.geometric(0.45)) - 1
        if rng.random() < 0.5:
            while more and a > 0:
                a -= 1
                more -= eng[seq[a]] == eng[v]
            mid = seq[a:b + 1]
            go = [i for i in mid if i == v or above[v] >> i & 1]
            if u in go:
                continue
            new = seq[:a] + go + [i for i in mid if not (i == v or above[v] >> i & 1)] + seq[b + 1:]
        else:
            while more and b < n - 1:
                b += 1
                more -= eng[seq[b]] == eng[u]
            mid = seq[a:b + 1]
            go = [i for i in mid if i == u or above[i] >> u & 1]
            if v in go:
                continue
            new = seq[:a] + [i for i in mid if not (i == u or above[i] >> u & 1)] + go + seq[b + 1:]
        t, w, s2, h2 = run(new)
        if w <= now + P["COOL"] * (1.0 - it / rounds) * rng.exponential():
            now, held = w, h2
            seq = sorted(new, key=lambda i: s2[i])
            if t < best:
                best, bst, bseq = t, s2, seq
    inb = {}
    for i in bseq:
        ops[i]["soft"] = set(inb[k] for k in banks[i] if k in inb and eng[inb[k]] != eng[i])
        inb.update({k: i for k in banks[i]})
    return {e: [i for i in bseq if ops[i]["eng"] == e] for e in "VSPGY"}, bst


PLAN = {}


def rank_program(g, core, T, topo):
    rank = T.rank_of(core)
    if rank is None:
        return
    if not PLAN:
        PLAN["ops"] = build()
        start = refine(PLAN["ops"], schedule(PLAN["ops"])[1], P["ROUNDS"])[1]
        P.update(P["AGAIN"])
        PLAN["order"] = polish(PLAN["ops"], refine(PLAN["ops"], start, P["ROUNDS"])[1], P["POLISH"])[0]
    ops, order = PLAN["ops"], PLAN["order"]
    N = len(T.cores)
    q = {"V": g.vector, "S": g.scalar, "P": g.tensor, "G": g, "Y": g.sync}
    place = {i: n for e in order for n, i in enumerate(order[e])}
    waits = []
    for o in ops:
        far = {}
        for d, wait in list(o["deps"].items()) + [(d, True) for d in o["soft"]]:
            key = d if ops[d]["dma"] else ops[d]["eng"]
            if wait and (key not in far or place[d] > place[far[key]]):
                far[key] = d
        waits.append(list(far.values()))
    needed = set(d for w in waits for d in w)
    mark, total = {}, {}
    for e in "VSPGY":
        for i in order[e]:
            o = ops[i]
            if o["dma"]:
                sem, inc = o["dma"]
                if inc is None:
                    parts = o["calls"][0][1][1]
                    per = min(len(topo.engines(core, T.cores[(rank + p[2]) % N])) for p in parts) // len(parts)
                    inc = per * len(parts)
                    for p in parts:
                        total[p[3]] = total.get(p[3], 0) + per
            elif i in needed:
                sem, inc = "c" + e, 1
            else:
                continue
            total[sem] = total.get(sem, 0) + inc
            mark[i] = (sem, total[sem])

    def real(a):
        if isinstance(a, tuple) and a[0] == "ap":
            return T[a[1]][a[2]]
        if isinstance(a, tuple) and a[0] == "ind":
            return real(a[1]).indirect(real(a[2]))
        return a

    meth = {"tensor_copy": lambda e: e.tensor_copy, "tensor_tensor": lambda e: e.tensor_tensor, "tensor_scalar": lambda e: e.tensor_scalar,
            "tensor_tensor_scan": lambda e: e.tensor_tensor_scan, "tensor_reduce": lambda e: e.tensor_reduce, "transpose": lambda e: e.transpose,
            "memset": lambda e: e.memset, "activation": lambda e: e.activation, "matmul": lambda e: e.matmul, "iota": lambda e: e.iota, "affine_select": lambda e: e.affine_select,
            "dma_start": lambda e: e.dma_start, "partition_broadcast": lambda e: e.partition_broadcast}
    for e in "VSPYG":
        seen = {}
        for i in order[e]:
            o = ops[i]
            want = {}
            for (sem, val) in [mark[d] for d in waits[i]] + [(s, total[s]) for s in o["ext"]]:
                want[sem] = max(want.get(sem, 0), val)
            for sem, val in want.items():
                if seen.get(sem, 0) < val:
                    q[e].wait_ge(T.sem[sem], val)
                    seen[sem] = val
            for (name, args, kw) in o["calls"]:
                if name == "send":
                    parts = args[1]
                    trs = []
                    for n, (src, dst, off, sem) in enumerate(parts):
                        peer = T.cores[(rank + off) % N]
                        eng = topo.engines(core, peer)
                        per = len(eng) // len(parts)
                        rid, pid = topo.addr(peer, core)
                        trs.append(RemoteDMATransfer(dst_ids=[DstId(rid=rid, pnc=pid)], dma_engine_mask=sum(1 << x for x in eng[n * per:(n + 1) * per]),
                                                     remote_sem=T.sem[sem], src=real(src), dst=real(dst)))
                    g.remote_dma_fused(trs, local_sem=T.sem[o["dma"][0]])
                else:
                    ins = meth[name](q[e])(*[real(a) for a in args], **{k: real(v) for k, v in kw.items() if k != "acc"})
            if i in mark and o["calls"][0][0] != "send":
                ins.then_inc(T.sem[mark[i][0]], o["dma"][1] if o["dma"] else 1)
        if e == "G":
            for sem, val in total.items():
                if seen.get(sem, 0) < val:
                    g.wait_ge(T.sem[sem], val)
